import numpy as np
import ml_dtypes


def mxq(x, axis, fmt="e4m3"):
    dtype, down = {"e4m3": (ml_dtypes.float8_e4m3fn, 7), "e5m2": (ml_dtypes.float8_e5m2, 14)}[fmt]
    v = np.moveaxis(np.asarray(x, np.float32).astype(ml_dtypes.bfloat16).astype(np.float64), axis, -1)
    blocks = v.reshape(v.shape[:-1] + (-1, 32))
    amax = np.abs(blocks).max(-1, keepdims=True)
    byte = np.maximum(np.where(amax > 0, np.frexp(amax)[1] - 1 + 127, 0) - down, 1)
    scale = np.exp2(byte - 127.0)
    codes = (blocks / scale).astype(np.float32).astype(dtype).astype(np.float64)
    return np.moveaxis((codes * scale).reshape(v.shape), -1, axis)


WIDE = False


def mx_kscale(k):
    if not WIDE:
        return np.ones(k)
    levels = np.array([10, -10, 5, -5, 0])
    if k % 512:
        return np.exp2(np.random.permutation(np.resize(levels, k // 32))).repeat(32)
    a = np.empty((k // 512, 16))
    for p in range(k // 512):
        a[p, :8] = np.random.permutation(np.resize(levels, 8))
        for g in range(8):
            far = levels[np.abs(levels - a[p, g]) >= 10]
            a[p, g + 8] = far[np.random.randint(len(far))]
    return np.exp2(a.ravel()).repeat(32)


def f64(x):
    return np.asarray(x).astype(np.float64)


def striped(idx):
    return np.tile(np.asarray(idx).reshape(-1, 16).T, (8, 1)).astype(np.uint16)


def unstriped(offs):
    return offs[:16].T.reshape(-1).astype(np.int64)


E2M1 = np.array([0.0, 0.5, 1.0, 1.5, 2.0, 3.0, 4.0, 6.0, -0.0, -0.5, -1.0, -1.5, -2.0, -3.0, -4.0, -6.0])


def pack_weight(w, fmt):
    k, n = w.shape
    w = f64(np.asarray(w, np.float32).astype(ml_dtypes.bfloat16)).reshape(k // 32, 32, n)
    amax = np.abs(w).max(1)
    if fmt == "e4m3":
        byte = np.frexp(amax)[1] - 1 + 127 - 7
    else:
        mant, ex = np.frexp(amax / 6.0)
        byte = np.where(mant > 0.5, ex, ex - 1) + 127
    byte = np.clip(np.where(amax > 0, byte, 1), 1, 254)
    scaled = (w * np.exp2(127.0 - byte)[:, None, :]).reshape(k, n).astype(np.float32)
    by_word = np.ascontiguousarray(scaled.reshape(k // 512, 128, 4, n).transpose(0, 1, 3, 2))
    if fmt == "e4m3":
        words = by_word.astype(ml_dtypes.float8_e4m3fn).view(np.uint8)
    else:
        c = by_word.astype(ml_dtypes.float4_e2m1fn).view(np.uint8) & 0xF
        words = (c[..., 0::2] | (c[..., 1::2] << 4)).reshape(k // 512, 128, 2 * n)
    return np.ascontiguousarray(words), np.ascontiguousarray(byte.astype(np.uint8).reshape(k // 512, 16, n))


def unpack_weight(words, scales, fmt):
    g, _, n = scales.shape
    words = np.ascontiguousarray(words).reshape(g, 128, n, -1)
    if fmt == "e4m3":
        vals = words.view(ml_dtypes.float8_e4m3fn).astype(np.float64)
    else:
        nib = np.empty((g, 128, n, 4), np.uint8)
        nib[..., 0::2] = words & 0xF
        nib[..., 1::2] = words >> 4
        vals = E2M1[nib]
    vals = vals * np.repeat(np.exp2(scales.astype(np.float64) - 127.0), 8, axis=1)[..., None]
    return vals.transpose(0, 1, 3, 2).reshape(g * 512, n)


B, N, T, D, DV, NQ = 1, 1024, 2048, 1024, 256, 256
CAP = 2.0


def setup_inputs():
    n = np.random.standard_normal
    idx = np.sort(np.random.permutation(T)[:B * N].reshape(B, N), axis=1).reshape(-1)
    s = mx_kscale(D)[:, None]
    u = np.ones(T)
    u[idx] = mx_kscale(B * N)
    r = np.random.uniform(0.5, 2.0, T)
    k = n((D, T)) / s
    v = n((DV, T)) / (u * r)
    kp = pack_weight(k, "e2m1")
    return {
        "qT": (n((B, D, NQ)) * s * (1.00 / np.sqrt(D))).astype(np.float32),
        "k_words": np.ascontiguousarray(kp[0].reshape(D // 1024, 2, 128, T, 2).transpose(0, 2, 3, 1, 4)).reshape(D // 1024, 128, T, 4),
        "k_scales": kp[1],
        "vT": v.astype(np.float32),
        "vs": np.tile(u * r, (128, 1)).astype(np.float32),
        "kb": np.tile(n(T), (128, 1)).astype(np.float32),
        "offs": striped(idx),
    }


def reference(qT, k_words, k_scales, vT, vs, kb, offs):
    idx = unstriped(offs)
    k = unpack_weight(k_words.reshape(D // 1024, 128, T, 2, 2).transpose(0, 3, 1, 2, 4).reshape(D // 512, 128, 2 * T), k_scales, "e2m1")
    v = f64(vT)
    pick = lambda x: x[:, idx].reshape(x.shape[0], B, N).transpose(1, 0, 2)
    q = f64(qT)
    score = mxq(q, 1, "e4m3").transpose(0, 2, 1) @ pick(k)
    score = score + pick(f64(kb))[:, :1, :]
    score = CAP * np.tanh(score / CAP)
    p = 1.0 / (1.0 + np.exp(-score))
    w = p * pick(f64(vs))[:, :1, :]
    y = mxq(w, 2, "e4m3") @ mxq(pick(v).transpose(0, 2, 1), 1, "e4m3")
    y = y / 16.0
    return y

@@ -1,0 +1,227 @@
+from contextlib import ExitStack
+
+import concourse.mybir as mybir
+from concourse.masks import make_identity
+
+F32 = mybir.dt.float32
+BF16 = mybir.dt.bfloat16
+I32 = mybir.dt.int32
+U32 = mybir.dt.uint32
+U16 = mybir.dt.uint16
+U8 = mybir.dt.uint8
+FP8X4 = mybir.dt.float8_e4m3fn_x4
+FP4X4 = mybir.dt.float4_e2m1fn_x4
+ACT = mybir.ActivationFunctionType
+ALU = mybir.AluOpType
+
+P = 128
+NQ, N, T, D, DV = 256, 1024, 2048, 1024, 256
+PACK = 4
+K_PASS = P * PACK
+RUN = 8
+BLOCKS = P // RUN
+SLOT_PASSES = N // K_PASS
+D_PASSES = D // K_PASS
+Q_TILES = NQ // P
+V_TILES = DV // P
+LIST_COLS = K_PASS // 16
+
+FLOPS = 2 * NQ * N * (D + DV)
+BYTES = 4 * D * NQ + 4 * P * T + 32 * T + 4 * DV * T + 2 * 4 * T + 2 * P * N // 16 + 4 * NQ * DV
+
+
+def tile_attend_sigm_cap_kb_srtq256n1024t2048_kernel(tc, qT, k_words, k_scales, vT, vs, kb, offs, out):
+    nc = tc.nc
+    with ExitStack() as ctx:
+        sb = ctx.enter_context(tc.tile_pool(name="sb", bufs=1))
+        ps = ctx.enter_context(tc.psum_pool(name="ps", bufs=1))
+
+        def tiles(count, shape, dtype, name):
+            return [sb.tile(shape, dtype, name="%s%d" % (name, i), align_bytes=64) for i in range(count)]
+
+        offsets = sb.tile([P, N // 16], U16, name="offsets")
+        nc.sync.dma_start(offsets[:], offs)
+
+        def listed(g):
+            return offsets[:, g * LIST_COLS:(g + 1) * LIST_COLS]
+
+        def dealt(tile):
+            return tile[:].rearrange("p (t b c) -> p b t c", t=PACK, c=RUN)
+
+        ks_pool = sb.tile([P, T], U8, name="ks_pool", align_bytes=64)
+        kb_pool = sb.tile([P, T], F32, name="kb_pool", align_bytes=64)
+        vs_pool = sb.tile([P, T], F32, name="vs_pool", align_bytes=64)
+        kw_pool = sb.tile([P, T], I32, name="kw_pool", align_bytes=64)
+        v_pool = [sb.tile([P, T], F32, name="v_pool", tag="v_pool%d" % h, align_bytes=64) for h in range(V_TILES)]
+        q_raw = tiles(D_PASSES, [P, PACK, NQ], F32, "q_raw")
+        k_plane = tiles(D_PASSES, [P, N], U8, "k_plane")
+
+        nc.vector.memset(ks_pool[:].bitcast(I32), 0)
+        nc.vector.memset(k_plane[1][:].bitcast(I32), 0)
+        nc.vector.memset(kb_pool[:].bitcast(I32), 0)
+        nc.vector.memset(vs_pool[:].bitcast(I32), 0)
+
+        warm_in = sb.tile([P, 1], F32, name="warm_in")
+        warm_out = sb.tile([P, 1], F32, name="warm_out")
+        nc.gpsimd.memset(warm_in[:], 0.0)
+        nc.scalar.activation(out=warm_out[:], in_=warm_in[:], func=ACT.Tanh)
+
+        ident32 = sb.tile([P, P], F32, name="ident32", align_bytes=64)
+        ident16 = sb.tile([P, P], BF16, name="ident16", align_bytes=64)
+        make_identity(nc, ident32[:])
+        nc.scalar.copy(out=ident16[:], in_=ident32[:])
+
+        def load_q(o):
+            rows = qT[0, o * K_PASS:(o + 1) * K_PASS, :]
+            nc.sync.dma_start(out=q_raw[o][:], in_=rows.rearrange("(p t) q -> p t q", t=PACK))
+
+        for quad in range(4):
+            nc.sync.dma_start(out=ks_pool[32 * quad:32 * quad + 8, :].bitcast(I32),
+                              in_=k_scales[:, 4 * quad:4 * quad + 4, :].bitcast(I32))
+        nc.scalar.dma_start(out=kb_pool[0:1, :], in_=kb[0:1, :])
+        nc.scalar.dma_start(out=vs_pool[0:1, :], in_=vs[0:1, :])
+        load_q(0)
+        nc.sync.dma_start(out=kw_pool[:], in_=k_words[0].rearrange("p t b -> p (t b)").bitcast(I32))
+        load_q(1)
+        for h in range(V_TILES):
+            nc.sync.dma_start(out=v_pool[h][:], in_=vT[h * P:(h + 1) * P, :])
+
+        q_bf = sb.tile([P, D_PASSES, NQ, PACK], BF16, name="q_bf", align_bytes=64)
+        q_codes = sb.tile([P, D_PASSES * NQ], U32, name="q_codes", align_bytes=64)
+        q_plane = sb.tile([P, D_PASSES * NQ], U8, name="q_plane", align_bytes=64)
+
+        def weave_q(o):
+            nc.scalar.copy(out=q_bf[:, o].rearrange("p (c i) t -> p c t i", i=4),
+                           in_=q_raw[o][:].rearrange("p t (c i) -> p c t i", i=4))
+
+        weave_q(0)
+
+        ks_got = sb.tile([P, N], U8, name="ks_got", align_bytes=64)
+        nc.vector.tensor_copy(out=ks_got[:], in_=ks_pool[:].indirect(offsets[:]))
+        nc.vector.tensor_copy(
+            out=k_plane[0][:].bitcast(I32).rearrange("p (t b w) -> p b t w", t=PACK, w=2),
+            in_=ks_got[:].bitcast(I32).rearrange("p (b t w) -> p b t w", t=PACK, w=2))
+        for quad in range(4):
+            nc.scalar.dma_start(out=k_plane[1][32 * quad:32 * quad + 4, :].bitcast(I32),
+                                in_=k_plane[0][32 * quad + 4:32 * quad + 8, :].bitcast(I32))
+        weave_q(1)
+
+        col_bank = ps.tile([P, 512], F32, name="col_bank")
+        half_kb = tiles(SLOT_PASSES, [P, PACK], F32, "half_kb")
+        half_vs = tiles(SLOT_PASSES, [P, PACK], F32, "half_vs")
+
+        def columns(pool_tile, g, tag, dest):
+            got = sb.tile([P, K_PASS], U32, name="row_got", tag=tag, align_bytes=64)
+            nc.vector.tensor_copy(out=dealt(got), in_=pool_tile[:].bitcast(U32).indirect(listed(g)))
+            for t in range(PACK):
+                nc.tensor.transpose(col_bank[:, 2 * t:2 * t + P], got[:, t * P:(t + 1) * P].bitcast(F32), ident32[:])
+            nc.scalar.activation(out=dest[:], in_=col_bank[:, 0:2 * PACK:2], func=ACT.Copy, scale=0.5)
+
+        k_codes = tiles(SLOT_PASSES, [P, D_PASSES * K_PASS], U16, "k_codes")
+
+        def keys(g):
+            kw_got = sb.tile([P, K_PASS], U32, name="kw_got", tag="got%d" % (g + 1), align_bytes=64)
+            nc.vector.tensor_copy(out=kw_got[:], in_=kw_pool[:].bitcast(U32).indirect(listed(g)))
+            nc.vector.tensor_copy(
+                out=k_codes[g][:].rearrange("p (o t b c) -> p b t o c", o=D_PASSES, t=PACK, c=RUN),
+                in_=kw_got[:].bitcast(U16).rearrange("p (b t c o) -> p b t o c", o=D_PASSES, t=PACK, c=RUN))
+
+        capped = tiles(SLOT_PASSES, [P, PACK, NQ], F32, "capped")
+        u = tiles(SLOT_PASSES * Q_TILES, [P, P, PACK], F32, "u")
+
+        def scores(g):
+            for pair in range(PACK // 2):
+                bank = ps.tile([P, 2, NQ], F32, name="score", tag="score%d" % (2 * g + pair))
+                for j in range(2):
+                    t = 2 * pair + j
+                    for qh in range(Q_TILES):
+                        for o in range(D_PASSES):
+                            kc = o * K_PASS + t * P
+                            sc = t * SLOT_PASSES * P + g * P
+                            qc = o * NQ + qh * P
+                            nc.tensor.matmul_mx(
+                                out=bank[:, j, qh * P:(qh + 1) * P],
+                                lhsT=k_codes[g][:, kc:kc + P].bitcast(FP4X4),
+                                lhsT_scale=k_plane[o][:, sc:sc + P],
+                                rhs=q_codes[:, qc:qc + P].bitcast(FP8X4),
+                                rhs_scale=q_plane[:, qc:qc + P],
+                                start=(o == 0), stop=(o == D_PASSES - 1))
+                for j in range(2):
+                    t = 2 * pair + j
+                    nc.scalar.activation(out=capped[g][:, t, :], in_=bank[:, j, :], func=ACT.Tanh,
+                                         bias=half_kb[g][:, t:t + 1], scale=0.5)
+            for qh in range(Q_TILES):
+                nc.scalar.activation(
+                    out=u[Q_TILES * g + qh][:].rearrange("p (c i) t -> p c t i", i=4),
+                    in_=capped[g][:, :, qh * P:(qh + 1) * P].rearrange("p t (c i) -> p c t i", i=4),
+                    func=ACT.Tanh)
+
+        v_got = tiles(SLOT_PASSES * V_TILES, [P, K_PASS], BF16, "v_got")
+        v_bf = tiles(SLOT_PASSES, [P, V_TILES, P, PACK], BF16, "v_bf")
+        v_codes = tiles(SLOT_PASSES, [P, DV], U32, "v_codes")
+        v_plane = tiles(SLOT_PASSES, [P, DV], U8, "v_plane")
+
+        def values(g):
+            bank = ps.tile([P, V_TILES, PACK, P], BF16, name="v_bank%d" % g)
+            for h in range(V_TILES):
+                got = v_got[V_TILES * g + h]
+                nc.vector.tensor_copy(out=dealt(got), in_=v_pool[h][:].indirect(listed(g)))
+                for t in range(PACK):
+                    nc.tensor.transpose(bank[:, h, t, :], got[:, t * P:(t + 1) * P], ident16[:])
+            nc.scalar.copy(out=v_bf[g][:], in_=bank[:].rearrange("p h t e -> p h e t"))
+
+        def quantise_values(g):
+            nc.vector.quantize_mx(out=v_codes[g][:].bitcast(FP8X4), scales=v_plane[g][:],
+                                  in_=v_bf[g][:].rearrange("p h e t -> p (h e t)"))
+
+        w_codes = tiles(SLOT_PASSES * Q_TILES, [P, P], U32, "w_codes")
+        w_plane = tiles(SLOT_PASSES * Q_TILES, [P, P], U8, "w_plane")
+
+        def weights(g, qh):
+            i = Q_TILES * g + qh
+            nc.vector.scalar_tensor_tensor(
+                out=w_all[:, i * K_PASS:(i + 1) * K_PASS].rearrange("p (q t) -> p q t", t=PACK), in0=u[i][:], scalar=1.0,
+                in1=half_vs[g][:].unsqueeze(1).to_broadcast([P, P, PACK]),
+                op0=ALU.add, op1=ALU.mult)
+
+        def quantise_weights(g, qh):
+            i = Q_TILES * g + qh
+            nc.vector.quantize_mx(out=w_codes[i][:].bitcast(FP8X4), scales=w_plane[i][:],
+                                  in_=w_all[:, i * K_PASS:(i + 1) * K_PASS])
+
+        columns(kb_pool, 0, "got0", half_kb[0])
+        keys(0)
+        nc.vector.quantize_mx(out=q_codes[:].bitcast(FP8X4), scales=q_plane[:],
+                              in_=q_bf[:].rearrange("p o q t -> p (o q t)"))
+        scores(0)
+        keys(1)
+        columns(kb_pool, 1, "got1", half_kb[1])
+        scores(1)
+        columns(vs_pool, 0, "got2", half_vs[0])
+        values(0)
+        columns(vs_pool, 1, "got1", half_vs[1])
+        values(1)
+
+        w_all = sb.tile([P, SLOT_PASSES * Q_TILES * K_PASS], BF16, name="w_all", tag="v_pool1", align_bytes=64)
+        y_bank = [ps.tile([P, 2, NQ], F32, name="y_bank", tag="score%d" % qh) for qh in range(Q_TILES)]
+        y = tiles(Q_TILES, [P, DV], F32, "y")
+
+        def product(g, qh):
+            i = Q_TILES * g + qh
+            nc.tensor.matmul_mx(
+                out=y_bank[qh][:, 0, :], lhsT=w_codes[i][:].bitcast(FP8X4), lhsT_scale=w_plane[i][:],
+                rhs=v_codes[g][:].bitcast(FP8X4), rhs_scale=v_plane[g][:],
+                start=(g == 0), stop=(g == SLOT_PASSES - 1))
+
+        for g in range(SLOT_PASSES):
+            weights(g, 0)
+            weights(g, 1)
+            quantise_values(g)
+            for qh in range(Q_TILES):
+                quantise_weights(g, qh)
+                product(g, qh)
+
+        nc.scalar.activation(out=y[0][:], in_=y_bank[0][:, 0, :], func=ACT.Copy, scale=1.0 / 16.0)
+        nc.sync.dma_start(out=out[0, 0:P, :], in_=y[0][:])
+        nc.vector.tensor_scalar_mul(y[1][:], y_bank[1][:, 0, :], 1.0 / 16.0)
+        nc.sync.dma_start(out=out[0, P:2 * P, :], in_=y[1][:])

@@ -12,19 +12,18 @@ U8 = mybir.dt.uint8
 FP8X4 = mybir.dt.float8_e4m3fn_x4
 FP4X4 = mybir.dt.float4_e2m1fn_x4
 ACT = mybir.ActivationFunctionType
-ALU = mybir.AluOpType
 
 P = 128
 NQ, N, T, D, DV = 256, 1024, 2048, 1024, 256
 PACK = 4
 K_PASS = P * PACK
 RUN = 8
-BLOCKS = P // RUN
 SLOT_PASSES = N // K_PASS
 D_PASSES = D // K_PASS
 Q_TILES = NQ // P
 V_TILES = DV // P
 LIST_COLS = K_PASS // 16
+CHUNKS = PACK * SLOT_PASSES
 
 FLOPS = 2 * NQ * N * (D + DV)
 BYTES = 4 * D * NQ + 4 * P * T + 32 * T + 4 * DV * T + 2 * 4 * T + 2 * P * N // 16 + 4 * NQ * DV
@@ -34,10 +33,14 @@ def tile_attend_sigm_cap_kb_srtq256n1024t2048_kernel(tc, qT, k_words, k_scales, 
     nc = tc.nc
     with ExitStack() as ctx:
         sb = ctx.enter_context(tc.tile_pool(name="sb", bufs=1))
+        late = ctx.enter_context(tc.tile_pool(name="late", bufs=1))
         ps = ctx.enter_context(tc.psum_pool(name="ps", bufs=1))
 
+        def sbuf(shape, dtype, name, tag=None):
+            return sb.tile(shape, dtype, name=name, tag=tag or name, align_bytes=64)
+
         def tiles(count, shape, dtype, name):
-            return [sb.tile(shape, dtype, name="%s%d" % (name, i), align_bytes=64) for i in range(count)]
+            return [sbuf(shape, dtype, "%s%d" % (name, i)) for i in range(count)]
 
         offsets = sb.tile([P, N // 16], U16, name="offsets")
         nc.sync.dma_start(offsets[:], offs)
@@ -45,91 +48,103 @@ def tile_attend_sigm_cap_kb_srtq256n1024t2048_kernel(tc, qT, k_words, k_scales, 
         def listed(g):
             return offsets[:, g * LIST_COLS:(g + 1) * LIST_COLS]
 
+        def reach(g):
+            return T - N + (g + 1) * K_PASS
+
         def dealt(tile):
             return tile[:].rearrange("p (t b c) -> p b t c", t=PACK, c=RUN)
 
-        ks_pool = sb.tile([P, T], U8, name="ks_pool", align_bytes=64)
-        kb_pool = sb.tile([P, T], F32, name="kb_pool", align_bytes=64)
-        vs_pool = sb.tile([P, T], F32, name="vs_pool", align_bytes=64)
-        kw_pool = sb.tile([P, T], I32, name="kw_pool", align_bytes=64)
-        v_pool = [sb.tile([P, T], F32, name="v_pool", tag="v_pool%d" % h, align_bytes=64) for h in range(V_TILES)]
+        ks_pool = sbuf([P, T], U8, "ks_pool")
+        kb_pool = late.tile([P, T], F32, name="kb_pool", align_bytes=64, offset=2 * T)
+        kw_pool = sbuf([P, T], I32, "kw_pool")
         q_raw = tiles(D_PASSES, [P, PACK, NQ], F32, "q_raw")
         k_plane = tiles(D_PASSES, [P, N], U8, "k_plane")
 
-        nc.vector.memset(ks_pool[:].bitcast(I32), 0)
-        nc.vector.memset(k_plane[1][:].bitcast(I32), 0)
+        nc.gpsimd.memset(ks_pool[:, 0:T // 2].bitcast(I32), 0)
+        nc.vector.memset(ks_pool[:, T // 2:T].bitcast(I32), 0)
         nc.vector.memset(kb_pool[:].bitcast(I32), 0)
-        nc.vector.memset(vs_pool[:].bitcast(I32), 0)
+        nc.vector.memset(k_plane[1][:].bitcast(I32), 0)
 
-        warm_in = sb.tile([P, 1], F32, name="warm_in")
-        warm_out = sb.tile([P, 1], F32, name="warm_out")
+        warm_in = sbuf([P, 1], F32, "warm_in")
+        warm_out = sbuf([P, 1], F32, "warm_out")
         nc.gpsimd.memset(warm_in[:], 0.0)
         nc.scalar.activation(out=warm_out[:], in_=warm_in[:], func=ACT.Tanh)
 
-        ident32 = sb.tile([P, P], F32, name="ident32", align_bytes=64)
-        ident16 = sb.tile([P, P], BF16, name="ident16", align_bytes=64)
+        ident32 = sbuf([P, P], F32, "ident32")
+        ident16 = sbuf([P, P], BF16, "ident16")
         make_identity(nc, ident32[:])
         nc.scalar.copy(out=ident16[:], in_=ident32[:])
-
-        def load_q(o):
-            rows = qT[0, o * K_PASS:(o + 1) * K_PASS, :]
-            nc.sync.dma_start(out=q_raw[o][:], in_=rows.rearrange("(p t) q -> p t q", t=PACK))
 
         for quad in range(4):
             nc.sync.dma_start(out=ks_pool[32 * quad:32 * quad + 8, :].bitcast(I32),
                               in_=k_scales[:, 4 * quad:4 * quad + 4, :].bitcast(I32))
-        nc.scalar.dma_start(out=kb_pool[0:1, :], in_=kb[0:1, :])
-        nc.scalar.dma_start(out=vs_pool[0:1, :], in_=vs[0:1, :])
-        load_q(0)
-        nc.sync.dma_start(out=kw_pool[:], in_=k_words[0].rearrange("p t b -> p (t b)").bitcast(I32))
-        load_q(1)
-        for h in range(V_TILES):
-            nc.sync.dma_start(out=v_pool[h][:], in_=vT[h * P:(h + 1) * P, :])
 
-        q_bf = sb.tile([P, D_PASSES, NQ, PACK], BF16, name="q_bf", align_bytes=64)
-        q_codes = sb.tile([P, D_PASSES * NQ], U32, name="q_codes", align_bytes=64)
-        q_plane = sb.tile([P, D_PASSES * NQ], U8, name="q_plane", align_bytes=64)
+        def load_queries(o):
+            rows = qT[0, o * K_PASS:(o + 1) * K_PASS, :]
+            nc.sync.dma_start(out=q_raw[o][:], in_=rows.rearrange("(p t) q -> p t q", t=PACK))
 
-        def weave_q(o):
+        load_queries(0)
+        nc.sync.dma_start(out=kb_pool[0:1, :], in_=kb[0:1, :])
+        load_queries(1)
+        words = k_words[0].rearrange("p t b -> p (t b)").bitcast(I32)
+        nc.sync.dma_start(out=kw_pool[:, 0:reach(0)], in_=words[:, 0:reach(0)])
+        nc.sync.dma_start(out=kw_pool[:, reach(0):T], in_=words[:, reach(0):T])
+
+        q_bf = sbuf([P, D_PASSES, NQ, PACK], BF16, "q_bf")
+        q_codes = sbuf([P, D_PASSES * NQ], U32, "q_codes")
+        q_plane = sbuf([P, D_PASSES * NQ], U8, "q_plane")
+
+        def weave_queries(o):
             nc.scalar.copy(out=q_bf[:, o].rearrange("p (c i) t -> p c t i", i=4),
                            in_=q_raw[o][:].rearrange("p t (c i) -> p c t i", i=4))
 
-        weave_q(0)
+        weave_queries(0)
 
-        ks_got = sb.tile([P, N], U8, name="ks_got", align_bytes=64)
+        ks_got = sbuf([P, N], U8, "ks_got")
         nc.vector.tensor_copy(out=ks_got[:], in_=ks_pool[:].indirect(offsets[:]))
         nc.vector.tensor_copy(
             out=k_plane[0][:].bitcast(I32).rearrange("p (t b w) -> p b t w", t=PACK, w=2),
             in_=ks_got[:].bitcast(I32).rearrange("p (b t w) -> p b t w", t=PACK, w=2))
-        for quad in range(4):
-            nc.scalar.dma_start(out=k_plane[1][32 * quad:32 * quad + 4, :].bitcast(I32),
-                                in_=k_plane[0][32 * quad + 4:32 * quad + 8, :].bitcast(I32))
-        weave_q(1)
+        nc.sync.dma_start(out=k_plane[1][0:100, :].bitcast(I32), in_=k_plane[0][4:104, :].bitcast(I32))
+        weave_queries(1)
+        vs_pool = late.tile([P, T], F32, name="vs_pool", align_bytes=64, offset=0)
+        v_pool = late.tile([P, V_TILES * T], F32, name="v_pool", align_bytes=64, offset=4 * T)
+        nc.sync.dma_start(out=vs_pool[:], in_=vs)
+        for h in range(V_TILES):
+            nc.sync.dma_start(out=v_pool[:, h * T:(h + 1) * T], in_=vT[h * P:(h + 1) * P, :])
 
-        col_bank = ps.tile([P, 512], F32, name="col_bank")
-        half_kb = tiles(SLOT_PASSES, [P, PACK], F32, "half_kb")
-        half_vs = tiles(SLOT_PASSES, [P, PACK], F32, "half_vs")
-
-        def columns(pool_tile, g, tag, dest):
-            got = sb.tile([P, K_PASS], U32, name="row_got", tag=tag, align_bytes=64)
-            nc.vector.tensor_copy(out=dealt(got), in_=pool_tile[:].bitcast(U32).indirect(listed(g)))
-            for t in range(PACK):
-                nc.tensor.transpose(col_bank[:, 2 * t:2 * t + P], got[:, t * P:(t + 1) * P].bitcast(F32), ident32[:])
-            nc.scalar.activation(out=dest[:], in_=col_bank[:, 0:2 * PACK:2], func=ACT.Copy, scale=0.5)
+        def half_columns(pool_tile, name, bank_tag, half_tag):
+            got = sbuf([P, N], U32, name + "_got")
+            bank = ps.tile([P, 512], F32, name=name + "_bank", tag=bank_tag)
+            half = sbuf([P, CHUNKS], F32, name + "_half", half_tag)
+            nc.vector.tensor_copy(out=dealt(got), in_=pool_tile[:].bitcast(U32).indirect(offsets[:]))
+            for j in range(CHUNKS):
+                nc.tensor.transpose(bank[:, 2 * j:2 * j + P], got[:, j * P:(j + 1) * P].bitcast(F32), ident32[:])
+            nc.scalar.activation(out=half[:], in_=bank[:, 0:2 * CHUNKS:2], func=ACT.Copy, scale=0.5)
+            return half
 
         k_codes = tiles(SLOT_PASSES, [P, D_PASSES * K_PASS], U16, "k_codes")
 
-        def keys(g):
-            kw_got = sb.tile([P, K_PASS], U32, name="kw_got", tag="got%d" % (g + 1), align_bytes=64)
-            nc.vector.tensor_copy(out=kw_got[:], in_=kw_pool[:].bitcast(U32).indirect(listed(g)))
+        def gather_words(g):
+            got = sbuf([P, K_PASS], U32, "kw_got")
+            nc.vector.tensor_copy(out=got[:], in_=kw_pool[:, 0:reach(g)].bitcast(U32).indirect(listed(g)))
+            return got
+
+        def part_words(g, got):
             nc.vector.tensor_copy(
                 out=k_codes[g][:].rearrange("p (o t b c) -> p b t o c", o=D_PASSES, t=PACK, c=RUN),
-                in_=kw_got[:].bitcast(U16).rearrange("p (b t c o) -> p b t o c", o=D_PASSES, t=PACK, c=RUN))
+                in_=got[:].bitcast(U16).rearrange("p (b t c o) -> p b t o c", o=D_PASSES, t=PACK, c=RUN))
 
-        capped = tiles(SLOT_PASSES, [P, PACK, NQ], F32, "capped")
-        u = tiles(SLOT_PASSES * Q_TILES, [P, P, PACK], F32, "u")
+        half_kb = half_columns(kb_pool, "kb", "kb_bank", None)
+        nc.vector.quantize_mx(out=q_codes[:].bitcast(FP8X4), scales=q_plane[:],
+                              in_=q_bf[:].rearrange("p o q t -> p (o q t)"))
+        for g in range(SLOT_PASSES):
+            part_words(g, gather_words(g))
 
-        def scores(g):
+        capped = tiles(SLOT_PASSES, [P, PACK * NQ], F32, "capped")
+        u = tiles(SLOT_PASSES, [P, PACK * NQ], F32, "u")
+        w_rows = tiles(SLOT_PASSES, [P, PACK, NQ], BF16, "w_rows")
+        for g in range(SLOT_PASSES):
             for pair in range(PACK // 2):
                 bank = ps.tile([P, 2, NQ], F32, name="score", tag="score%d" % (2 * g + pair))
                 for j in range(2):
@@ -137,7 +152,7 @@ def tile_attend_sigm_cap_kb_srtq256n1024t2048_kernel(tc, qT, k_words, k_scales, 
                     for qh in range(Q_TILES):
                         for o in range(D_PASSES):
                             kc = o * K_PASS + t * P
-                            sc = t * SLOT_PASSES * P + g * P
+                            sc = (t * SLOT_PASSES + g) * P
                             qc = o * NQ + qh * P
                             nc.tensor.matmul_mx(
                                 out=bank[:, j, qh * P:(qh + 1) * P],
@@ -148,80 +163,59 @@ def tile_attend_sigm_cap_kb_srtq256n1024t2048_kernel(tc, qT, k_words, k_scales, 
                                 start=(o == 0), stop=(o == D_PASSES - 1))
                 for j in range(2):
                     t = 2 * pair + j
-                    nc.scalar.activation(out=capped[g][:, t, :], in_=bank[:, j, :], func=ACT.Tanh,
-                                         bias=half_kb[g][:, t:t + 1], scale=0.5)
-            for qh in range(Q_TILES):
-                nc.scalar.activation(
-                    out=u[Q_TILES * g + qh][:].rearrange("p (c i) t -> p c t i", i=4),
-                    in_=capped[g][:, :, qh * P:(qh + 1) * P].rearrange("p t (c i) -> p c t i", i=4),
-                    func=ACT.Tanh)
+                    col = t * SLOT_PASSES + g
+                    nc.scalar.activation(out=capped[g][:, t * NQ:(t + 1) * NQ], in_=bank[:, j, :], func=ACT.Tanh,
+                                         bias=half_kb[:, col:col + 1], scale=0.5)
+            nc.scalar.activation(out=u[g][:], in_=capped[g][:], func=ACT.Tanh)
 
-        v_got = tiles(SLOT_PASSES * V_TILES, [P, K_PASS], BF16, "v_got")
-        v_bf = tiles(SLOT_PASSES, [P, V_TILES, P, PACK], BF16, "v_bf")
+        half_vs = half_columns(vs_pool, "vs", "score0", "capped1")
+        for g in range(SLOT_PASSES):
+            for t in range(PACK):
+                col = t * SLOT_PASSES + g
+                nc.scalar.activation(out=w_rows[g][:, t, :], in_=u[g][:, t * NQ:(t + 1) * NQ], func=ACT.Identity,
+                                     bias=half_vs[:, col:col + 1], scale=half_vs[:, col:col + 1])
+
+        v_bf = sbuf([P, SLOT_PASSES, V_TILES, P, PACK], BF16, "v_bf", "u1")
+        got = sbuf([P, N], BF16, "v_got_low")
+        bank = ps.tile([P, PACK, SLOT_PASSES, P], BF16, name="v_bank_low", tag="score1")
+        nc.vector.tensor_copy(out=dealt(got), in_=v_pool[:, 0:T].indirect(offsets[:]))
+        for t in range(PACK):
+            for g in range(SLOT_PASSES):
+                col = (t * SLOT_PASSES + g) * P
+                nc.tensor.transpose(bank[:, t, g, :], got[:, col:col + P], ident16[:])
+        nc.scalar.copy(out=v_bf[:, :, 0], in_=bank[:].rearrange("p t g e -> p g e t"))
+        for g in range(SLOT_PASSES):
+            got = sbuf([P, K_PASS], BF16, "v_got_high%d" % g)
+            bank = ps.tile([P, PACK, P], BF16, name="v_bank_high", tag="score%d" % (2 + g))
+            nc.vector.tensor_copy(out=dealt(got), in_=v_pool[:, T:2 * T].indirect(listed(g)))
+            for t in range(PACK):
+                nc.tensor.transpose(bank[:, t, :], got[:, t * P:(t + 1) * P], ident16[:])
+            nc.scalar.copy(out=v_bf[:, g, 1], in_=bank[:].rearrange("p t e -> p e t"))
+
+        w_bf = late.tile([P, SLOT_PASSES, NQ, PACK], BF16, name="w_bf", align_bytes=64, offset=8 * T)
+        w_codes = tiles(SLOT_PASSES, [P, NQ], U32, "w_codes")
+        w_plane = tiles(SLOT_PASSES, [P, NQ], U8, "w_plane")
         v_codes = tiles(SLOT_PASSES, [P, DV], U32, "v_codes")
         v_plane = tiles(SLOT_PASSES, [P, DV], U8, "v_plane")
-
-        def values(g):
-            bank = ps.tile([P, V_TILES, PACK, P], BF16, name="v_bank%d" % g)
-            for h in range(V_TILES):
-                got = v_got[V_TILES * g + h]
-                nc.vector.tensor_copy(out=dealt(got), in_=v_pool[h][:].indirect(listed(g)))
-                for t in range(PACK):
-                    nc.tensor.transpose(bank[:, h, t, :], got[:, t * P:(t + 1) * P], ident16[:])
-            nc.scalar.copy(out=v_bf[g][:], in_=bank[:].rearrange("p h t e -> p h e t"))
-
-        def quantise_values(g):
-            nc.vector.quantize_mx(out=v_codes[g][:].bitcast(FP8X4), scales=v_plane[g][:],
-                                  in_=v_bf[g][:].rearrange("p h e t -> p (h e t)"))
-
-        w_codes = tiles(SLOT_PASSES * Q_TILES, [P, P], U32, "w_codes")
-        w_plane = tiles(SLOT_PASSES * Q_TILES, [P, P], U8, "w_plane")
-
-        def weights(g, qh):
-            i = Q_TILES * g + qh
-            nc.vector.scalar_tensor_tensor(
-                out=w_all[:, i * K_PASS:(i + 1) * K_PASS].rearrange("p (q t) -> p q t", t=PACK), in0=u[i][:], scalar=1.0,
-                in1=half_vs[g][:].unsqueeze(1).to_broadcast([P, P, PACK]),
-                op0=ALU.add, op1=ALU.mult)
-
-        def quantise_weights(g, qh):
-            i = Q_TILES * g + qh
-            nc.vector.quantize_mx(out=w_codes[i][:].bitcast(FP8X4), scales=w_plane[i][:],
-                                  in_=w_all[:, i * K_PASS:(i + 1) * K_PASS])
-
-        columns(kb_pool, 0, "got0", half_kb[0])
-        keys(0)
-        nc.vector.quantize_mx(out=q_codes[:].bitcast(FP8X4), scales=q_plane[:],
-                              in_=q_bf[:].rearrange("p o q t -> p (o q t)"))
-        scores(0)
-        keys(1)
-        columns(kb_pool, 1, "got1", half_kb[1])
-        scores(1)
-        columns(vs_pool, 0, "got2", half_vs[0])
-        values(0)
-        columns(vs_pool, 1, "got1", half_vs[1])
-        values(1)
-
-        w_all = sb.tile([P, SLOT_PASSES * Q_TILES * K_PASS], BF16, name="w_all", tag="v_pool1", align_bytes=64)
-        y_bank = [ps.tile([P, 2, NQ], F32, name="y_bank", tag="score%d" % qh) for qh in range(Q_TILES)]
+        y_bank = [ps.tile([P, DV], F32, name="y_bank%d" % qh) for qh in range(Q_TILES)]
         y = tiles(Q_TILES, [P, DV], F32, "y")
 
-        def product(g, qh):
-            i = Q_TILES * g + qh
-            nc.tensor.matmul_mx(
-                out=y_bank[qh][:, 0, :], lhsT=w_codes[i][:].bitcast(FP8X4), lhsT_scale=w_plane[i][:],
-                rhs=v_codes[g][:].bitcast(FP8X4), rhs_scale=v_plane[g][:],
-                start=(g == 0), stop=(g == SLOT_PASSES - 1))
-
         for g in range(SLOT_PASSES):
-            weights(g, 0)
-            weights(g, 1)
-            quantise_values(g)
+            nc.vector.tensor_copy(out=w_bf[:, g].rearrange("p (c i) t -> p c t i", i=4),
+                                  in_=w_rows[g][:].rearrange("p t (c i) -> p c t i", i=4))
+        for g in range(SLOT_PASSES):
+            nc.vector.quantize_mx(out=w_codes[g][:].bitcast(FP8X4), scales=w_plane[g][:],
+                                  in_=w_bf[:, g].rearrange("p q t -> p (q t)"))
+            nc.vector.quantize_mx(out=v_codes[g][:].bitcast(FP8X4), scales=v_plane[g][:],
+                                  in_=v_bf[:, g].rearrange("p h e t -> p (h e t)"))
             for qh in range(Q_TILES):
-                quantise_weights(g, qh)
-                product(g, qh)
+                nc.tensor.matmul_mx(
+                    out=y_bank[qh][:],
+                    lhsT=w_codes[g][:, qh * P:(qh + 1) * P].bitcast(FP8X4), lhsT_scale=w_plane[g][:, qh * P:(qh + 1) * P],
+                    rhs=v_codes[g][:].bitcast(FP8X4), rhs_scale=v_plane[g][:],
+                    start=(g == 0), stop=(g == SLOT_PASSES - 1))
 
-        nc.scalar.activation(out=y[0][:], in_=y_bank[0][:, 0, :], func=ACT.Copy, scale=1.0 / 16.0)
+        nc.scalar.activation(out=y[0][:], in_=y_bank[0][:], func=ACT.Copy, scale=1.0 / 16.0)
         nc.sync.dma_start(out=out[0, 0:P, :], in_=y[0][:])
-        nc.vector.tensor_scalar_mul(y[1][:], y_bank[1][:, 0, :], 1.0 / 16.0)
+        nc.vector.tensor_scalar_mul(y[1][:], y_bank[1][:], 1.0 / 16.0)
         nc.sync.dma_start(out=out[0, P:2 * P, :], in_=y[1][:])

@@ -12,6 +12,7 @@ U8 = mybir.dt.uint8
 FP8X4 = mybir.dt.float8_e4m3fn_x4
 FP4X4 = mybir.dt.float4_e2m1fn_x4
 ACT = mybir.ActivationFunctionType
+ALU = mybir.AluOpType
 
 P = 128
 NQ, N, T, D, DV = 256, 1024, 2048, 1024, 256
@@ -24,6 +25,7 @@ Q_TILES = NQ // P
 V_TILES = DV // P
 LIST_COLS = K_PASS // 16
 CHUNKS = PACK * SLOT_PASSES
+LAST = P - 1
 
 FLOPS = 2 * NQ * N * (D + DV)
 BYTES = 4 * D * NQ + 4 * P * T + 32 * T + 4 * DV * T + 2 * 4 * T + 2 * P * N // 16 + 4 * NQ * DV
@@ -42,6 +44,12 @@ def tile_attend_sigm_cap_kb_srtq256n1024t2048_kernel(tc, qT, k_words, k_scales, 
         def tiles(count, shape, dtype, name):
             return [sbuf(shape, dtype, "%s%d" % (name, i)) for i in range(count)]
 
+        def placed(shape, dtype, name, offset):
+            return late.tile(shape, dtype, name=name, align_bytes=64, offset=offset)
+
+        def bank(index, shape, dtype, name):
+            return ps.tile(shape, dtype, name=name, tag="bank%d" % index)
+
         offsets = sb.tile([P, N // 16], U16, name="offsets")
         nc.sync.dma_start(offsets[:], offs)
 
@@ -55,14 +63,14 @@ def tile_attend_sigm_cap_kb_srtq256n1024t2048_kernel(tc, qT, k_words, k_scales, 
             return tile[:].rearrange("p (t b c) -> p b t c", t=PACK, c=RUN)
 
         ks_pool = sbuf([P, T], U8, "ks_pool")
-        kb_pool = late.tile([P, T], F32, name="kb_pool", align_bytes=64, offset=2 * T)
+        kb_pool = placed([P, T], F32, "kb_pool", 8192)
+        vs_pool = sbuf([P, T], F32, "vs_pool")
         kw_pool = sbuf([P, T], I32, "kw_pool")
-        q_raw = tiles(D_PASSES, [P, PACK, NQ], F32, "q_raw")
+        q_raw = [placed([P, PACK, NQ], F32, "q_raw%d" % o, 28672 + 4096 * o) for o in range(D_PASSES)]
         k_plane = tiles(D_PASSES, [P, N], U8, "k_plane")
 
-        nc.gpsimd.memset(ks_pool[:, 0:T // 2].bitcast(I32), 0)
-        nc.vector.memset(ks_pool[:, T // 2:T].bitcast(I32), 0)
-        nc.vector.memset(kb_pool[:].bitcast(I32), 0)
+        nc.gpsimd.memset(ks_pool[:].bitcast(I32), 0)
+        nc.vector.memset(kb_pool[0:LAST, :].bitcast(I32), 0)
         nc.vector.memset(k_plane[1][:].bitcast(I32), 0)
 
         warm_in = sbuf([P, 1], F32, "warm_in")
@@ -74,59 +82,48 @@ def tile_attend_sigm_cap_kb_srtq256n1024t2048_kernel(tc, qT, k_words, k_scales, 
         ident16 = sbuf([P, P], BF16, "ident16")
         make_identity(nc, ident32[:])
         nc.scalar.copy(out=ident16[:], in_=ident32[:])
+        nc.gpsimd.memset(vs_pool[0:LAST, :].bitcast(I32), 0)
 
-        for quad in range(4):
-            nc.sync.dma_start(out=ks_pool[32 * quad:32 * quad + 8, :].bitcast(I32),
-                              in_=k_scales[:, 4 * quad:4 * quad + 4, :].bitcast(I32))
-
-        def load_queries(o):
+        nc.sync.dma_start(out=kb_pool[LAST:P, :], in_=kb[LAST:P, :])
+        for r in range(4):
+            nc.sync.dma_start(out=ks_pool[r:P:16, :].bitcast(I32),
+                              in_=k_scales[:, r:16:4, :].rearrange("o q t -> q o t").bitcast(I32))
+        for o in range(D_PASSES):
             rows = qT[0, o * K_PASS:(o + 1) * K_PASS, :]
             nc.sync.dma_start(out=q_raw[o][:], in_=rows.rearrange("(p t) q -> p t q", t=PACK))
-
-        load_queries(0)
-        nc.sync.dma_start(out=kb_pool[0:1, :], in_=kb[0:1, :])
-        load_queries(1)
+        v_low = sbuf([P, T], F32, "v_low")
+        nc.sync.dma_start(out=v_low[:], in_=vT[0:P, :])
         words = k_words[0].rearrange("p t b -> p (t b)").bitcast(I32)
         nc.sync.dma_start(out=kw_pool[:, 0:reach(0)], in_=words[:, 0:reach(0)])
         nc.sync.dma_start(out=kw_pool[:, reach(0):T], in_=words[:, reach(0):T])
+        nc.sync.dma_start(out=vs_pool[LAST:P, :], in_=vs[LAST:P, :])
 
-        q_bf = sbuf([P, D_PASSES, NQ, PACK], BF16, "q_bf")
+        q_bf = placed([P, D_PASSES, NQ, PACK], BF16, "q_bf", 0)
         q_codes = sbuf([P, D_PASSES * NQ], U32, "q_codes")
         q_plane = sbuf([P, D_PASSES * NQ], U8, "q_plane")
-
-        def weave_queries(o):
+        for o in range(D_PASSES):
             nc.scalar.copy(out=q_bf[:, o].rearrange("p (c i) t -> p c t i", i=4),
                            in_=q_raw[o][:].rearrange("p t (c i) -> p c t i", i=4))
 
-        weave_queries(0)
+        v_low_bf = sbuf([P, T], BF16, "v_low_bf")
+        v_got_low = sbuf([P, N], BF16, "v_got_low")
+        nc.scalar.activation(out=v_low_bf[:], in_=v_low[:], func=ACT.Copy)
+        nc.scalar.activation(out=dealt(v_got_low), in_=v_low_bf[:].indirect(offsets[:]), func=ACT.Copy)
 
-        ks_got = sbuf([P, N], U8, "ks_got")
-        nc.vector.tensor_copy(out=ks_got[:], in_=ks_pool[:].indirect(offsets[:]))
-        nc.vector.tensor_copy(
-            out=k_plane[0][:].bitcast(I32).rearrange("p (t b w) -> p b t w", t=PACK, w=2),
-            in_=ks_got[:].bitcast(I32).rearrange("p (b t w) -> p b t w", t=PACK, w=2))
-        nc.sync.dma_start(out=k_plane[1][0:100, :].bitcast(I32), in_=k_plane[0][4:104, :].bitcast(I32))
-        weave_queries(1)
-        vs_pool = late.tile([P, T], F32, name="vs_pool", align_bytes=64, offset=0)
-        v_pool = late.tile([P, V_TILES * T], F32, name="v_pool", align_bytes=64, offset=4 * T)
-        nc.sync.dma_start(out=vs_pool[:], in_=vs)
-        for h in range(V_TILES):
-            nc.sync.dma_start(out=v_pool[:, h * T:(h + 1) * T], in_=vT[h * P:(h + 1) * P, :])
-
-        def half_columns(pool_tile, name, bank_tag, half_tag):
-            got = sbuf([P, N], U32, name + "_got")
-            bank = ps.tile([P, 512], F32, name=name + "_bank", tag=bank_tag)
-            half = sbuf([P, CHUNKS], F32, name + "_half", half_tag)
+        def half_columns(pool_tile, got, banks, half, name):
             nc.vector.tensor_copy(out=dealt(got), in_=pool_tile[:].bitcast(U32).indirect(offsets[:]))
-            for j in range(CHUNKS):
-                nc.tensor.transpose(bank[:, 2 * j:2 * j + P], got[:, j * P:(j + 1) * P].bitcast(F32), ident32[:])
-            nc.scalar.activation(out=half[:], in_=bank[:, 0:2 * CHUNKS:2], func=ACT.Copy, scale=0.5)
+            for g in range(SLOT_PASSES):
+                turned = bank(banks[g], [P, PACK, P], F32, name + "_turned")
+                for t in range(PACK):
+                    col = (t * SLOT_PASSES + g) * P
+                    nc.tensor.transpose(turned[:, t, :], got[:, col:col + P].bitcast(F32), ident32[:])
+                nc.scalar.activation(out=half[g][:], in_=turned[:, :, LAST], func=ACT.Copy, scale=0.5)
             return half
 
         k_codes = tiles(SLOT_PASSES, [P, D_PASSES * K_PASS], U16, "k_codes")
 
         def gather_words(g):
-            got = sbuf([P, K_PASS], U32, "kw_got")
+            got = placed([P, K_PASS], U32, "kw_got%d" % g, (17408, 16384)[g])
             nc.vector.tensor_copy(out=got[:], in_=kw_pool[:, 0:reach(g)].bitcast(U32).indirect(listed(g)))
             return got
 
@@ -135,69 +132,84 @@ def tile_attend_sigm_cap_kb_srtq256n1024t2048_kernel(tc, qT, k_words, k_scales, 
                 out=k_codes[g][:].rearrange("p (o t b c) -> p b t o c", o=D_PASSES, t=PACK, c=RUN),
                 in_=got[:].bitcast(U16).rearrange("p (b t c o) -> p b t o c", o=D_PASSES, t=PACK, c=RUN))
 
-        half_kb = half_columns(kb_pool, "kb", "kb_bank", None)
+        half_kb = half_columns(kb_pool, sbuf([P, N], U32, "kb_got"), (4, 5),
+                               [placed([P, PACK], F32, "half_kb%d" % g, 32768 + 64 * g) for g in range(SLOT_PASSES)], "kb")
+        ks_got = sbuf([P, N], U8, "ks_got")
+        nc.vector.tensor_copy(out=ks_got[:], in_=ks_pool[:].indirect(offsets[:]))
+        nc.vector.tensor_copy(
+            out=k_plane[0][:].bitcast(I32).rearrange("p (t b w) -> p b t w", t=PACK, w=2),
+            in_=ks_got[:].bitcast(I32).rearrange("p (b t w) -> p b t w", t=PACK, w=2))
+        for quad in range(4):
+            nc.sync.dma_start(out=k_plane[1][32 * quad:32 * quad + 4, :].bitcast(I32),
+                              in_=k_plane[0][32 * quad + 16:32 * quad + 20, :].bitcast(I32))
+
+        got = gather_words(0)
         nc.vector.quantize_mx(out=q_codes[:].bitcast(FP8X4), scales=q_plane[:],
                               in_=q_bf[:].rearrange("p o q t -> p (o q t)"))
-        for g in range(SLOT_PASSES):
-            part_words(g, gather_words(g))
+        part_words(0, got)
+        v_high = placed([P, T], F32, "v_high", 0)
+        nc.sync.dma_start(out=v_high[:], in_=vT[P:2 * P, :])
 
-        capped = tiles(SLOT_PASSES, [P, PACK * NQ], F32, "capped")
+        capped = [placed([P, PACK * NQ], F32, "capped%d" % g, 20480 + 4096 * g) for g in range(SLOT_PASSES)]
         u = tiles(SLOT_PASSES, [P, PACK * NQ], F32, "u")
-        w_rows = tiles(SLOT_PASSES, [P, PACK, NQ], BF16, "w_rows")
-        for g in range(SLOT_PASSES):
-            for pair in range(PACK // 2):
-                bank = ps.tile([P, 2, NQ], F32, name="score", tag="score%d" % (2 * g + pair))
-                for j in range(2):
-                    t = 2 * pair + j
-                    for qh in range(Q_TILES):
-                        for o in range(D_PASSES):
-                            kc = o * K_PASS + t * P
-                            sc = (t * SLOT_PASSES + g) * P
-                            qc = o * NQ + qh * P
-                            nc.tensor.matmul_mx(
-                                out=bank[:, j, qh * P:(qh + 1) * P],
-                                lhsT=k_codes[g][:, kc:kc + P].bitcast(FP4X4),
-                                lhsT_scale=k_plane[o][:, sc:sc + P],
-                                rhs=q_codes[:, qc:qc + P].bitcast(FP8X4),
-                                rhs_scale=q_plane[:, qc:qc + P],
-                                start=(o == 0), stop=(o == D_PASSES - 1))
-                for j in range(2):
-                    t = 2 * pair + j
-                    col = t * SLOT_PASSES + g
-                    nc.scalar.activation(out=capped[g][:, t * NQ:(t + 1) * NQ], in_=bank[:, j, :], func=ACT.Tanh,
-                                         bias=half_kb[:, col:col + 1], scale=0.5)
+
+        def weigh(g):
+            for t in range(PACK):
+                score = bank(t, [P, NQ], F32, "score")
+                for qh in range(Q_TILES):
+                    for o in reversed(range(D_PASSES)):
+                        kc = o * K_PASS + t * P
+                        sc = (t * SLOT_PASSES + g) * P
+                        qc = o * NQ + qh * P
+                        nc.tensor.matmul_mx(
+                            out=score[:, qh * P:(qh + 1) * P],
+                            lhsT=k_codes[g][:, kc:kc + P].bitcast(FP4X4),
+                            lhsT_scale=k_plane[o][:, sc:sc + P],
+                            rhs=q_codes[:, qc:qc + P].bitcast(FP8X4),
+                            rhs_scale=q_plane[:, qc:qc + P],
+                            start=(o == D_PASSES - 1), stop=(o == 0))
+                nc.scalar.activation(out=capped[g][:, t * NQ:(t + 1) * NQ], in_=score[:], func=ACT.Tanh,
+                                     bias=half_kb[g][:, t:t + 1], scale=0.5)
             nc.scalar.activation(out=u[g][:], in_=capped[g][:], func=ACT.Tanh)
 
-        half_vs = half_columns(vs_pool, "vs", "score0", "capped1")
-        for g in range(SLOT_PASSES):
-            for t in range(PACK):
-                col = t * SLOT_PASSES + g
-                nc.scalar.activation(out=w_rows[g][:, t, :], in_=u[g][:, t * NQ:(t + 1) * NQ], func=ACT.Identity,
-                                     bias=half_vs[:, col:col + 1], scale=half_vs[:, col:col + 1])
+        weigh(0)
+        got = gather_words(1)
+        part_words(1, got)
+        weigh(1)
 
-        v_bf = sbuf([P, SLOT_PASSES, V_TILES, P, PACK], BF16, "v_bf", "u1")
-        got = sbuf([P, N], BF16, "v_got_low")
-        bank = ps.tile([P, PACK, SLOT_PASSES, P], BF16, name="v_bank_low", tag="score1")
-        nc.vector.tensor_copy(out=dealt(got), in_=v_pool[:, 0:T].indirect(offsets[:]))
+        half_vs = [placed([P, PACK], F32, "half_vs%d" % g, 24576 + 64 * g) for g in range(SLOT_PASSES)]
+        half_columns(vs_pool, placed([P, N], U32, "vs_got", 16384), (0, 1), half_vs, "vs")
+        w_rows = [sbuf([P, PACK, NQ], BF16, "w_rows0")]
+        for t in range(PACK):
+            nc.scalar.activation(out=w_rows[0][:, t, :], in_=u[0][:, t * NQ:(t + 1) * NQ], func=ACT.Identity,
+                                 bias=half_vs[0][:, t:t + 1], scale=half_vs[0][:, t:t + 1])
+
+        v_bf = sbuf([P, SLOT_PASSES, V_TILES, P, PACK], BF16, "v_bf", "u0")
+        turned = bank(2, [P, PACK, SLOT_PASSES, P], BF16, "v_turned_low")
         for t in range(PACK):
             for g in range(SLOT_PASSES):
                 col = (t * SLOT_PASSES + g) * P
-                nc.tensor.transpose(bank[:, t, g, :], got[:, col:col + P], ident16[:])
-        nc.scalar.copy(out=v_bf[:, :, 0], in_=bank[:].rearrange("p t g e -> p g e t"))
+                nc.tensor.transpose(turned[:, t, g, :], v_got_low[:, col:col + P], ident16[:])
+        nc.scalar.copy(out=v_bf[:, :, 0], in_=turned[:].rearrange("p t g e -> p g e t"))
         for g in range(SLOT_PASSES):
             got = sbuf([P, K_PASS], BF16, "v_got_high%d" % g)
-            bank = ps.tile([P, PACK, P], BF16, name="v_bank_high", tag="score%d" % (2 + g))
-            nc.vector.tensor_copy(out=dealt(got), in_=v_pool[:, T:2 * T].indirect(listed(g)))
+            turned = bank((3, 0)[g], [P, PACK, P], BF16, "v_turned_high")
+            nc.vector.tensor_copy(out=dealt(got), in_=v_high[:].indirect(listed(g)))
             for t in range(PACK):
-                nc.tensor.transpose(bank[:, t, :], got[:, t * P:(t + 1) * P], ident16[:])
-            nc.scalar.copy(out=v_bf[:, g, 1], in_=bank[:].rearrange("p t e -> p e t"))
+                nc.tensor.transpose(turned[:, t, :], got[:, t * P:(t + 1) * P], ident16[:])
+            nc.scalar.copy(out=v_bf[:, g, 1], in_=turned[:].rearrange("p t e -> p e t"))
 
-        w_bf = late.tile([P, SLOT_PASSES, NQ, PACK], BF16, name="w_bf", align_bytes=64, offset=8 * T)
+        w_rows.append(placed([P, PACK, NQ], BF16, "w_rows1", 4096))
+        for t in range(PACK):
+            nc.vector.tensor_scalar(out=w_rows[1][:, t, :], in0=u[1][:, t * NQ:(t + 1) * NQ],
+                                    scalar1=half_vs[1][:, t:t + 1], scalar2=half_vs[1][:, t:t + 1],
+                                    op0=ALU.mult, op1=ALU.add)
+        w_bf = placed([P, SLOT_PASSES, NQ, PACK], BF16, "w_bf", 0)
         w_codes = tiles(SLOT_PASSES, [P, NQ], U32, "w_codes")
         w_plane = tiles(SLOT_PASSES, [P, NQ], U8, "w_plane")
         v_codes = tiles(SLOT_PASSES, [P, DV], U32, "v_codes")
         v_plane = tiles(SLOT_PASSES, [P, DV], U8, "v_plane")
-        y_bank = [ps.tile([P, DV], F32, name="y_bank%d" % qh) for qh in range(Q_TILES)]
+        y_bank = [bank(6 + qh, [P, DV], F32, "y_bank") for qh in range(Q_TILES)]
         y = tiles(Q_TILES, [P, DV], F32, "y")
 
         for g in range(SLOT_PASSES):

@@ -70,7 +70,8 @@ def tile_attend_sigm_cap_kb_srtq256n1024t2048_kernel(tc, qT, k_words, k_scales, 
         k_plane = tiles(D_PASSES, [P, N], U8, "k_plane")
 
         nc.gpsimd.memset(ks_pool[:].bitcast(I32), 0)
-        nc.vector.memset(kb_pool[0:LAST, :].bitcast(I32), 0)
+        nc.vector.memset(kb_pool[0:LAST, 0:T // 2].bitcast(I32), 0)
+        nc.gpsimd.memset(kb_pool[0:LAST, T // 2:T].bitcast(I32), 0)
         nc.vector.memset(k_plane[1][:].bitcast(I32), 0)
 
         warm_in = sbuf([P, 1], F32, "warm_in")
@@ -92,11 +93,10 @@ def tile_attend_sigm_cap_kb_srtq256n1024t2048_kernel(tc, qT, k_words, k_scales, 
             rows = qT[0, o * K_PASS:(o + 1) * K_PASS, :]
             nc.sync.dma_start(out=q_raw[o][:], in_=rows.rearrange("(p t) q -> p t q", t=PACK))
         v_low = sbuf([P, T], F32, "v_low")
-        nc.sync.dma_start(out=v_low[:], in_=vT[0:P, :])
         words = k_words[0].rearrange("p t b -> p (t b)").bitcast(I32)
-        nc.sync.dma_start(out=kw_pool[:, 0:reach(0)], in_=words[:, 0:reach(0)])
-        nc.sync.dma_start(out=kw_pool[:, reach(0):T], in_=words[:, reach(0):T])
-        nc.sync.dma_start(out=vs_pool[LAST:P, :], in_=vs[LAST:P, :])
+        for cols in (slice(0, reach(0)), slice(reach(0), T)):
+            nc.sync.dma_start(out=v_low[:, cols], in_=vT[0:P, cols])
+            nc.sync.dma_start(out=kw_pool[:, cols], in_=words[:, cols])
 
         q_bf = placed([P, D_PASSES, NQ, PACK], BF16, "q_bf", 0)
         q_codes = sbuf([P, D_PASSES * NQ], U32, "q_codes")
@@ -106,24 +106,30 @@ def tile_attend_sigm_cap_kb_srtq256n1024t2048_kernel(tc, qT, k_words, k_scales, 
                            in_=q_raw[o][:].rearrange("p t (c i) -> p c t i", i=4))
 
         v_low_bf = sbuf([P, T], BF16, "v_low_bf")
-        v_got_low = sbuf([P, N], BF16, "v_got_low")
-        nc.scalar.activation(out=v_low_bf[:], in_=v_low[:], func=ACT.Copy)
-        nc.scalar.activation(out=dealt(v_got_low), in_=v_low_bf[:].indirect(offsets[:]), func=ACT.Copy)
+        v_got_low = tiles(SLOT_PASSES, [P, K_PASS], BF16, "v_got_low")
+        for g, cols in enumerate((slice(0, reach(0)), slice(reach(0), T))):
+            nc.scalar.activation(out=v_low_bf[:, cols], in_=v_low[:, cols], func=ACT.Copy)
+            nc.scalar.activation(out=dealt(v_got_low[g]), in_=v_low_bf[:, 0:reach(g)].indirect(listed(g)),
+                                 func=ACT.Copy)
 
-        def half_columns(pool_tile, got, banks, half, name):
+        def turned_columns(pool_tile, got, banks, name):
             nc.vector.tensor_copy(out=dealt(got), in_=pool_tile[:].bitcast(U32).indirect(offsets[:]))
+            turned = [bank(banks[g], [P, PACK, P], F32, name + "_turned") for g in range(SLOT_PASSES)]
             for g in range(SLOT_PASSES):
-                turned = bank(banks[g], [P, PACK, P], F32, name + "_turned")
                 for t in range(PACK):
                     col = (t * SLOT_PASSES + g) * P
-                    nc.tensor.transpose(turned[:, t, :], got[:, col:col + P].bitcast(F32), ident32[:])
-                nc.scalar.activation(out=half[g][:], in_=turned[:, :, LAST], func=ACT.Copy, scale=0.5)
+                    nc.tensor.transpose(turned[g][:, t, :], got[:, col:col + P].bitcast(F32), ident32[:])
+            return turned
+
+        def halved(turned, half):
+            for g in range(SLOT_PASSES):
+                nc.scalar.activation(out=half[g][:], in_=turned[g][:, :, LAST], func=ACT.Copy, scale=0.5)
             return half
 
         k_codes = tiles(SLOT_PASSES, [P, D_PASSES * K_PASS], U16, "k_codes")
 
         def gather_words(g):
-            got = placed([P, K_PASS], U32, "kw_got%d" % g, (17408, 16384)[g])
+            got = sbuf([P, K_PASS], U32, "kw_got")
             nc.vector.tensor_copy(out=got[:], in_=kw_pool[:, 0:reach(g)].bitcast(U32).indirect(listed(g)))
             return got
 
@@ -132,16 +138,18 @@ def tile_attend_sigm_cap_kb_srtq256n1024t2048_kernel(tc, qT, k_words, k_scales, 
                 out=k_codes[g][:].rearrange("p (o t b c) -> p b t o c", o=D_PASSES, t=PACK, c=RUN),
                 in_=got[:].bitcast(U16).rearrange("p (b t c o) -> p b t o c", o=D_PASSES, t=PACK, c=RUN))
 
-        half_kb = half_columns(kb_pool, sbuf([P, N], U32, "kb_got"), (4, 5),
-                               [placed([P, PACK], F32, "half_kb%d" % g, 32768 + 64 * g) for g in range(SLOT_PASSES)], "kb")
+        kb_turned = turned_columns(kb_pool, sbuf([P, N], U32, "kb_got"), (4, 5), "kb")
         ks_got = sbuf([P, N], U8, "ks_got")
         nc.vector.tensor_copy(out=ks_got[:], in_=ks_pool[:].indirect(offsets[:]))
+        half_kb = halved(kb_turned, [placed([P, PACK], F32, "half_kb%d" % g, 32768 + 64 * g)
+                                     for g in range(SLOT_PASSES)])
         nc.vector.tensor_copy(
             out=k_plane[0][:].bitcast(I32).rearrange("p (t b w) -> p b t w", t=PACK, w=2),
             in_=ks_got[:].bitcast(I32).rearrange("p (b t w) -> p b t w", t=PACK, w=2))
         for quad in range(4):
             nc.sync.dma_start(out=k_plane[1][32 * quad:32 * quad + 4, :].bitcast(I32),
                               in_=k_plane[0][32 * quad + 16:32 * quad + 20, :].bitcast(I32))
+        nc.sync.dma_start(out=vs_pool[LAST:P, :], in_=vs[LAST:P, :])
 
         got = gather_words(0)
         nc.vector.quantize_mx(out=q_codes[:].bitcast(FP8X4), scales=q_plane[:],
@@ -151,7 +159,7 @@ def tile_attend_sigm_cap_kb_srtq256n1024t2048_kernel(tc, qT, k_words, k_scales, 
         nc.sync.dma_start(out=v_high[:], in_=vT[P:2 * P, :])
 
         capped = [placed([P, PACK * NQ], F32, "capped%d" % g, 20480 + 4096 * g) for g in range(SLOT_PASSES)]
-        u = tiles(SLOT_PASSES, [P, PACK * NQ], F32, "u")
+        u = tiles(SLOT_PASSES, [P, NQ, PACK], F32, "u")
 
         def weigh(g):
             for t in range(PACK):
@@ -170,63 +178,56 @@ def tile_attend_sigm_cap_kb_srtq256n1024t2048_kernel(tc, qT, k_words, k_scales, 
                             start=(o == D_PASSES - 1), stop=(o == 0))
                 nc.scalar.activation(out=capped[g][:, t * NQ:(t + 1) * NQ], in_=score[:], func=ACT.Tanh,
                                      bias=half_kb[g][:, t:t + 1], scale=0.5)
-            nc.scalar.activation(out=u[g][:], in_=capped[g][:], func=ACT.Tanh)
+            nc.scalar.activation(out=u[g][:].rearrange("p (c i) t -> p c t i", i=4),
+                                 in_=capped[g][:].rearrange("p (t c i) -> p c t i", t=PACK, i=4), func=ACT.Tanh)
 
         weigh(0)
         got = gather_words(1)
         part_words(1, got)
         weigh(1)
 
-        half_vs = [placed([P, PACK], F32, "half_vs%d" % g, 24576 + 64 * g) for g in range(SLOT_PASSES)]
-        half_columns(vs_pool, placed([P, N], U32, "vs_got", 16384), (0, 1), half_vs, "vs")
-        w_rows = [sbuf([P, PACK, NQ], BF16, "w_rows0")]
-        for t in range(PACK):
-            nc.scalar.activation(out=w_rows[0][:, t, :], in_=u[0][:, t * NQ:(t + 1) * NQ], func=ACT.Identity,
-                                 bias=half_vs[0][:, t:t + 1], scale=half_vs[0][:, t:t + 1])
+        vs_turned = turned_columns(vs_pool, sbuf([P, N], U32, "vs_got"), (4, 5), "vs")
 
-        v_bf = sbuf([P, SLOT_PASSES, V_TILES, P, PACK], BF16, "v_bf", "u0")
-        turned = bank(2, [P, PACK, SLOT_PASSES, P], BF16, "v_turned_low")
-        for t in range(PACK):
-            for g in range(SLOT_PASSES):
-                col = (t * SLOT_PASSES + g) * P
-                nc.tensor.transpose(turned[:, t, g, :], v_got_low[:, col:col + P], ident16[:])
-        nc.scalar.copy(out=v_bf[:, :, 0], in_=turned[:].rearrange("p t g e -> p g e t"))
+        half_vs = halved(vs_turned, tiles(SLOT_PASSES, [P, PACK], F32, "half_vs"))
+
+        v_got_high = sbuf([P, N], BF16, "v_got_high")
+        nc.vector.tensor_copy(out=dealt(v_got_high), in_=v_high[:].indirect(offsets[:]))
+        v_bf = [placed([P, V_TILES, P, PACK], BF16, "v_bf%d" % g, 24576 + 2048 * g) for g in range(SLOT_PASSES)]
         for g in range(SLOT_PASSES):
-            got = sbuf([P, K_PASS], BF16, "v_got_high%d" % g)
-            turned = bank((3, 0)[g], [P, PACK, P], BF16, "v_turned_high")
-            nc.vector.tensor_copy(out=dealt(got), in_=v_high[:].indirect(listed(g)))
+            turned = bank(2 + g, [P, PACK, V_TILES, P], BF16, "v_turned")
             for t in range(PACK):
-                nc.tensor.transpose(turned[:, t, :], got[:, t * P:(t + 1) * P], ident16[:])
-            nc.scalar.copy(out=v_bf[:, g, 1], in_=turned[:].rearrange("p t e -> p e t"))
+                col = (t * SLOT_PASSES + g) * P
+                nc.tensor.transpose(turned[:, t, 0, :], v_got_low[g][:, t * P:(t + 1) * P], ident16[:])
+                nc.tensor.transpose(turned[:, t, 1, :], v_got_high[:, col:col + P], ident16[:])
+            nc.scalar.copy(out=v_bf[g][:], in_=turned[:].rearrange("p t h e -> p h e t"))
 
-        w_rows.append(placed([P, PACK, NQ], BF16, "w_rows1", 4096))
-        for t in range(PACK):
-            nc.vector.tensor_scalar(out=w_rows[1][:, t, :], in0=u[1][:, t * NQ:(t + 1) * NQ],
-                                    scalar1=half_vs[1][:, t:t + 1], scalar2=half_vs[1][:, t:t + 1],
-                                    op0=ALU.mult, op1=ALU.add)
-        w_bf = placed([P, SLOT_PASSES, NQ, PACK], BF16, "w_bf", 0)
-        w_codes = tiles(SLOT_PASSES, [P, NQ], U32, "w_codes")
-        w_plane = tiles(SLOT_PASSES, [P, NQ], U8, "w_plane")
-        v_codes = tiles(SLOT_PASSES, [P, DV], U32, "v_codes")
-        v_plane = tiles(SLOT_PASSES, [P, DV], U8, "v_plane")
+        def quantised(source, width, name):
+            codes = sbuf([P, width], U32, name + "_codes")
+            plane = sbuf([P, width], U8, name + "_plane")
+            nc.vector.quantize_mx(out=codes[:].bitcast(FP8X4), scales=plane[:], in_=source)
+            return codes, plane
+
+        w_bf = [placed([P, NQ, PACK], BF16, "w_bf%d" % g, 2048 * g) for g in range(SLOT_PASSES)]
+        for g in range(SLOT_PASSES):
+            nc.vector.scalar_tensor_tensor(out=w_bf[g][:], in0=u[g][:], scalar=1.0,
+                                           in1=half_vs[g][:].unsqueeze(1).to_broadcast([P, NQ, PACK]),
+                                           op0=ALU.add, op1=ALU.mult)
+        w_first = quantised(w_bf[0][:].rearrange("p q t -> p (q t)"), NQ, "w_first")
+        v_mx = [quantised(v_bf[g][:].rearrange("p h e t -> p (h e t)"), DV, "v%d" % g) for g in range(SLOT_PASSES)]
+
+        def product(target, g, w_codes, w_plane):
+            nc.tensor.matmul_mx(out=target, lhsT=w_codes.bitcast(FP8X4), lhsT_scale=w_plane,
+                                rhs=v_mx[g][0][:].bitcast(FP8X4), rhs_scale=v_mx[g][1][:],
+                                start=(g == 0), stop=(g == SLOT_PASSES - 1))
+
         y_bank = [bank(6 + qh, [P, DV], F32, "y_bank") for qh in range(Q_TILES)]
         y = tiles(Q_TILES, [P, DV], F32, "y")
-
-        for g in range(SLOT_PASSES):
-            nc.vector.tensor_copy(out=w_bf[:, g].rearrange("p (c i) t -> p c t i", i=4),
-                                  in_=w_rows[g][:].rearrange("p t (c i) -> p c t i", i=4))
-        for g in range(SLOT_PASSES):
-            nc.vector.quantize_mx(out=w_codes[g][:].bitcast(FP8X4), scales=w_plane[g][:],
-                                  in_=w_bf[:, g].rearrange("p q t -> p (q t)"))
-            nc.vector.quantize_mx(out=v_codes[g][:].bitcast(FP8X4), scales=v_plane[g][:],
-                                  in_=v_bf[:, g].rearrange("p h e t -> p (h e t)"))
-            for qh in range(Q_TILES):
-                nc.tensor.matmul_mx(
-                    out=y_bank[qh][:],
-                    lhsT=w_codes[g][:, qh * P:(qh + 1) * P].bitcast(FP8X4), lhsT_scale=w_plane[g][:, qh * P:(qh + 1) * P],
-                    rhs=v_codes[g][:].bitcast(FP8X4), rhs_scale=v_plane[g][:],
-                    start=(g == 0), stop=(g == SLOT_PASSES - 1))
-
+        for qh in range(Q_TILES):
+            product(y_bank[qh][:], 0, w_first[0][:, qh * P:(qh + 1) * P], w_first[1][:, qh * P:(qh + 1) * P])
+        for qh in range(Q_TILES):
+            codes, plane = quantised(w_bf[1][:, qh * P:(qh + 1) * P, :].rearrange("p q t -> p (q t)"), P,
+                                     "w_second%d" % qh)
+            product(y_bank[qh][:], 1, codes[:], plane[:])
         nc.scalar.activation(out=y[0][:], in_=y_bank[0][:], func=ACT.Copy, scale=1.0 / 16.0)
         nc.sync.dma_start(out=out[0, 0:P, :], in_=y[0][:])
         nc.vector.tensor_scalar_mul(y[1][:], y_bank[1][:], 1.0 / 16.0)

@@ -83,7 +83,6 @@ def tile_attend_sigm_cap_kb_srtq256n1024t2048_kernel(tc, qT, k_words, k_scales, 
         ident16 = sbuf([P, P], BF16, "ident16")
         make_identity(nc, ident32[:])
         nc.scalar.copy(out=ident16[:], in_=ident32[:])
-        nc.gpsimd.memset(vs_pool[0:LAST, :].bitcast(I32), 0)
 
         nc.sync.dma_start(out=kb_pool[LAST:P, :], in_=kb[LAST:P, :])
         for r in range(4):
@@ -129,7 +128,7 @@ def tile_attend_sigm_cap_kb_srtq256n1024t2048_kernel(tc, qT, k_words, k_scales, 
         k_codes = tiles(SLOT_PASSES, [P, D_PASSES * K_PASS], U16, "k_codes")
 
         def gather_words(g):
-            got = sbuf([P, K_PASS], U32, "kw_got")
+            got = sbuf([P, K_PASS], U32, "kw_got%d" % g)
             nc.vector.tensor_copy(out=got[:], in_=kw_pool[:, 0:reach(g)].bitcast(U32).indirect(listed(g)))
             return got
 
@@ -149,7 +148,7 @@ def tile_attend_sigm_cap_kb_srtq256n1024t2048_kernel(tc, qT, k_words, k_scales, 
         for quad in range(4):
             nc.sync.dma_start(out=k_plane[1][32 * quad:32 * quad + 4, :].bitcast(I32),
                               in_=k_plane[0][32 * quad + 16:32 * quad + 20, :].bitcast(I32))
-        nc.sync.dma_start(out=vs_pool[LAST:P, :], in_=vs[LAST:P, :])
+        nc.sync.dma_start(out=vs_pool[:], in_=vs)
 
         got = gather_words(0)
         nc.vector.quantize_mx(out=q_codes[:].bitcast(FP8X4), scales=q_plane[:],
@@ -192,14 +191,21 @@ def tile_attend_sigm_cap_kb_srtq256n1024t2048_kernel(tc, qT, k_words, k_scales, 
 
         v_got_high = sbuf([P, N], BF16, "v_got_high")
         nc.vector.tensor_copy(out=dealt(v_got_high), in_=v_high[:].indirect(offsets[:]))
-        v_bf = [placed([P, V_TILES, P, PACK], BF16, "v_bf%d" % g, 24576 + 2048 * g) for g in range(SLOT_PASSES)]
-        for g in range(SLOT_PASSES):
-            turned = bank(2 + g, [P, PACK, V_TILES, P], BF16, "v_turned")
+        v_first = placed([P, V_TILES, P, PACK], BF16, "v_first", 24576)
+        v_second = [placed([P, P, PACK], BF16, "v_second%d" % h, 26624 + 1024 * h) for h in range(V_TILES)]
+        turned = bank(2, [P, PACK, V_TILES, P], BF16, "v_turned")
+        for t in range(PACK):
+            col = t * SLOT_PASSES * P
+            nc.tensor.transpose(turned[:, t, 0, :], v_got_low[0][:, t * P:(t + 1) * P], ident16[:])
+            nc.tensor.transpose(turned[:, t, 1, :], v_got_high[:, col:col + P], ident16[:])
+        nc.scalar.copy(out=v_first[:], in_=turned[:].rearrange("p t h e -> p h e t"))
+        for h in range(V_TILES):
+            turned = bank((3, 0)[h], [P, PACK, P], BF16, "v_turned")
             for t in range(PACK):
-                col = (t * SLOT_PASSES + g) * P
-                nc.tensor.transpose(turned[:, t, 0, :], v_got_low[g][:, t * P:(t + 1) * P], ident16[:])
-                nc.tensor.transpose(turned[:, t, 1, :], v_got_high[:, col:col + P], ident16[:])
-            nc.scalar.copy(out=v_bf[g][:], in_=turned[:].rearrange("p t h e -> p h e t"))
+                col = (t * SLOT_PASSES + 1) * P
+                got = (v_got_low[1][:, t * P:(t + 1) * P], v_got_high[:, col:col + P])[h]
+                nc.tensor.transpose(turned[:, t, :], got, ident16[:])
+            nc.scalar.copy(out=v_second[h][:], in_=turned[:].rearrange("p t e -> p e t"))
 
         def quantised(source, width, name):
             codes = sbuf([P, width], U32, name + "_codes")
@@ -212,23 +218,29 @@ def tile_attend_sigm_cap_kb_srtq256n1024t2048_kernel(tc, qT, k_words, k_scales, 
             nc.vector.scalar_tensor_tensor(out=w_bf[g][:], in0=u[g][:], scalar=1.0,
                                            in1=half_vs[g][:].unsqueeze(1).to_broadcast([P, NQ, PACK]),
                                            op0=ALU.add, op1=ALU.mult)
-        w_first = quantised(w_bf[0][:].rearrange("p q t -> p (q t)"), NQ, "w_first")
-        v_mx = [quantised(v_bf[g][:].rearrange("p h e t -> p (h e t)"), DV, "v%d" % g) for g in range(SLOT_PASSES)]
+        w_mx = [quantised(w_bf[0][:].rearrange("p q t -> p (q t)"), NQ, "w0")]
+        v_first_mx = quantised(v_first[:].rearrange("p h e t -> p (h e t)"), DV, "v_first")
+        w_mx.append(quantised(w_bf[1][:].rearrange("p q t -> p (q t)"), NQ, "w1"))
 
-        def product(target, g, w_codes, w_plane):
-            nc.tensor.matmul_mx(out=target, lhsT=w_codes.bitcast(FP8X4), lhsT_scale=w_plane,
-                                rhs=v_mx[g][0][:].bitcast(FP8X4), rhs_scale=v_mx[g][1][:],
+        def product(target, qh, g, codes, plane):
+            cols = slice(qh * P, (qh + 1) * P)
+            nc.tensor.matmul_mx(out=target, lhsT=w_mx[g][0][:, cols].bitcast(FP8X4), lhsT_scale=w_mx[g][1][:, cols],
+                                rhs=codes.bitcast(FP8X4), rhs_scale=plane,
                                 start=(g == 0), stop=(g == SLOT_PASSES - 1))
 
-        y_bank = [bank(6 + qh, [P, DV], F32, "y_bank") for qh in range(Q_TILES)]
-        y = tiles(Q_TILES, [P, DV], F32, "y")
-        for qh in range(Q_TILES):
-            product(y_bank[qh][:], 0, w_first[0][:, qh * P:(qh + 1) * P], w_first[1][:, qh * P:(qh + 1) * P])
-        for qh in range(Q_TILES):
-            codes, plane = quantised(w_bf[1][:, qh * P:(qh + 1) * P, :].rearrange("p q t -> p (q t)"), P,
-                                     "w_second%d" % qh)
-            product(y_bank[qh][:], 1, codes[:], plane[:])
-        nc.scalar.activation(out=y[0][:], in_=y_bank[0][:], func=ACT.Copy, scale=1.0 / 16.0)
-        nc.sync.dma_start(out=out[0, 0:P, :], in_=y[0][:])
-        nc.vector.tensor_scalar_mul(y[1][:], y_bank[1][:], 1.0 / 16.0)
-        nc.sync.dma_start(out=out[0, P:2 * P, :], in_=y[1][:])
+        rows = out[0].rearrange("(qh p) e -> p qh e", p=P)
+        for h in range(V_TILES):
+            cols = slice(h * P, (h + 1) * P)
+            y_bank = [bank(4 + 2 * h + qh, [P, P], F32, "y_bank") for qh in range(Q_TILES)]
+            for qh in range(Q_TILES):
+                product(y_bank[qh][:], qh, 0, v_first_mx[0][:, cols], v_first_mx[1][:, cols])
+            codes, plane = quantised(v_second[h][:].rearrange("p e t -> p (e t)"), P, "v_second%d" % h)
+            for qh in range(Q_TILES):
+                product(y_bank[qh][:], qh, 1, codes[:], plane[:])
+            y = sbuf([P, Q_TILES, P], F32, "y%d" % h)
+            nc.scalar.activation(out=y[:, 0, :], in_=y_bank[0][:], func=ACT.Copy, scale=1.0 / 16.0)
+            if h == 0:
+                nc.scalar.activation(out=y[:, 1, :], in_=y_bank[1][:], func=ACT.Copy, scale=1.0 / 16.0)
+            else:
+                nc.vector.tensor_scalar_mul(y[:, 1, :], y_bank[1][:], 1.0 / 16.0)
+            nc.sync.dma_start(out=rows[:, :, cols], in_=y[:])

@@ -83,6 +83,7 @@ def tile_attend_sigm_cap_kb_srtq256n1024t2048_kernel(tc, qT, k_words, k_scales, 
         ident16 = sbuf([P, P], BF16, "ident16")
         make_identity(nc, ident32[:])
         nc.scalar.copy(out=ident16[:], in_=ident32[:])
+        nc.gpsimd.memset(vs_pool[0:LAST, :].bitcast(I32), 0)
 
         nc.sync.dma_start(out=kb_pool[LAST:P, :], in_=kb[LAST:P, :])
         for r in range(4):
@@ -148,7 +149,7 @@ def tile_attend_sigm_cap_kb_srtq256n1024t2048_kernel(tc, qT, k_words, k_scales, 
         for quad in range(4):
             nc.sync.dma_start(out=k_plane[1][32 * quad:32 * quad + 4, :].bitcast(I32),
                               in_=k_plane[0][32 * quad + 16:32 * quad + 20, :].bitcast(I32))
-        nc.sync.dma_start(out=vs_pool[:], in_=vs)
+        nc.sync.dma_start(out=vs_pool[LAST:P, :], in_=vs[LAST:P, :])
 
         got = gather_words(0)
         nc.vector.quantize_mx(out=q_codes[:].bitcast(FP8X4), scales=q_plane[:],

@@ -112,6 +112,17 @@ def tile_attend_sigm_cap_kb_srtq256n1024t2048_kernel(tc, qT, k_words, k_scales, 
             nc.scalar.activation(out=dealt(v_got_low[g]), in_=v_low_bf[:, 0:reach(g)].indirect(listed(g)),
                                  func=ACT.Copy)
 
+        def turn_values(got, first_col, step, index, woven):
+            turned = bank(index, [P, PACK, P], BF16, "v_turned")
+            for t in range(PACK):
+                col = first_col + t * step
+                nc.tensor.transpose(turned[:, t, :], got[:, col:col + P], ident16[:])
+            nc.scalar.copy(out=woven.rearrange("p (c i) t -> p c t i", i=4),
+                           in_=turned[:].rearrange("p t (c i) -> p c t i", i=4))
+
+        v_low_woven = sbuf([P, SLOT_PASSES, P, PACK], BF16, "v_low_woven")
+        turn_values(v_got_low[0], 0, P, 6, v_low_woven[:, 0])
+
         def turned_columns(pool_tile, got, banks, name):
             nc.vector.tensor_copy(out=dealt(got), in_=pool_tile[:].bitcast(U32).indirect(offsets[:]))
             turned = [bank(banks[g], [P, PACK, P], F32, name + "_turned") for g in range(SLOT_PASSES)]
@@ -192,21 +203,10 @@ def tile_attend_sigm_cap_kb_srtq256n1024t2048_kernel(tc, qT, k_words, k_scales, 
 
         v_got_high = sbuf([P, N], BF16, "v_got_high")
         nc.vector.tensor_copy(out=dealt(v_got_high), in_=v_high[:].indirect(offsets[:]))
-        v_first = placed([P, V_TILES, P, PACK], BF16, "v_first", 24576)
-        v_second = [placed([P, P, PACK], BF16, "v_second%d" % h, 26624 + 1024 * h) for h in range(V_TILES)]
-        turned = bank(2, [P, PACK, V_TILES, P], BF16, "v_turned")
-        for t in range(PACK):
-            col = t * SLOT_PASSES * P
-            nc.tensor.transpose(turned[:, t, 0, :], v_got_low[0][:, t * P:(t + 1) * P], ident16[:])
-            nc.tensor.transpose(turned[:, t, 1, :], v_got_high[:, col:col + P], ident16[:])
-        nc.scalar.copy(out=v_first[:], in_=turned[:].rearrange("p t h e -> p h e t"))
-        for h in range(V_TILES):
-            turned = bank((3, 0)[h], [P, PACK, P], BF16, "v_turned")
-            for t in range(PACK):
-                col = (t * SLOT_PASSES + 1) * P
-                got = (v_got_low[1][:, t * P:(t + 1) * P], v_got_high[:, col:col + P])[h]
-                nc.tensor.transpose(turned[:, t, :], got, ident16[:])
-            nc.scalar.copy(out=v_second[h][:], in_=turned[:].rearrange("p t e -> p e t"))
+        turn_values(v_got_low[1], 0, P, 3, v_low_woven[:, 1])
+        v_high_woven = [placed([P, P, PACK], BF16, "v_high_woven%d" % g, 24576 + 1024 * g) for g in range(SLOT_PASSES)]
+        for g in range(SLOT_PASSES):
+            turn_values(v_got_high, g * P, SLOT_PASSES * P, (2, 0)[g], v_high_woven[g][:])
 
         def quantised(source, width, name):
             codes = sbuf([P, width], U32, name + "_codes")
@@ -220,7 +220,7 @@ def tile_attend_sigm_cap_kb_srtq256n1024t2048_kernel(tc, qT, k_words, k_scales, 
                                            in1=half_vs[g][:].unsqueeze(1).to_broadcast([P, NQ, PACK]),
                                            op0=ALU.add, op1=ALU.mult)
         w_mx = [quantised(w_bf[0][:].rearrange("p q t -> p (q t)"), NQ, "w0")]
-        v_first_mx = quantised(v_first[:].rearrange("p h e t -> p (h e t)"), DV, "v_first")
+        v_low_mx = quantised(v_low_woven[:].rearrange("p g e t -> p (g e t)"), SLOT_PASSES * P, "v_low")
         w_mx.append(quantised(w_bf[1][:].rearrange("p q t -> p (q t)"), NQ, "w1"))
 
         def product(target, qh, g, codes, plane):
@@ -231,17 +231,19 @@ def tile_attend_sigm_cap_kb_srtq256n1024t2048_kernel(tc, qT, k_words, k_scales, 
 
         rows = out[0].rearrange("(qh p) e -> p qh e", p=P)
         for h in range(V_TILES):
-            cols = slice(h * P, (h + 1) * P)
             y_bank = [bank(4 + 2 * h + qh, [P, P], F32, "y_bank") for qh in range(Q_TILES)]
-            for qh in range(Q_TILES):
-                product(y_bank[qh][:], qh, 0, v_first_mx[0][:, cols], v_first_mx[1][:, cols])
-            codes, plane = quantised(v_second[h][:].rearrange("p e t -> p (e t)"), P, "v_second%d" % h)
-            for qh in range(Q_TILES):
-                product(y_bank[qh][:], qh, 1, codes[:], plane[:])
+            for g in range(SLOT_PASSES):
+                if h == 0:
+                    codes, plane = (part[:, g * P:(g + 1) * P] for part in v_low_mx)
+                else:
+                    codes, plane = (part[:] for part in quantised(
+                        v_high_woven[g][:].rearrange("p e t -> p (e t)"), P, "v_high%d" % g))
+                for qh in range(Q_TILES):
+                    product(y_bank[qh][:], qh, g, codes, plane)
             y = sbuf([P, Q_TILES, P], F32, "y%d" % h)
-            nc.scalar.activation(out=y[:, 0, :], in_=y_bank[0][:], func=ACT.Copy, scale=1.0 / 16.0)
             if h == 0:
-                nc.scalar.activation(out=y[:, 1, :], in_=y_bank[1][:], func=ACT.Copy, scale=1.0 / 16.0)
+                nc.vector.tensor_scalar_mul(y[:, 0, :], y_bank[0][:], 1.0 / 16.0)
             else:
-                nc.vector.tensor_scalar_mul(y[:, 1, :], y_bank[1][:], 1.0 / 16.0)
-            nc.sync.dma_start(out=rows[:, :, cols], in_=y[:])
+                nc.scalar.activation(out=y[:, 0, :], in_=y_bank[0][:], func=ACT.Copy, scale=1.0 / 16.0)
+            nc.vector.tensor_scalar_mul(y[:, 1, :], y_bank[1][:], 1.0 / 16.0)
+            nc.sync.dma_start(out=rows[:, :, h * P:(h + 1) * P], in_=y[:])

@@ -77,7 +77,7 @@ def tile_attend_sigm_cap_kb_srtq256n1024t2048_kernel(tc, qT, k_words, k_scales, 
         warm_in = sbuf([P, 1], F32, "warm_in")
         warm_out = sbuf([P, 1], F32, "warm_out")
         nc.gpsimd.memset(warm_in[:], 0.0)
-        nc.scalar.activation(out=warm_out[:], in_=warm_in[:], func=ACT.Tanh)
+        nc.scalar.activation(out=warm_out[:], in_=warm_in[:], func=ACT.Sigmoid)
 
         ident32 = sbuf([P, P], F32, "ident32")
         ident16 = sbuf([P, P], BF16, "ident16")
@@ -190,7 +190,8 @@ def tile_attend_sigm_cap_kb_srtq256n1024t2048_kernel(tc, qT, k_words, k_scales, 
                 nc.scalar.activation(out=capped[g][:, t * NQ:(t + 1) * NQ], in_=score[:], func=ACT.Tanh,
                                      bias=half_kb[g][:, t:t + 1], scale=0.5)
             nc.scalar.activation(out=u[g][:].rearrange("p (c i) t -> p c t i", i=4),
-                                 in_=capped[g][:].rearrange("p (t c i) -> p c t i", t=PACK, i=4), func=ACT.Tanh)
+                                 in_=capped[g][:].rearrange("p (t c i) -> p c t i", t=PACK, i=4),
+                                 func=ACT.Sigmoid, scale=2.0)
 
         weigh(0)
         got = gather_words(1)
@@ -198,8 +199,6 @@ def tile_attend_sigm_cap_kb_srtq256n1024t2048_kernel(tc, qT, k_words, k_scales, 
         weigh(1)
 
         vs_turned = turned_columns(vs_pool, sbuf([P, N], U32, "vs_got"), (4, 5), "vs")
-
-        half_vs = halved(vs_turned, tiles(SLOT_PASSES, [P, PACK], F32, "half_vs"))
 
         v_got_high = sbuf([P, N], BF16, "v_got_high")
         nc.vector.tensor_copy(out=dealt(v_got_high), in_=v_high[:].indirect(offsets[:]))
@@ -216,9 +215,9 @@ def tile_attend_sigm_cap_kb_srtq256n1024t2048_kernel(tc, qT, k_words, k_scales, 
 
         w_bf = [placed([P, NQ, PACK], BF16, "w_bf%d" % g, 2048 * g) for g in range(SLOT_PASSES)]
         for g in range(SLOT_PASSES):
-            nc.vector.scalar_tensor_tensor(out=w_bf[g][:], in0=u[g][:], scalar=1.0,
-                                           in1=half_vs[g][:].unsqueeze(1).to_broadcast([P, NQ, PACK]),
-                                           op0=ALU.add, op1=ALU.mult)
+            nc.vector.tensor_tensor(out=w_bf[g][:], in0=u[g][:],
+                                    in1=vs_turned[g][:, :, LAST].unsqueeze(1).to_broadcast([P, NQ, PACK]),
+                                    op=ALU.mult)
         w_mx = [quantised(w_bf[0][:].rearrange("p q t -> p (q t)"), NQ, "w0")]
         v_low_mx = quantised(v_low_woven[:].rearrange("p g e t -> p (g e t)"), SLOT_PASSES * P, "v_low")
         w_mx.append(quantised(w_bf[1][:].rearrange("p q t -> p (q t)"), NQ, "w1"))

@@ -24,7 +24,6 @@ D_PASSES = D // K_PASS
 Q_TILES = NQ // P
 V_TILES = DV // P
 LIST_COLS = K_PASS // 16
-CHUNKS = PACK * SLOT_PASSES
 LAST = P - 1
 
 FLOPS = 2 * NQ * N * (D + DV)
@@ -62,19 +61,18 @@ def tile_attend_sigm_cap_kb_srtq256n1024t2048_kernel(tc, qT, k_words, k_scales, 
         def dealt(tile):
             return tile[:].rearrange("p (t b c) -> p b t c", t=PACK, c=RUN)
 
+        head, tail = slice(0, reach(0)), slice(reach(0), T)
         ks_pool = sbuf([P, T], U8, "ks_pool")
-        kb_pool = placed([P, T], F32, "kb_pool", 8192)
-        vs_pool = sbuf([P, T], F32, "vs_pool")
+        kb_pool = sbuf([P, T], F32, "kb_pool")
         kw_pool = sbuf([P, T], I32, "kw_pool")
-        q_raw = [placed([P, PACK, NQ], F32, "q_raw%d" % o, 28672 + 4096 * o) for o in range(D_PASSES)]
         k_plane = tiles(D_PASSES, [P, N], U8, "k_plane")
 
-        nc.gpsimd.memset(ks_pool[:].bitcast(I32), 0)
+        nc.vector.memset(ks_pool[:].bitcast(I32), 0)
         nc.vector.memset(kb_pool[0:LAST, 0:T // 2].bitcast(I32), 0)
         nc.gpsimd.memset(kb_pool[0:LAST, T // 2:T].bitcast(I32), 0)
         nc.vector.memset(k_plane[1][:].bitcast(I32), 0)
 
-        warm_in = sbuf([P, 1], F32, "warm_in")
+        warm_in = sbuf([P, 1], F32, "warm_in", "vs_pool")
         warm_out = sbuf([P, 1], F32, "warm_out")
         nc.gpsimd.memset(warm_in[:], 0.0)
         nc.scalar.activation(out=warm_out[:], in_=warm_in[:], func=ACT.Sigmoid)
@@ -83,34 +81,62 @@ def tile_attend_sigm_cap_kb_srtq256n1024t2048_kernel(tc, qT, k_words, k_scales, 
         ident16 = sbuf([P, P], BF16, "ident16")
         make_identity(nc, ident32[:])
         nc.scalar.copy(out=ident16[:], in_=ident32[:])
+        vs_pool = sbuf([P, T], F32, "vs_pool")
         nc.gpsimd.memset(vs_pool[0:LAST, :].bitcast(I32), 0)
 
         nc.sync.dma_start(out=kb_pool[LAST:P, :], in_=kb[LAST:P, :])
+        q_raw = tiles(D_PASSES, [P, PACK, NQ], F32, "q_raw")
+
+        def load_queries(o):
+            rows = qT[0, o * K_PASS:(o + 1) * K_PASS, :]
+            nc.sync.dma_start(out=q_raw[o][:], in_=rows.rearrange("(p t) q -> p t q", t=PACK))
+
+        load_queries(0)
         for r in range(4):
             nc.sync.dma_start(out=ks_pool[r:P:16, :].bitcast(I32),
                               in_=k_scales[:, r:16:4, :].rearrange("o q t -> q o t").bitcast(I32))
-        for o in range(D_PASSES):
-            rows = qT[0, o * K_PASS:(o + 1) * K_PASS, :]
-            nc.sync.dma_start(out=q_raw[o][:], in_=rows.rearrange("(p t) q -> p t q", t=PACK))
-        v_low = sbuf([P, T], F32, "v_low")
+        load_queries(1)
+        v_low = [sbuf([P, reach(0)], F32, "v_low0"), sbuf([P, T - reach(0)], F32, "v_low1")]
         words = k_words[0].rearrange("p t b -> p (t b)").bitcast(I32)
-        for cols in (slice(0, reach(0)), slice(reach(0), T)):
-            nc.sync.dma_start(out=v_low[:, cols], in_=vT[0:P, cols])
-            nc.sync.dma_start(out=kw_pool[:, cols], in_=words[:, cols])
+        nc.sync.dma_start(out=v_low[0][:], in_=vT[0:P, head])
+        nc.sync.dma_start(out=kw_pool[:, head], in_=words[:, head])
+        nc.sync.dma_start(out=v_low[1][:], in_=vT[0:P, tail])
 
-        q_bf = placed([P, D_PASSES, NQ, PACK], BF16, "q_bf", 0)
+        q_bf = sbuf([P, D_PASSES, NQ, PACK], BF16, "q_bf")
         q_codes = sbuf([P, D_PASSES * NQ], U32, "q_codes")
         q_plane = sbuf([P, D_PASSES * NQ], U8, "q_plane")
         for o in range(D_PASSES):
             nc.scalar.copy(out=q_bf[:, o].rearrange("p (c i) t -> p c t i", i=4),
                            in_=q_raw[o][:].rearrange("p t (c i) -> p c t i", i=4))
 
+        def columns(got, first, count, index, name):
+            turned = bank(index, [P, P + count - 1], F32, name)
+            for j in reversed(range(count)):
+                col = (first + j) * P
+                nc.tensor.transpose(turned[:, j:j + P], got[:, col:col + P].bitcast(F32), ident32[:])
+            return turned[:, LAST:LAST + count]
+
+        kb_got = sbuf([P, N], U32, "kb_got")
+        nc.vector.tensor_copy(out=kb_got[:].rearrange("p (g t b c) -> p g b t c", g=SLOT_PASSES, t=PACK, c=RUN),
+                              in_=kb_pool[:].bitcast(U32).indirect(offsets[:]))
+        kb_cols = columns(kb_got, 0, SLOT_PASSES * PACK, 4, "kb_turned")
+        ks_got = sbuf([P, N], U8, "ks_got")
+        nc.vector.tensor_copy(out=ks_got[:], in_=ks_pool[:].indirect(offsets[:]))
+        nc.vector.tensor_copy(
+            out=k_plane[0][:].bitcast(I32).rearrange("p (t b w) -> p b t w", t=PACK, w=2),
+            in_=ks_got[:].bitcast(I32).rearrange("p (b t w) -> p b t w", t=PACK, w=2))
+        for quad in range(4):
+            nc.sync.dma_start(out=k_plane[1][32 * quad:32 * quad + 4, :].bitcast(I32),
+                              in_=k_plane[0][32 * quad + 16:32 * quad + 20, :].bitcast(I32))
+        nc.sync.dma_start(out=vs_pool[LAST:P, :], in_=vs[LAST:P, :])
+        nc.sync.dma_start(out=kw_pool[:, tail], in_=words[:, tail])
+        v_high = placed([P, T], F32, "v_high", 0)
+        nc.sync.dma_start(out=v_high[:], in_=vT[P:2 * P, :])
+        nc.vector.quantize_mx(out=q_codes[:].bitcast(FP8X4), scales=q_plane[:],
+                              in_=q_bf[:].rearrange("p o q t -> p (o q t)"))
+
         v_low_bf = sbuf([P, T], BF16, "v_low_bf")
-        v_got_low = tiles(SLOT_PASSES, [P, K_PASS], BF16, "v_got_low")
-        for g, cols in enumerate((slice(0, reach(0)), slice(reach(0), T))):
-            nc.scalar.activation(out=v_low_bf[:, cols], in_=v_low[:, cols], func=ACT.Copy)
-            nc.scalar.activation(out=dealt(v_got_low[g]), in_=v_low_bf[:, 0:reach(g)].indirect(listed(g)),
-                                 func=ACT.Copy)
+        v_woven = tiles(V_TILES, [P, SLOT_PASSES, P, PACK], BF16, "v_woven")
 
         def turn_values(got, first_col, step, index, woven):
             turned = bank(index, [P, PACK, P], BF16, "v_turned")
@@ -120,61 +146,36 @@ def tile_attend_sigm_cap_kb_srtq256n1024t2048_kernel(tc, qT, k_words, k_scales, 
             nc.scalar.copy(out=woven.rearrange("p (c i) t -> p c t i", i=4),
                            in_=turned[:].rearrange("p t (c i) -> p c t i", i=4))
 
-        v_low_woven = sbuf([P, SLOT_PASSES, P, PACK], BF16, "v_low_woven")
-        turn_values(v_got_low[0], 0, P, 6, v_low_woven[:, 0])
+        def low_values(g, cols):
+            got = sbuf([P, K_PASS], BF16, "v_got_low%d" % g)
+            nc.scalar.activation(out=v_low_bf[:, cols], in_=v_low[g][:], func=ACT.Copy)
+            nc.scalar.activation(out=dealt(got), in_=v_low_bf[:, 0:reach(g)].indirect(listed(g)), func=ACT.Copy)
+            return got
 
-        def turned_columns(pool_tile, got, banks, name):
-            nc.vector.tensor_copy(out=dealt(got), in_=pool_tile[:].bitcast(U32).indirect(offsets[:]))
-            turned = [bank(banks[g], [P, PACK, P], F32, name + "_turned") for g in range(SLOT_PASSES)]
-            for g in range(SLOT_PASSES):
-                for t in range(PACK):
-                    col = (t * SLOT_PASSES + g) * P
-                    nc.tensor.transpose(turned[g][:, t, :], got[:, col:col + P].bitcast(F32), ident32[:])
-            return turned
-
-        def halved(turned, half):
-            for g in range(SLOT_PASSES):
-                nc.scalar.activation(out=half[g][:], in_=turned[g][:, :, LAST], func=ACT.Copy, scale=0.5)
-            return half
+        got_low = [low_values(0, head)]
+        half_kb = sbuf([P, SLOT_PASSES * PACK], F32, "half_kb", "v_low0")
+        nc.scalar.activation(out=half_kb[:], in_=kb_cols, func=ACT.Copy, scale=0.5)
+        got_low.append(low_values(1, tail))
+        turn_values(got_low[0], 0, P, 6, v_woven[0][:, 0])
 
         k_codes = tiles(SLOT_PASSES, [P, D_PASSES * K_PASS], U16, "k_codes")
 
-        def gather_words(g):
+        def keys(g):
             got = sbuf([P, K_PASS], U32, "kw_got%d" % g)
             nc.vector.tensor_copy(out=got[:], in_=kw_pool[:, 0:reach(g)].bitcast(U32).indirect(listed(g)))
-            return got
-
-        def part_words(g, got):
             nc.vector.tensor_copy(
                 out=k_codes[g][:].rearrange("p (o t b c) -> p b t o c", o=D_PASSES, t=PACK, c=RUN),
                 in_=got[:].bitcast(U16).rearrange("p (b t c o) -> p b t o c", o=D_PASSES, t=PACK, c=RUN))
 
-        kb_turned = turned_columns(kb_pool, sbuf([P, N], U32, "kb_got"), (4, 5), "kb")
-        ks_got = sbuf([P, N], U8, "ks_got")
-        nc.vector.tensor_copy(out=ks_got[:], in_=ks_pool[:].indirect(offsets[:]))
-        half_kb = halved(kb_turned, [placed([P, PACK], F32, "half_kb%d" % g, 32768 + 64 * g)
-                                     for g in range(SLOT_PASSES)])
-        nc.vector.tensor_copy(
-            out=k_plane[0][:].bitcast(I32).rearrange("p (t b w) -> p b t w", t=PACK, w=2),
-            in_=ks_got[:].bitcast(I32).rearrange("p (b t w) -> p b t w", t=PACK, w=2))
-        for quad in range(4):
-            nc.sync.dma_start(out=k_plane[1][32 * quad:32 * quad + 4, :].bitcast(I32),
-                              in_=k_plane[0][32 * quad + 16:32 * quad + 20, :].bitcast(I32))
-        nc.sync.dma_start(out=vs_pool[LAST:P, :], in_=vs[LAST:P, :])
+        def token_scales(g, index, tag):
+            got = sbuf([P, K_PASS], U32, "vs_got%d" % g, tag)
+            nc.vector.tensor_copy(out=dealt(got), in_=vs_pool[:, 0:reach(g)].bitcast(U32).indirect(listed(g)))
+            return columns(got, 0, PACK, index, "vs_turned")
 
-        got = gather_words(0)
-        nc.vector.quantize_mx(out=q_codes[:].bitcast(FP8X4), scales=q_plane[:],
-                              in_=q_bf[:].rearrange("p o q t -> p (o q t)"))
-        part_words(0, got)
-        v_high = placed([P, T], F32, "v_high", 0)
-        nc.sync.dma_start(out=v_high[:], in_=vT[P:2 * P, :])
-
-        capped = [placed([P, PACK * NQ], F32, "capped%d" % g, 20480 + 4096 * g) for g in range(SLOT_PASSES)]
-        u = tiles(SLOT_PASSES, [P, NQ, PACK], F32, "u")
-
-        def weigh(g):
+        def capped_scores(g):
+            capped = sbuf([P, PACK * NQ], F32, "capped%d" % g)
             for t in range(PACK):
-                score = bank(t, [P, NQ], F32, "score")
+                score = bank(((0, 1, 2, 3), (1, 2, 3, 7))[g][t], [P, NQ], F32, "score")
                 for qh in range(Q_TILES):
                     for o in reversed(range(D_PASSES)):
                         kc = o * K_PASS + t * P
@@ -187,62 +188,69 @@ def tile_attend_sigm_cap_kb_srtq256n1024t2048_kernel(tc, qT, k_words, k_scales, 
                             rhs=q_codes[:, qc:qc + P].bitcast(FP8X4),
                             rhs_scale=q_plane[:, qc:qc + P],
                             start=(o == D_PASSES - 1), stop=(o == 0))
-                nc.scalar.activation(out=capped[g][:, t * NQ:(t + 1) * NQ], in_=score[:], func=ACT.Tanh,
-                                     bias=half_kb[g][:, t:t + 1], scale=0.5)
-            nc.scalar.activation(out=u[g][:].rearrange("p (c i) t -> p c t i", i=4),
-                                 in_=capped[g][:].rearrange("p (t c i) -> p c t i", t=PACK, i=4),
+                col = g * PACK + t
+                nc.scalar.activation(out=capped[:, t * NQ:(t + 1) * NQ], in_=score[:], func=ACT.Tanh,
+                                     bias=half_kb[:, col:col + 1], scale=0.5)
+            return capped
+
+        def sigmoid(g, capped):
+            p = sbuf([P, NQ, PACK], F32, "p%d" % g)
+            nc.scalar.activation(out=p[:].rearrange("p (c i) t -> p c t i", i=4),
+                                 in_=capped[:].rearrange("p (t c i) -> p c t i", t=PACK, i=4),
                                  func=ACT.Sigmoid, scale=2.0)
+            return p
 
-        weigh(0)
-        got = gather_words(1)
-        part_words(1, got)
-        weigh(1)
+        def spread(cols):
+            return cols.unsqueeze(1).to_broadcast([P, NQ, PACK])
 
-        vs_turned = turned_columns(vs_pool, sbuf([P, N], U32, "vs_got"), (4, 5), "vs")
+        keys(0)
+        vs_cols0 = token_scales(0, 5, None)
+        keys(1)
+        capped0 = capped_scores(0)
+        turn_values(got_low[1], 0, P, 0, v_woven[0][:, 1])
+        p0 = sigmoid(0, capped0)
+        vs_first = sbuf([P, PACK], F32, "vs_first")
+        nc.scalar.copy(out=vs_first[:], in_=vs_cols0)
+        p1 = sigmoid(1, capped_scores(1))
+        vs_cols1 = token_scales(1, 4, "kw_got1")
 
         v_got_high = sbuf([P, N], BF16, "v_got_high")
         nc.vector.tensor_copy(out=dealt(v_got_high), in_=v_high[:].indirect(offsets[:]))
-        turn_values(v_got_low[1], 0, P, 3, v_low_woven[:, 1])
-        v_high_woven = [placed([P, P, PACK], BF16, "v_high_woven%d" % g, 24576 + 1024 * g) for g in range(SLOT_PASSES)]
         for g in range(SLOT_PASSES):
-            turn_values(v_got_high, g * P, SLOT_PASSES * P, (2, 0)[g], v_high_woven[g][:])
+            turn_values(v_got_high, g * P, SLOT_PASSES * P, 6 - g, v_woven[1][:, g])
 
-        def quantised(source, width, name):
-            codes = sbuf([P, width], U32, name + "_codes")
+        def quantised(source, width, name, offset=None):
+            if offset is None:
+                codes = sbuf([P, width], U32, name + "_codes")
+            else:
+                codes = placed([P, width], U32, name + "_codes", offset)
             plane = sbuf([P, width], U8, name + "_plane")
             nc.vector.quantize_mx(out=codes[:].bitcast(FP8X4), scales=plane[:], in_=source)
             return codes, plane
 
-        w_bf = [placed([P, NQ, PACK], BF16, "w_bf%d" % g, 2048 * g) for g in range(SLOT_PASSES)]
-        for g in range(SLOT_PASSES):
-            nc.vector.tensor_tensor(out=w_bf[g][:], in0=u[g][:],
-                                    in1=vs_turned[g][:, :, LAST].unsqueeze(1).to_broadcast([P, NQ, PACK]),
-                                    op=ALU.mult)
-        w_mx = [quantised(w_bf[0][:].rearrange("p q t -> p (q t)"), NQ, "w0")]
-        v_low_mx = quantised(v_low_woven[:].rearrange("p g e t -> p (g e t)"), SLOT_PASSES * P, "v_low")
-        w_mx.append(quantised(w_bf[1][:].rearrange("p q t -> p (q t)"), NQ, "w1"))
+        w0 = sbuf([P, NQ, PACK], BF16, "w0")
+        nc.gpsimd.tensor_tensor(out=w0[:], in0=p0[:], in1=spread(vs_first[:]), op=ALU.mult)
+        v_mx = [quantised(v_woven[0][:].rearrange("p g e t -> p (g e t)"), SLOT_PASSES * P, "v_low", 0)]
+        w0_mx = quantised(w0[:].rearrange("p q t -> p (q t)"), NQ, "w0", 1024)
+        w1 = placed([P, NQ, PACK], BF16, "w1", 2048)
+        nc.vector.tensor_tensor(out=w1[:], in0=p1[:], in1=spread(vs_cols1), op=ALU.mult)
+        v_mx.append(quantised(v_woven[1][:].rearrange("p g e t -> p (g e t)"), SLOT_PASSES * P, "v_high"))
 
-        def product(target, qh, g, codes, plane):
+        for qh in range(Q_TILES):
             cols = slice(qh * P, (qh + 1) * P)
-            nc.tensor.matmul_mx(out=target, lhsT=w_mx[g][0][:, cols].bitcast(FP8X4), lhsT_scale=w_mx[g][1][:, cols],
-                                rhs=codes.bitcast(FP8X4), rhs_scale=plane,
-                                start=(g == 0), stop=(g == SLOT_PASSES - 1))
-
-        rows = out[0].rearrange("(qh p) e -> p qh e", p=P)
-        for h in range(V_TILES):
-            y_bank = [bank(4 + 2 * h + qh, [P, P], F32, "y_bank") for qh in range(Q_TILES)]
+            w1_mx = quantised(w1[:, cols, :].rearrange("p q t -> p (q t)"), P, "w1_%d" % qh)
+            y_bank = bank(1 + qh, [P, DV], F32, "y_bank")
             for g in range(SLOT_PASSES):
-                if h == 0:
-                    codes, plane = (part[:, g * P:(g + 1) * P] for part in v_low_mx)
-                else:
-                    codes, plane = (part[:] for part in quantised(
-                        v_high_woven[g][:].rearrange("p e t -> p (e t)"), P, "v_high%d" % g))
-                for qh in range(Q_TILES):
-                    product(y_bank[qh][:], qh, g, codes, plane)
-            y = sbuf([P, Q_TILES, P], F32, "y%d" % h)
-            if h == 0:
-                nc.vector.tensor_scalar_mul(y[:, 0, :], y_bank[0][:], 1.0 / 16.0)
+                w_codes, w_plane = (part[:, cols] for part in w0_mx) if g == 0 else (part[:] for part in w1_mx)
+                for h in range(V_TILES):
+                    v_codes, v_plane = (part[:, g * P:(g + 1) * P] for part in v_mx[h])
+                    nc.tensor.matmul_mx(out=y_bank[:, h * P:(h + 1) * P], lhsT=w_codes.bitcast(FP8X4),
+                                        lhsT_scale=w_plane, rhs=v_codes.bitcast(FP8X4), rhs_scale=v_plane,
+                                        start=(g == 0 and h == 0),
+                                        stop=(g == SLOT_PASSES - 1 and h == V_TILES - 1))
+            y = sbuf([P, DV], F32, "y%d" % qh)
+            if qh == 0:
+                nc.scalar.activation(out=y[:], in_=y_bank[:], func=ACT.Copy, scale=1.0 / 16.0)
             else:
-                nc.scalar.activation(out=y[:, 0, :], in_=y_bank[0][:], func=ACT.Copy, scale=1.0 / 16.0)
-            nc.vector.tensor_scalar_mul(y[:, 1, :], y_bank[1][:], 1.0 / 16.0)
-            nc.sync.dma_start(out=rows[:, :, h * P:(h + 1) * P], in_=y[:])
+                nc.vector.tensor_scalar_mul(y[:], y_bank[:], 1.0 / 16.0)
+            nc.sync.dma_start(out=out[0, cols, :], in_=y[:])

@@ -34,7 +34,6 @@ def tile_attend_sigm_cap_kb_srtq256n1024t2048_kernel(tc, qT, k_words, k_scales, 
     nc = tc.nc
     with ExitStack() as ctx:
         sb = ctx.enter_context(tc.tile_pool(name="sb", bufs=1))
-        late = ctx.enter_context(tc.tile_pool(name="late", bufs=1))
         ps = ctx.enter_context(tc.psum_pool(name="ps", bufs=1))
 
         def sbuf(shape, dtype, name, tag=None):
@@ -42,9 +41,6 @@ def tile_attend_sigm_cap_kb_srtq256n1024t2048_kernel(tc, qT, k_words, k_scales, 
 
         def tiles(count, shape, dtype, name):
             return [sbuf(shape, dtype, "%s%d" % (name, i)) for i in range(count)]
-
-        def placed(shape, dtype, name, offset):
-            return late.tile(shape, dtype, name=name, align_bytes=64, offset=offset)
 
         def bank(index, shape, dtype, name):
             return ps.tile(shape, dtype, name=name, tag="bank%d" % index)
@@ -72,7 +68,7 @@ def tile_attend_sigm_cap_kb_srtq256n1024t2048_kernel(tc, qT, k_words, k_scales, 
         nc.gpsimd.memset(kb_pool[0:LAST, T // 2:T].bitcast(I32), 0)
         nc.vector.memset(k_plane[1][:].bitcast(I32), 0)
 
-        warm_in = sbuf([P, 1], F32, "warm_in", "vs_pool")
+        warm_in = sbuf([P, 1], F32, "warm_in")
         warm_out = sbuf([P, 1], F32, "warm_out")
         nc.gpsimd.memset(warm_in[:], 0.0)
         nc.scalar.activation(out=warm_out[:], in_=warm_in[:], func=ACT.Sigmoid)
@@ -91,16 +87,25 @@ def tile_attend_sigm_cap_kb_srtq256n1024t2048_kernel(tc, qT, k_words, k_scales, 
             rows = qT[0, o * K_PASS:(o + 1) * K_PASS, :]
             nc.sync.dma_start(out=q_raw[o][:], in_=rows.rearrange("(p t) q -> p t q", t=PACK))
 
-        load_queries(0)
-        for r in range(4):
+        def load_scales(r):
             nc.sync.dma_start(out=ks_pool[r:P:16, :].bitcast(I32),
                               in_=k_scales[:, r:16:4, :].rearrange("o q t -> q o t").bitcast(I32))
+
+        load_queries(0)
+        nc.sync.dma_start(out=vs_pool[LAST:P, head], in_=vs[LAST:P, head])
+        for r in range(3):
+            load_scales(r)
         load_queries(1)
+        load_scales(3)
         v_low = [sbuf([P, reach(0)], F32, "v_low0"), sbuf([P, T - reach(0)], F32, "v_low1")]
         words = k_words[0].rearrange("p t b -> p (t b)").bitcast(I32)
         nc.sync.dma_start(out=v_low[0][:], in_=vT[0:P, head])
         nc.sync.dma_start(out=kw_pool[:, head], in_=words[:, head])
         nc.sync.dma_start(out=v_low[1][:], in_=vT[0:P, tail])
+        nc.sync.dma_start(out=kw_pool[:, tail], in_=words[:, tail])
+        nc.sync.dma_start(out=vs_pool[LAST:P, tail], in_=vs[LAST:P, tail])
+        v_high = sbuf([P, T], F32, "v_high")
+        nc.sync.dma_start(out=v_high[:, head], in_=vT[P:2 * P, head])
 
         q_bf = sbuf([P, D_PASSES, NQ, PACK], BF16, "q_bf")
         q_codes = sbuf([P, D_PASSES * NQ], U32, "q_codes")
@@ -116,27 +121,29 @@ def tile_attend_sigm_cap_kb_srtq256n1024t2048_kernel(tc, qT, k_words, k_scales, 
                 nc.tensor.transpose(turned[:, j:j + P], got[:, col:col + P].bitcast(F32), ident32[:])
             return turned[:, LAST:LAST + count]
 
+        def token_scales(g):
+            got = sbuf([P, K_PASS], U32, "vs_got%d" % g)
+            nc.vector.tensor_copy(out=dealt(got), in_=vs_pool[:, 0:reach(g)].bitcast(U32).indirect(listed(g)))
+            return got
+
         kb_got = sbuf([P, N], U32, "kb_got")
         nc.vector.tensor_copy(out=kb_got[:].rearrange("p (g t b c) -> p g b t c", g=SLOT_PASSES, t=PACK, c=RUN),
                               in_=kb_pool[:].bitcast(U32).indirect(offsets[:]))
         kb_cols = columns(kb_got, 0, SLOT_PASSES * PACK, 4, "kb_turned")
+        vs_cols0 = columns(token_scales(0), 0, PACK, 5, "vs_turned")
         ks_got = sbuf([P, N], U8, "ks_got")
         nc.vector.tensor_copy(out=ks_got[:], in_=ks_pool[:].indirect(offsets[:]))
+        nc.vector.quantize_mx(out=q_codes[:].bitcast(FP8X4), scales=q_plane[:],
+                              in_=q_bf[:].rearrange("p o q t -> p (o q t)"))
         nc.vector.tensor_copy(
             out=k_plane[0][:].bitcast(I32).rearrange("p (t b w) -> p b t w", t=PACK, w=2),
             in_=ks_got[:].bitcast(I32).rearrange("p (b t w) -> p b t w", t=PACK, w=2))
         for quad in range(4):
             nc.sync.dma_start(out=k_plane[1][32 * quad:32 * quad + 4, :].bitcast(I32),
                               in_=k_plane[0][32 * quad + 16:32 * quad + 20, :].bitcast(I32))
-        nc.sync.dma_start(out=vs_pool[LAST:P, :], in_=vs[LAST:P, :])
-        nc.sync.dma_start(out=kw_pool[:, tail], in_=words[:, tail])
-        v_high = placed([P, T], F32, "v_high", 0)
-        nc.sync.dma_start(out=v_high[:], in_=vT[P:2 * P, :])
-        nc.vector.quantize_mx(out=q_codes[:].bitcast(FP8X4), scales=q_plane[:],
-                              in_=q_bf[:].rearrange("p o q t -> p (o q t)"))
+        nc.sync.dma_start(out=v_high[:, tail], in_=vT[P:2 * P, tail])
 
         v_low_bf = sbuf([P, T], BF16, "v_low_bf")
-        v_woven = tiles(V_TILES, [P, SLOT_PASSES, P, PACK], BF16, "v_woven")
 
         def turn_values(got, first_col, step, index, woven):
             turned = bank(index, [P, PACK, P], BF16, "v_turned")
@@ -156,26 +163,30 @@ def tile_attend_sigm_cap_kb_srtq256n1024t2048_kernel(tc, qT, k_words, k_scales, 
         half_kb = sbuf([P, SLOT_PASSES * PACK], F32, "half_kb", "v_low0")
         nc.scalar.activation(out=half_kb[:], in_=kb_cols, func=ACT.Copy, scale=0.5)
         got_low.append(low_values(1, tail))
-        turn_values(got_low[0], 0, P, 6, v_woven[0][:, 0])
+        low_woven = sbuf([P, SLOT_PASSES, P, PACK], BF16, "low_woven", "v_low1")
+        turn_values(got_low[0], 0, P, 6, low_woven[:, 0])
 
-        k_codes = tiles(SLOT_PASSES, [P, D_PASSES * K_PASS], U16, "k_codes")
-
-        def keys(g):
+        def gather_words(g):
             got = sbuf([P, K_PASS], U32, "kw_got%d" % g)
             nc.vector.tensor_copy(out=got[:], in_=kw_pool[:, 0:reach(g)].bitcast(U32).indirect(listed(g)))
-            nc.vector.tensor_copy(
-                out=k_codes[g][:].rearrange("p (o t b c) -> p b t o c", o=D_PASSES, t=PACK, c=RUN),
-                in_=got[:].bitcast(U16).rearrange("p (b t c o) -> p b t o c", o=D_PASSES, t=PACK, c=RUN))
+            return got
 
-        def token_scales(g, index, tag):
-            got = sbuf([P, K_PASS], U32, "vs_got%d" % g, tag)
-            nc.vector.tensor_copy(out=dealt(got), in_=vs_pool[:, 0:reach(g)].bitcast(U32).indirect(listed(g)))
-            return columns(got, 0, PACK, index, "vs_turned")
+        def part_words(got, name, tag):
+            codes = sbuf([P, D_PASSES * K_PASS], U16, name, tag)
+            nc.vector.tensor_copy(
+                out=codes[:].rearrange("p (o t b c) -> p b t o c", o=D_PASSES, t=PACK, c=RUN),
+                in_=got[:].bitcast(U16).rearrange("p (b t c o) -> p b t o c", o=D_PASSES, t=PACK, c=RUN))
+            return codes
+
+        k_codes = [part_words(gather_words(0), "k_codes0", None)]
+        got = gather_words(1)
+        vs_got1 = token_scales(1)
+        k_codes.append(part_words(got, "k_codes1", "v_low_bf"))
 
         def capped_scores(g):
             capped = sbuf([P, PACK * NQ], F32, "capped%d" % g)
             for t in range(PACK):
-                score = bank(((0, 1, 2, 3), (1, 2, 3, 7))[g][t], [P, NQ], F32, "score")
+                score = bank(((0, 1, 2, 3), (2, 3, 4, 7))[g][t], [P, NQ], F32, "score")
                 for qh in range(Q_TILES):
                     for o in reversed(range(D_PASSES)):
                         kc = o * K_PASS + t * P
@@ -193,57 +204,56 @@ def tile_attend_sigm_cap_kb_srtq256n1024t2048_kernel(tc, qT, k_words, k_scales, 
                                      bias=half_kb[:, col:col + 1], scale=0.5)
             return capped
 
-        def sigmoid(g, capped):
-            p = sbuf([P, NQ, PACK], F32, "p%d" % g)
+        def sigmoid(capped, first, width, name):
+            p = sbuf([P, width, PACK], F32, name)
+            rows = capped[:].rearrange("p (t q) -> p t q", t=PACK)[:, :, first:first + width]
             nc.scalar.activation(out=p[:].rearrange("p (c i) t -> p c t i", i=4),
-                                 in_=capped[:].rearrange("p (t c i) -> p c t i", t=PACK, i=4),
-                                 func=ACT.Sigmoid, scale=2.0)
+                                 in_=rows.rearrange("p t (c i) -> p c t i", i=4), func=ACT.Sigmoid, scale=2.0)
             return p
 
-        def spread(cols):
-            return cols.unsqueeze(1).to_broadcast([P, NQ, PACK])
+        def weights(p, cols, width, name):
+            w = sbuf([P, width, PACK], BF16, name)
+            nc.vector.tensor_tensor(out=w[:], in0=p[:], in1=cols.unsqueeze(1).to_broadcast([P, width, PACK]),
+                                    op=ALU.mult)
+            return w[:].rearrange("p q t -> p (q t)")
 
-        keys(0)
-        vs_cols0 = token_scales(0, 5, None)
-        keys(1)
-        capped0 = capped_scores(0)
-        turn_values(got_low[1], 0, P, 0, v_woven[0][:, 1])
-        p0 = sigmoid(0, capped0)
-        vs_first = sbuf([P, PACK], F32, "vs_first")
-        nc.scalar.copy(out=vs_first[:], in_=vs_cols0)
-        p1 = sigmoid(1, capped_scores(1))
-        vs_cols1 = token_scales(1, 4, "kw_got1")
-
-        v_got_high = sbuf([P, N], BF16, "v_got_high")
-        nc.vector.tensor_copy(out=dealt(v_got_high), in_=v_high[:].indirect(offsets[:]))
-        for g in range(SLOT_PASSES):
-            turn_values(v_got_high, g * P, SLOT_PASSES * P, 6 - g, v_woven[1][:, g])
-
-        def quantised(source, width, name, offset=None):
-            if offset is None:
-                codes = sbuf([P, width], U32, name + "_codes")
-            else:
-                codes = placed([P, width], U32, name + "_codes", offset)
+        def quantised(source, width, name, tag=None):
+            codes = sbuf([P, width], U32, name + "_codes", tag)
             plane = sbuf([P, width], U8, name + "_plane")
             nc.vector.quantize_mx(out=codes[:].bitcast(FP8X4), scales=plane[:], in_=source)
             return codes, plane
 
-        w0 = sbuf([P, NQ, PACK], BF16, "w0")
-        nc.gpsimd.tensor_tensor(out=w0[:], in0=p0[:], in1=spread(vs_first[:]), op=ALU.mult)
-        v_mx = [quantised(v_woven[0][:].rearrange("p g e t -> p (g e t)"), SLOT_PASSES * P, "v_low", 0)]
-        w0_mx = quantised(w0[:].rearrange("p q t -> p (q t)"), NQ, "w0", 1024)
-        w1 = placed([P, NQ, PACK], BF16, "w1", 2048)
-        nc.vector.tensor_tensor(out=w1[:], in0=p1[:], in1=spread(vs_cols1), op=ALU.mult)
-        v_mx.append(quantised(v_woven[1][:].rearrange("p g e t -> p (g e t)"), SLOT_PASSES * P, "v_high"))
+        capped0 = capped_scores(0)
+        turn_values(got_low[1], 0, P, 0, low_woven[:, 1])
+        vs_cols1 = columns(vs_got1, 0, PACK, 1, "vs_turned")
+        p0 = sigmoid(capped0, 0, NQ, "p0")
+        capped1 = capped_scores(1)
+        p1 = [sigmoid(capped1, qh * P, P, "p1_%d" % qh) for qh in range(Q_TILES)]
+
+        v_got_high = sbuf([P, N], BF16, "v_got_high")
+        nc.vector.tensor_copy(out=dealt(v_got_high), in_=v_high[:].indirect(offsets[:]))
+        high_woven = sbuf([P, SLOT_PASSES, P, PACK], BF16, "high_woven", "capped1")
+        for g in range(SLOT_PASSES):
+            turn_values(v_got_high, g * P, SLOT_PASSES * P, (0, 7)[g], high_woven[:, g])
+
+        w0 = weights(p0, vs_cols0, NQ, "w0")
+        low_mx = quantised(low_woven[:].rearrange("p g e t -> p (g e t)"), SLOT_PASSES * P, "v_low", "capped0")
+        w0_mx = quantised(w0, NQ, "w0")
+        w1 = [weights(p1[qh], vs_cols1, P, "w1_%d" % qh) for qh in range(Q_TILES)]
+        w1_mx = [quantised(w1[qh], P, "w1_%d" % qh) for qh in range(Q_TILES)]
+        high_mx = [quantised(high_woven[:, g].rearrange("p e t -> p (e t)"), P, "v_high%d" % g)
+                   for g in range(SLOT_PASSES)]
 
         for qh in range(Q_TILES):
             cols = slice(qh * P, (qh + 1) * P)
-            w1_mx = quantised(w1[:, cols, :].rearrange("p q t -> p (q t)"), P, "w1_%d" % qh)
-            y_bank = bank(1 + qh, [P, DV], F32, "y_bank")
-            for g in range(SLOT_PASSES):
-                w_codes, w_plane = (part[:, cols] for part in w0_mx) if g == 0 else (part[:] for part in w1_mx)
-                for h in range(V_TILES):
-                    v_codes, v_plane = (part[:, g * P:(g + 1) * P] for part in v_mx[h])
+            y_bank = bank(2 + qh, [P, DV], F32, "y_bank")
+            for h in range(V_TILES):
+                for g in range(SLOT_PASSES):
+                    w_codes, w_plane = (part[:, cols] for part in w0_mx) if g == 0 else (part[:] for part in w1_mx[qh])
+                    if h == 0:
+                        v_codes, v_plane = (part[:, g * P:(g + 1) * P] for part in low_mx)
+                    else:
+                        v_codes, v_plane = (part[:] for part in high_mx[g])
                     nc.tensor.matmul_mx(out=y_bank[:, h * P:(h + 1) * P], lhsT=w_codes.bitcast(FP8X4),
                                         lhsT_scale=w_plane, rhs=v_codes.bitcast(FP8X4), rhs_scale=v_plane,
                                         start=(g == 0 and h == 0),

@@ -65,10 +65,9 @@ def tile_attend_sigm_cap_kb_srtq256n1024t2048_kernel(tc, qT, k_words, k_scales, 
 
         nc.vector.memset(ks_pool[:].bitcast(I32), 0)
         nc.vector.memset(kb_pool[0:LAST, 0:T // 2].bitcast(I32), 0)
-        nc.gpsimd.memset(kb_pool[0:LAST, T // 2:T].bitcast(I32), 0)
         nc.vector.memset(k_plane[1][:].bitcast(I32), 0)
 
-        warm_in = sbuf([P, 1], F32, "warm_in")
+        warm_in = sbuf([P, 1], F32, "warm_in", "vs_pool")
         warm_out = sbuf([P, 1], F32, "warm_out")
         nc.gpsimd.memset(warm_in[:], 0.0)
         nc.scalar.activation(out=warm_out[:], in_=warm_in[:], func=ACT.Sigmoid)
@@ -76,7 +75,8 @@ def tile_attend_sigm_cap_kb_srtq256n1024t2048_kernel(tc, qT, k_words, k_scales, 
         ident32 = sbuf([P, P], F32, "ident32")
         ident16 = sbuf([P, P], BF16, "ident16")
         make_identity(nc, ident32[:])
-        nc.scalar.copy(out=ident16[:], in_=ident32[:])
+        make_identity(nc, ident16[:])
+        nc.gpsimd.memset(kb_pool[0:LAST, T // 2:T].bitcast(I32), 0)
         vs_pool = sbuf([P, T], F32, "vs_pool")
         nc.gpsimd.memset(vs_pool[0:LAST, :].bitcast(I32), 0)
 
@@ -92,11 +92,11 @@ def tile_attend_sigm_cap_kb_srtq256n1024t2048_kernel(tc, qT, k_words, k_scales, 
                               in_=k_scales[:, r:16:4, :].rearrange("o q t -> q o t").bitcast(I32))
 
         load_queries(0)
-        nc.sync.dma_start(out=vs_pool[LAST:P, head], in_=vs[LAST:P, head])
         for r in range(3):
             load_scales(r)
         load_queries(1)
         load_scales(3)
+        nc.sync.dma_start(out=vs_pool[LAST:P, head], in_=vs[LAST:P, head])
         v_low = [sbuf([P, reach(0)], F32, "v_low0"), sbuf([P, T - reach(0)], F32, "v_low1")]
         words = k_words[0].rearrange("p t b -> p (t b)").bitcast(I32)
         nc.sync.dma_start(out=v_low[0][:], in_=vT[0:P, head])
@@ -104,8 +104,6 @@ def tile_attend_sigm_cap_kb_srtq256n1024t2048_kernel(tc, qT, k_words, k_scales, 
         nc.sync.dma_start(out=v_low[1][:], in_=vT[0:P, tail])
         nc.sync.dma_start(out=kw_pool[:, tail], in_=words[:, tail])
         nc.sync.dma_start(out=vs_pool[LAST:P, tail], in_=vs[LAST:P, tail])
-        v_high = sbuf([P, T], F32, "v_high")
-        nc.sync.dma_start(out=v_high[:, head], in_=vT[P:2 * P, head])
 
         q_bf = sbuf([P, D_PASSES, NQ, PACK], BF16, "q_bf")
         q_codes = sbuf([P, D_PASSES * NQ], U32, "q_codes")
@@ -130,7 +128,6 @@ def tile_attend_sigm_cap_kb_srtq256n1024t2048_kernel(tc, qT, k_words, k_scales, 
         nc.vector.tensor_copy(out=kb_got[:].rearrange("p (g t b c) -> p g b t c", g=SLOT_PASSES, t=PACK, c=RUN),
                               in_=kb_pool[:].bitcast(U32).indirect(offsets[:]))
         kb_cols = columns(kb_got, 0, SLOT_PASSES * PACK, 4, "kb_turned")
-        vs_cols0 = columns(token_scales(0), 0, PACK, 5, "vs_turned")
         ks_got = sbuf([P, N], U8, "ks_got")
         nc.vector.tensor_copy(out=ks_got[:], in_=ks_pool[:].indirect(offsets[:]))
         nc.vector.quantize_mx(out=q_codes[:].bitcast(FP8X4), scales=q_plane[:],
@@ -141,7 +138,10 @@ def tile_attend_sigm_cap_kb_srtq256n1024t2048_kernel(tc, qT, k_words, k_scales, 
         for quad in range(4):
             nc.sync.dma_start(out=k_plane[1][32 * quad:32 * quad + 4, :].bitcast(I32),
                               in_=k_plane[0][32 * quad + 16:32 * quad + 20, :].bitcast(I32))
-        nc.sync.dma_start(out=v_high[:, tail], in_=vT[P:2 * P, tail])
+        v_high = sbuf([P, T], F32, "v_high")
+        nc.sync.dma_start(out=v_high[:], in_=vT[P:2 * P, :])
+
+        vs_cols0 = columns(token_scales(0), 0, PACK, 5, "vs_turned")
 
         v_low_bf = sbuf([P, T], BF16, "v_low_bf")
 

@@ -34,6 +34,7 @@ def tile_attend_sigm_cap_kb_srtq256n1024t2048_kernel(tc, qT, k_words, k_scales, 
     nc = tc.nc
     with ExitStack() as ctx:
         sb = ctx.enter_context(tc.tile_pool(name="sb", bufs=1))
+        late = ctx.enter_context(tc.tile_pool(name="late", bufs=1))
         ps = ctx.enter_context(tc.psum_pool(name="ps", bufs=1))
 
         def sbuf(shape, dtype, name, tag=None):
@@ -41,6 +42,9 @@ def tile_attend_sigm_cap_kb_srtq256n1024t2048_kernel(tc, qT, k_words, k_scales, 
 
         def tiles(count, shape, dtype, name):
             return [sbuf(shape, dtype, "%s%d" % (name, i)) for i in range(count)]
+
+        def placed(shape, dtype, name, offset):
+            return late.tile(shape, dtype, name=name, align_bytes=64, offset=offset)
 
         def bank(index, shape, dtype, name):
             return ps.tile(shape, dtype, name=name, tag="bank%d" % index)
@@ -73,9 +77,7 @@ def tile_attend_sigm_cap_kb_srtq256n1024t2048_kernel(tc, qT, k_words, k_scales, 
         nc.scalar.activation(out=warm_out[:], in_=warm_in[:], func=ACT.Sigmoid)
 
         ident32 = sbuf([P, P], F32, "ident32")
-        ident16 = sbuf([P, P], BF16, "ident16")
         make_identity(nc, ident32[:])
-        make_identity(nc, ident16[:])
         nc.gpsimd.memset(kb_pool[0:LAST, T // 2:T].bitcast(I32), 0)
         vs_pool = sbuf([P, T], F32, "vs_pool")
         nc.gpsimd.memset(vs_pool[0:LAST, :].bitcast(I32), 0)
@@ -96,14 +98,13 @@ def tile_attend_sigm_cap_kb_srtq256n1024t2048_kernel(tc, qT, k_words, k_scales, 
             load_scales(r)
         load_queries(1)
         load_scales(3)
-        nc.sync.dma_start(out=vs_pool[LAST:P, head], in_=vs[LAST:P, head])
-        v_low = [sbuf([P, reach(0)], F32, "v_low0"), sbuf([P, T - reach(0)], F32, "v_low1")]
+        v_low = [sbuf([P, reach(0)], F32, "v_low0"), placed([P, T - reach(0)], F32, "v_low1", 8192)]
         words = k_words[0].rearrange("p t b -> p (t b)").bitcast(I32)
         nc.sync.dma_start(out=v_low[0][:], in_=vT[0:P, head])
         nc.sync.dma_start(out=kw_pool[:, head], in_=words[:, head])
-        nc.sync.dma_start(out=v_low[1][:], in_=vT[0:P, tail])
         nc.sync.dma_start(out=kw_pool[:, tail], in_=words[:, tail])
-        nc.sync.dma_start(out=vs_pool[LAST:P, tail], in_=vs[LAST:P, tail])
+        nc.sync.dma_start(out=v_low[1][:], in_=vT[0:P, tail])
+        nc.sync.dma_start(out=vs_pool[LAST:P, :], in_=vs[LAST:P, :])
 
         q_bf = sbuf([P, D_PASSES, NQ, PACK], BF16, "q_bf")
         q_codes = sbuf([P, D_PASSES * NQ], U32, "q_codes")
@@ -119,15 +120,13 @@ def tile_attend_sigm_cap_kb_srtq256n1024t2048_kernel(tc, qT, k_words, k_scales, 
                 nc.tensor.transpose(turned[:, j:j + P], got[:, col:col + P].bitcast(F32), ident32[:])
             return turned[:, LAST:LAST + count]
 
-        def token_scales(g):
-            got = sbuf([P, K_PASS], U32, "vs_got%d" % g)
-            nc.vector.tensor_copy(out=dealt(got), in_=vs_pool[:, 0:reach(g)].bitcast(U32).indirect(listed(g)))
+        def token_row(pool_tile, name):
+            got = sbuf([P, N], U32, name)
+            nc.vector.tensor_copy(out=got[:].rearrange("p (g t b c) -> p g b t c", g=SLOT_PASSES, t=PACK, c=RUN),
+                                  in_=pool_tile[:].bitcast(U32).indirect(offsets[:]))
             return got
 
-        kb_got = sbuf([P, N], U32, "kb_got")
-        nc.vector.tensor_copy(out=kb_got[:].rearrange("p (g t b c) -> p g b t c", g=SLOT_PASSES, t=PACK, c=RUN),
-                              in_=kb_pool[:].bitcast(U32).indirect(offsets[:]))
-        kb_cols = columns(kb_got, 0, SLOT_PASSES * PACK, 4, "kb_turned")
+        kb_cols = columns(token_row(kb_pool, "kb_got"), 0, SLOT_PASSES * PACK, 4, "kb_turned")
         ks_got = sbuf([P, N], U8, "ks_got")
         nc.vector.tensor_copy(out=ks_got[:], in_=ks_pool[:].indirect(offsets[:]))
         nc.vector.quantize_mx(out=q_codes[:].bitcast(FP8X4), scales=q_plane[:],
@@ -141,52 +140,66 @@ def tile_attend_sigm_cap_kb_srtq256n1024t2048_kernel(tc, qT, k_words, k_scales, 
         v_high = sbuf([P, T], F32, "v_high")
         nc.sync.dma_start(out=v_high[:], in_=vT[P:2 * P, :])
 
-        vs_cols0 = columns(token_scales(0), 0, PACK, 5, "vs_turned")
-
         v_low_bf = sbuf([P, T], BF16, "v_low_bf")
 
-        def turn_values(got, first_col, step, index, woven):
-            turned = bank(index, [P, PACK, P], BF16, "v_turned")
-            for t in range(PACK):
-                col = first_col + t * step
-                nc.tensor.transpose(turned[:, t, :], got[:, col:col + P], ident16[:])
-            nc.scalar.copy(out=woven.rearrange("p (c i) t -> p c t i", i=4),
-                           in_=turned[:].rearrange("p t (c i) -> p c t i", i=4))
+        def turn_words(got, first_word, index, woven):
+            turned = bank(index, [P, 2, P], F32, "v_turned")
+            for u in range(2):
+                pairs = got[:].bitcast(F32)[:, first_word + u:first_word + 2 * P:2]
+                nc.tensor.transpose(turned[:, u, :], pairs, ident32[:])
+            nc.scalar.copy(out=woven.rearrange("p e t -> p (e t)").bitcast(F32).rearrange("p (c i u) -> p c u i", i=2, u=2),
+                           in_=turned[:].rearrange("p u (c i) -> p c u i", i=2))
+
+        def woven_slots(tile):
+            return tile[:].rearrange("p (b c t) -> p b t c", t=PACK, c=RUN)
 
         def low_values(g, cols):
             got = sbuf([P, K_PASS], BF16, "v_got_low%d" % g)
             nc.scalar.activation(out=v_low_bf[:, cols], in_=v_low[g][:], func=ACT.Copy)
-            nc.scalar.activation(out=dealt(got), in_=v_low_bf[:, 0:reach(g)].indirect(listed(g)), func=ACT.Copy)
+            nc.scalar.activation(out=woven_slots(got), in_=v_low_bf[:, 0:reach(g)].indirect(listed(g)), func=ACT.Copy)
             return got
+
+        def quantised(source, width, name, offset=None):
+            if offset is None:
+                codes = sbuf([P, width], U32, name + "_codes")
+            else:
+                codes = placed([P, width], U32, name + "_codes", offset)
+            plane = sbuf([P, width], U8, name + "_plane")
+            nc.vector.quantize_mx(out=codes[:].bitcast(FP8X4), scales=plane[:], in_=source)
+            return codes, plane
 
         got_low = [low_values(0, head)]
         half_kb = sbuf([P, SLOT_PASSES * PACK], F32, "half_kb", "v_low0")
         nc.scalar.activation(out=half_kb[:], in_=kb_cols, func=ACT.Copy, scale=0.5)
+        warm_bank = bank(4, [P, K_PASS], F32, "warm_bank")
+        for half in range(2):
+            nc.tensor.matmul_mx(out=warm_bank[:], lhsT=q_codes[:, 0:P].bitcast(FP8X4), lhsT_scale=q_plane[:, 0:P],
+                                rhs=q_codes[:].bitcast(FP8X4), rhs_scale=q_plane[:],
+                                start=(half == 0), stop=(half == 1))
         got_low.append(low_values(1, tail))
-        low_woven = sbuf([P, SLOT_PASSES, P, PACK], BF16, "low_woven", "v_low1")
-        turn_values(got_low[0], 0, P, 6, low_woven[:, 0])
+        low_woven = [placed([P, P, PACK], BF16, "low_woven0", 8704)]
+        turn_words(got_low[0], 0, 6, low_woven[0][:])
 
         def gather_words(g):
             got = sbuf([P, K_PASS], U32, "kw_got%d" % g)
             nc.vector.tensor_copy(out=got[:], in_=kw_pool[:, 0:reach(g)].bitcast(U32).indirect(listed(g)))
             return got
 
-        def part_words(got, name, tag):
-            codes = sbuf([P, D_PASSES * K_PASS], U16, name, tag)
+        def part_words(got, codes):
             nc.vector.tensor_copy(
                 out=codes[:].rearrange("p (o t b c) -> p b t o c", o=D_PASSES, t=PACK, c=RUN),
                 in_=got[:].bitcast(U16).rearrange("p (b t c o) -> p b t o c", o=D_PASSES, t=PACK, c=RUN))
             return codes
 
-        k_codes = [part_words(gather_words(0), "k_codes0", None)]
-        got = gather_words(1)
-        vs_got1 = token_scales(1)
-        k_codes.append(part_words(got, "k_codes1", "v_low_bf"))
+        kw_got = [gather_words(g) for g in range(SLOT_PASSES)]
+        k_codes = [part_words(kw_got[g], placed([P, D_PASSES * K_PASS], U16, "k_codes%d" % g, (6656, 9728)[g]))
+                   for g in range(SLOT_PASSES)]
+        vs_got = token_row(vs_pool, "vs_got")
 
         def capped_scores(g):
-            capped = sbuf([P, PACK * NQ], F32, "capped%d" % g)
+            capped = placed([P, PACK * NQ], F32, "capped%d" % g, 12288 * g)
             for t in range(PACK):
-                score = bank(((0, 1, 2, 3), (2, 3, 4, 7))[g][t], [P, NQ], F32, "score")
+                score = bank(((0, 1, 2, 3), (4, 7, 2, 3))[g][t], [P, NQ], F32, "score")
                 for qh in range(Q_TILES):
                     for o in reversed(range(D_PASSES)):
                         kc = o * K_PASS + t * P
@@ -217,43 +230,36 @@ def tile_attend_sigm_cap_kb_srtq256n1024t2048_kernel(tc, qT, k_words, k_scales, 
                                     op=ALU.mult)
             return w[:].rearrange("p q t -> p (q t)")
 
-        def quantised(source, width, name, tag=None):
-            codes = sbuf([P, width], U32, name + "_codes", tag)
-            plane = sbuf([P, width], U8, name + "_plane")
-            nc.vector.quantize_mx(out=codes[:].bitcast(FP8X4), scales=plane[:], in_=source)
-            return codes, plane
-
         capped0 = capped_scores(0)
-        turn_values(got_low[1], 0, P, 0, low_woven[:, 1])
-        vs_cols1 = columns(vs_got1, 0, PACK, 1, "vs_turned")
         p0 = sigmoid(capped0, 0, NQ, "p0")
         capped1 = capped_scores(1)
+        low_woven.append(sbuf([P, P, PACK], BF16, "low_woven1"))
+        turn_words(got_low[1], 0, 0, low_woven[1][:])
+        vs_cols = columns(vs_got, 0, SLOT_PASSES * PACK, 1, "vs_turned")
         p1 = [sigmoid(capped1, qh * P, P, "p1_%d" % qh) for qh in range(Q_TILES)]
 
         v_got_high = sbuf([P, N], BF16, "v_got_high")
-        nc.vector.tensor_copy(out=dealt(v_got_high), in_=v_high[:].indirect(offsets[:]))
-        high_woven = sbuf([P, SLOT_PASSES, P, PACK], BF16, "high_woven", "capped1")
+        nc.vector.tensor_copy(out=woven_slots(v_got_high), in_=v_high[:].indirect(offsets[:]))
+        high_woven = placed([P, SLOT_PASSES, P, PACK], BF16, "high_woven", 12288)
         for g in range(SLOT_PASSES):
-            turn_values(v_got_high, g * P, SLOT_PASSES * P, (0, 7)[g], high_woven[:, g])
+            turn_words(v_got_high, g * 2 * P, (2, 3)[g], high_woven[:, g])
 
-        w0 = weights(p0, vs_cols0, NQ, "w0")
-        low_mx = quantised(low_woven[:].rearrange("p g e t -> p (g e t)"), SLOT_PASSES * P, "v_low", "capped0")
+        w0 = weights(p0, vs_cols[:, 0:PACK], NQ, "w0")
+        low_mx = [quantised(low_woven[g][:].rearrange("p e t -> p (e t)"), P, "v_low%d" % g, (1024, None)[g])
+                  for g in range(SLOT_PASSES)]
         w0_mx = quantised(w0, NQ, "w0")
-        w1 = [weights(p1[qh], vs_cols1, P, "w1_%d" % qh) for qh in range(Q_TILES)]
+        w1 = [weights(p1[qh], vs_cols[:, PACK:2 * PACK], P, "w1_%d" % qh) for qh in range(Q_TILES)]
         w1_mx = [quantised(w1[qh], P, "w1_%d" % qh) for qh in range(Q_TILES)]
         high_mx = [quantised(high_woven[:, g].rearrange("p e t -> p (e t)"), P, "v_high%d" % g)
                    for g in range(SLOT_PASSES)]
 
         for qh in range(Q_TILES):
             cols = slice(qh * P, (qh + 1) * P)
-            y_bank = bank(2 + qh, [P, DV], F32, "y_bank")
+            y_bank = bank(4 * qh, [P, DV], F32, "y_bank")
             for h in range(V_TILES):
                 for g in range(SLOT_PASSES):
                     w_codes, w_plane = (part[:, cols] for part in w0_mx) if g == 0 else (part[:] for part in w1_mx[qh])
-                    if h == 0:
-                        v_codes, v_plane = (part[:, g * P:(g + 1) * P] for part in low_mx)
-                    else:
-                        v_codes, v_plane = (part[:] for part in high_mx[g])
+                    v_codes, v_plane = (part[:] for part in (low_mx, high_mx)[h][g])
                     nc.tensor.matmul_mx(out=y_bank[:, h * P:(h + 1) * P], lhsT=w_codes.bitcast(FP8X4),
                                         lhsT_scale=w_plane, rhs=v_codes.bitcast(FP8X4), rhs_scale=v_plane,
                                         start=(g == 0 and h == 0),

@@ -77,7 +77,9 @@ def tile_attend_sigm_cap_kb_srtq256n1024t2048_kernel(tc, qT, k_words, k_scales, 
         nc.scalar.activation(out=warm_out[:], in_=warm_in[:], func=ACT.Sigmoid)
 
         ident32 = sbuf([P, P], F32, "ident32")
+        ident16 = sbuf([P, P], BF16, "ident16")
         make_identity(nc, ident32[:])
+        make_identity(nc, ident16[:])
         nc.gpsimd.memset(kb_pool[0:LAST, T // 2:T].bitcast(I32), 0)
         vs_pool = sbuf([P, T], F32, "vs_pool")
         nc.gpsimd.memset(vs_pool[0:LAST, :].bitcast(I32), 0)
@@ -142,21 +144,18 @@ def tile_attend_sigm_cap_kb_srtq256n1024t2048_kernel(tc, qT, k_words, k_scales, 
 
         v_low_bf = sbuf([P, T], BF16, "v_low_bf")
 
-        def turn_words(got, first_word, index, woven):
-            turned = bank(index, [P, 2, P], F32, "v_turned")
-            for u in range(2):
-                pairs = got[:].bitcast(F32)[:, first_word + u:first_word + 2 * P:2]
-                nc.tensor.transpose(turned[:, u, :], pairs, ident32[:])
-            nc.scalar.copy(out=woven.rearrange("p e t -> p (e t)").bitcast(F32).rearrange("p (c i u) -> p c u i", i=2, u=2),
-                           in_=turned[:].rearrange("p u (c i) -> p c u i", i=2))
-
-        def woven_slots(tile):
-            return tile[:].rearrange("p (b c t) -> p b t c", t=PACK, c=RUN)
+        def turn_values(got, first_col, step, index, woven):
+            turned = bank(index, [P, PACK, P], BF16, "v_turned")
+            for t in range(PACK):
+                col = first_col + t * step
+                nc.tensor.transpose(turned[:, t, :], got[:, col:col + P], ident16[:])
+            nc.scalar.copy(out=woven.rearrange("p (c i) t -> p c t i", i=4),
+                           in_=turned[:].rearrange("p t (c i) -> p c t i", i=4))
 
         def low_values(g, cols):
             got = sbuf([P, K_PASS], BF16, "v_got_low%d" % g)
             nc.scalar.activation(out=v_low_bf[:, cols], in_=v_low[g][:], func=ACT.Copy)
-            nc.scalar.activation(out=woven_slots(got), in_=v_low_bf[:, 0:reach(g)].indirect(listed(g)), func=ACT.Copy)
+            nc.scalar.activation(out=dealt(got), in_=v_low_bf[:, 0:reach(g)].indirect(listed(g)), func=ACT.Copy)
             return got
 
         def quantised(source, width, name, offset=None):
@@ -178,7 +177,7 @@ def tile_attend_sigm_cap_kb_srtq256n1024t2048_kernel(tc, qT, k_words, k_scales, 
                                 start=(half == 0), stop=(half == 1))
         got_low.append(low_values(1, tail))
         low_woven = [placed([P, P, PACK], BF16, "low_woven0", 8704)]
-        turn_words(got_low[0], 0, 6, low_woven[0][:])
+        turn_values(got_low[0], 0, P, 6, low_woven[0][:])
 
         def gather_words(g):
             got = sbuf([P, K_PASS], U32, "kw_got%d" % g)
@@ -234,15 +233,15 @@ def tile_attend_sigm_cap_kb_srtq256n1024t2048_kernel(tc, qT, k_words, k_scales, 
         p0 = sigmoid(capped0, 0, NQ, "p0")
         capped1 = capped_scores(1)
         low_woven.append(sbuf([P, P, PACK], BF16, "low_woven1"))
-        turn_words(got_low[1], 0, 0, low_woven[1][:])
+        turn_values(got_low[1], 0, P, 0, low_woven[1][:])
         vs_cols = columns(vs_got, 0, SLOT_PASSES * PACK, 1, "vs_turned")
         p1 = [sigmoid(capped1, qh * P, P, "p1_%d" % qh) for qh in range(Q_TILES)]
 
         v_got_high = sbuf([P, N], BF16, "v_got_high")
-        nc.vector.tensor_copy(out=woven_slots(v_got_high), in_=v_high[:].indirect(offsets[:]))
+        nc.vector.tensor_copy(out=dealt(v_got_high), in_=v_high[:].indirect(offsets[:]))
         high_woven = placed([P, SLOT_PASSES, P, PACK], BF16, "high_woven", 12288)
         for g in range(SLOT_PASSES):
-            turn_words(v_got_high, g * 2 * P, (2, 3)[g], high_woven[:, g])
+            turn_values(v_got_high, g * P, SLOT_PASSES * P, (2, 3)[g], high_woven[:, g])
 
         w0 = weights(p0, vs_cols[:, 0:PACK], NQ, "w0")
         low_mx = [quantised(low_woven[g][:].rearrange("p e t -> p (e t)"), P, "v_low%d" % g, (1024, None)[g])

@@ -100,12 +100,15 @@ def tile_attend_sigm_cap_kb_srtq256n1024t2048_kernel(tc, qT, k_words, k_scales, 
             load_scales(r)
         load_queries(1)
         load_scales(3)
-        v_low = [sbuf([P, reach(0)], F32, "v_low0"), placed([P, T - reach(0)], F32, "v_low1", 8192)]
+        pieces = (slice(0, reach(0) // 2), slice(reach(0) // 2, reach(0)), tail)
+        v_low = [sbuf([P, reach(0) // 2], F32, "v_low0"), sbuf([P, reach(0) // 2], F32, "v_low1"),
+                 placed([P, T - reach(0)], F32, "v_low2", 8192)]
         words = k_words[0].rearrange("p t b -> p (t b)").bitcast(I32)
-        nc.sync.dma_start(out=v_low[0][:], in_=vT[0:P, head])
+        for i in range(2):
+            nc.sync.dma_start(out=v_low[i][:], in_=vT[0:P, pieces[i]])
         nc.sync.dma_start(out=kw_pool[:, head], in_=words[:, head])
+        nc.sync.dma_start(out=v_low[2][:], in_=vT[0:P, tail])
         nc.sync.dma_start(out=kw_pool[:, tail], in_=words[:, tail])
-        nc.sync.dma_start(out=v_low[1][:], in_=vT[0:P, tail])
         nc.sync.dma_start(out=vs_pool[LAST:P, :], in_=vs[LAST:P, :])
 
         q_bf = sbuf([P, D_PASSES, NQ, PACK], BF16, "q_bf")
@@ -152,9 +155,11 @@ def tile_attend_sigm_cap_kb_srtq256n1024t2048_kernel(tc, qT, k_words, k_scales, 
             nc.scalar.copy(out=woven.rearrange("p (c i) t -> p c t i", i=4),
                            in_=turned[:].rearrange("p t (c i) -> p c t i", i=4))
 
-        def low_values(g, cols):
+        def cast_low(i):
+            nc.scalar.activation(out=v_low_bf[:, pieces[i]], in_=v_low[i][:], func=ACT.Copy)
+
+        def gather_low(g):
             got = sbuf([P, K_PASS], BF16, "v_got_low%d" % g)
-            nc.scalar.activation(out=v_low_bf[:, cols], in_=v_low[g][:], func=ACT.Copy)
             nc.scalar.activation(out=dealt(got), in_=v_low_bf[:, 0:reach(g)].indirect(listed(g)), func=ACT.Copy)
             return got
 
@@ -167,15 +172,13 @@ def tile_attend_sigm_cap_kb_srtq256n1024t2048_kernel(tc, qT, k_words, k_scales, 
             nc.vector.quantize_mx(out=codes[:].bitcast(FP8X4), scales=plane[:], in_=source)
             return codes, plane
 
-        got_low = [low_values(0, head)]
+        cast_low(0)
+        cast_low(1)
         half_kb = sbuf([P, SLOT_PASSES * PACK], F32, "half_kb", "v_low0")
         nc.scalar.activation(out=half_kb[:], in_=kb_cols, func=ACT.Copy, scale=0.5)
-        warm_bank = bank(4, [P, K_PASS], F32, "warm_bank")
-        for half in range(2):
-            nc.tensor.matmul_mx(out=warm_bank[:], lhsT=q_codes[:, 0:P].bitcast(FP8X4), lhsT_scale=q_plane[:, 0:P],
-                                rhs=q_codes[:].bitcast(FP8X4), rhs_scale=q_plane[:],
-                                start=(half == 0), stop=(half == 1))
-        got_low.append(low_values(1, tail))
+        got_low = [gather_low(0)]
+        cast_low(2)
+        got_low.append(gather_low(1))
         low_woven = [placed([P, P, PACK], BF16, "low_woven0", 8704)]
         turn_values(got_low[0], 0, P, 6, low_woven[0][:])
 
@@ -190,8 +193,7 @@ def tile_attend_sigm_cap_kb_srtq256n1024t2048_kernel(tc, qT, k_words, k_scales, 
                 in_=got[:].bitcast(U16).rearrange("p (b t c o) -> p b t o c", o=D_PASSES, t=PACK, c=RUN))
             return codes
 
-        kw_got = [gather_words(g) for g in range(SLOT_PASSES)]
-        k_codes = [part_words(kw_got[g], placed([P, D_PASSES * K_PASS], U16, "k_codes%d" % g, (6656, 9728)[g]))
+        k_codes = [part_words(gather_words(g), sbuf([P, D_PASSES * K_PASS], U16, "k_codes%d" % g))
                    for g in range(SLOT_PASSES)]
         vs_got = token_row(vs_pool, "vs_got")
 

@@ -18,13 +18,14 @@ P = 128
 NQ, N, T, D, DV = 256, 1024, 2048, 1024, 256
 PACK = 4
 K_PASS = P * PACK
-RUN = 8
 SLOT_PASSES = N // K_PASS
 D_PASSES = D // K_PASS
 Q_TILES = NQ // P
 V_TILES = DV // P
 LIST_COLS = K_PASS // 16
 LAST = P - 1
+SCALE_ROWS = 16 * D_PASSES
+SCALE_BASE = P - SCALE_ROWS
 
 FLOPS = 2 * NQ * N * (D + DV)
 BYTES = 4 * D * NQ + 4 * P * T + 32 * T + 4 * DV * T + 2 * 4 * T + 2 * P * N // 16 + 4 * NQ * DV
@@ -34,7 +35,6 @@ def tile_attend_sigm_cap_kb_srtq256n1024t2048_kernel(tc, qT, k_words, k_scales, 
     nc = tc.nc
     with ExitStack() as ctx:
         sb = ctx.enter_context(tc.tile_pool(name="sb", bufs=1))
-        late = ctx.enter_context(tc.tile_pool(name="late", bufs=1))
         ps = ctx.enter_context(tc.psum_pool(name="ps", bufs=1))
 
         def sbuf(shape, dtype, name, tag=None):
@@ -42,9 +42,6 @@ def tile_attend_sigm_cap_kb_srtq256n1024t2048_kernel(tc, qT, k_words, k_scales, 
 
         def tiles(count, shape, dtype, name):
             return [sbuf(shape, dtype, "%s%d" % (name, i)) for i in range(count)]
-
-        def placed(shape, dtype, name, offset):
-            return late.tile(shape, dtype, name=name, align_bytes=64, offset=offset)
 
         def bank(index, shape, dtype, name):
             return ps.tile(shape, dtype, name=name, tag="bank%d" % index)
@@ -55,219 +52,167 @@ def tile_attend_sigm_cap_kb_srtq256n1024t2048_kernel(tc, qT, k_words, k_scales, 
         def listed(g):
             return offsets[:, g * LIST_COLS:(g + 1) * LIST_COLS]
 
-        def reach(g):
-            return T - N + (g + 1) * K_PASS
-
-        def dealt(tile):
-            return tile[:].rearrange("p (t b c) -> p b t c", t=PACK, c=RUN)
-
-        head, tail = slice(0, reach(0)), slice(reach(0), T)
         ks_pool = sbuf([P, T], U8, "ks_pool")
         kb_pool = sbuf([P, T], F32, "kb_pool")
         kw_pool = sbuf([P, T], I32, "kw_pool")
-        k_plane = tiles(D_PASSES, [P, N], U8, "k_plane")
-
-        nc.vector.memset(ks_pool[:].bitcast(I32), 0)
-        nc.vector.memset(kb_pool[0:LAST, 0:T // 2].bitcast(I32), 0)
-        nc.vector.memset(k_plane[1][:].bitcast(I32), 0)
+        k_planes = sbuf([P, D_PASSES, N], U8, "k_planes")
 
         warm_in = sbuf([P, 1], F32, "warm_in", "vs_pool")
         warm_out = sbuf([P, 1], F32, "warm_out")
         nc.gpsimd.memset(warm_in[:], 0.0)
+        nc.gpsimd.memset(ks_pool[0:SCALE_BASE, :].bitcast(I32), 0)
+        nc.vector.memset(kb_pool[0:LAST, :].bitcast(I32), 0)
+        nc.gpsimd.memset(k_planes[:].rearrange("p o n -> p (o n)").bitcast(I32), 0)
         nc.scalar.activation(out=warm_out[:], in_=warm_in[:], func=ACT.Sigmoid)
 
-        ident32 = sbuf([P, P], F32, "ident32")
-        ident16 = sbuf([P, P], BF16, "ident16")
-        make_identity(nc, ident32[:])
-        make_identity(nc, ident16[:])
-        nc.gpsimd.memset(kb_pool[0:LAST, T // 2:T].bitcast(I32), 0)
+        ident = sbuf([P, P], F32, "ident")
+        make_identity(nc, ident[:])
         vs_pool = sbuf([P, T], F32, "vs_pool")
         nc.gpsimd.memset(vs_pool[0:LAST, :].bitcast(I32), 0)
 
-        nc.sync.dma_start(out=kb_pool[LAST:P, :], in_=kb[LAST:P, :])
         q_raw = tiles(D_PASSES, [P, PACK, NQ], F32, "q_raw")
 
         def load_queries(o):
             rows = qT[0, o * K_PASS:(o + 1) * K_PASS, :]
             nc.sync.dma_start(out=q_raw[o][:], in_=rows.rearrange("(p t) q -> p t q", t=PACK))
 
-        def load_scales(r):
-            nc.sync.dma_start(out=ks_pool[r:P:16, :].bitcast(I32),
-                              in_=k_scales[:, r:16:4, :].rearrange("o q t -> q o t").bitcast(I32))
-
-        load_queries(0)
-        for r in range(3):
-            load_scales(r)
-        load_queries(1)
-        load_scales(3)
-        pieces = (slice(0, reach(0) // 2), slice(reach(0) // 2, reach(0)), tail)
-        v_low = [sbuf([P, reach(0) // 2], F32, "v_low0"), sbuf([P, reach(0) // 2], F32, "v_low1"),
-                 placed([P, T - reach(0)], F32, "v_low2", 8192)]
         words = k_words[0].rearrange("p t b -> p (t b)").bitcast(I32)
-        for i in range(2):
-            nc.sync.dma_start(out=v_low[i][:], in_=vT[0:P, pieces[i]])
-        nc.sync.dma_start(out=kw_pool[:, head], in_=words[:, head])
-        nc.sync.dma_start(out=v_low[2][:], in_=vT[0:P, tail])
-        nc.sync.dma_start(out=kw_pool[:, tail], in_=words[:, tail])
+        nc.sync.dma_start(out=ks_pool[SCALE_BASE:P, :].bitcast(I32),
+                          in_=k_scales.rearrange("o f t -> f o t").bitcast(I32))
+        nc.sync.dma_start(out=kb_pool[LAST:P, :], in_=kb[LAST:P, :])
+        nc.sync.dma_start(out=kw_pool[:], in_=words)
         nc.sync.dma_start(out=vs_pool[LAST:P, :], in_=vs[LAST:P, :])
+        load_queries(0)
+        load_queries(1)
 
-        q_bf = sbuf([P, D_PASSES, NQ, PACK], BF16, "q_bf")
-        q_codes = sbuf([P, D_PASSES * NQ], U32, "q_codes")
-        q_plane = sbuf([P, D_PASSES * NQ], U8, "q_plane")
-        for o in range(D_PASSES):
-            nc.scalar.copy(out=q_bf[:, o].rearrange("p (c i) t -> p c t i", i=4),
-                           in_=q_raw[o][:].rearrange("p t (c i) -> p c t i", i=4))
-
-        def columns(got, first, count, index, name):
-            turned = bank(index, [P, P + count - 1], F32, name)
-            for j in reversed(range(count)):
-                col = (first + j) * P
-                nc.tensor.transpose(turned[:, j:j + P], got[:, col:col + P].bitcast(F32), ident32[:])
-            return turned[:, LAST:LAST + count]
-
-        def token_row(pool_tile, name):
-            got = sbuf([P, N], U32, name)
-            nc.vector.tensor_copy(out=got[:].rearrange("p (g t b c) -> p g b t c", g=SLOT_PASSES, t=PACK, c=RUN),
-                                  in_=pool_tile[:].bitcast(U32).indirect(offsets[:]))
-            return got
-
-        kb_cols = columns(token_row(kb_pool, "kb_got"), 0, SLOT_PASSES * PACK, 4, "kb_turned")
         ks_got = sbuf([P, N], U8, "ks_got")
-        nc.vector.tensor_copy(out=ks_got[:], in_=ks_pool[:].indirect(offsets[:]))
-        nc.vector.quantize_mx(out=q_codes[:].bitcast(FP8X4), scales=q_plane[:],
-                              in_=q_bf[:].rearrange("p o q t -> p (o q t)"))
-        nc.vector.tensor_copy(
-            out=k_plane[0][:].bitcast(I32).rearrange("p (t b w) -> p b t w", t=PACK, w=2),
-            in_=ks_got[:].bitcast(I32).rearrange("p (b t w) -> p b t w", t=PACK, w=2))
-        for quad in range(4):
-            nc.sync.dma_start(out=k_plane[1][32 * quad:32 * quad + 4, :].bitcast(I32),
-                              in_=k_plane[0][32 * quad + 16:32 * quad + 20, :].bitcast(I32))
-        v_high = sbuf([P, T], F32, "v_high")
-        nc.sync.dma_start(out=v_high[:], in_=vT[P:2 * P, :])
+        nc.vector.tensor_copy(out=ks_got[:].rearrange("p (g t m) -> p g m t", g=SLOT_PASSES, t=PACK),
+                              in_=ks_pool[:].indirect(offsets[:]))
 
-        v_low_bf = sbuf([P, T], BF16, "v_low_bf")
-
-        def turn_values(got, first_col, step, index, woven):
-            turned = bank(index, [P, PACK, P], BF16, "v_turned")
-            for t in range(PACK):
-                col = first_col + t * step
-                nc.tensor.transpose(turned[:, t, :], got[:, col:col + P], ident16[:])
-            nc.scalar.copy(out=woven.rearrange("p (c i) t -> p c t i", i=4),
-                           in_=turned[:].rearrange("p t (c i) -> p c t i", i=4))
-
-        def cast_low(i):
-            nc.scalar.activation(out=v_low_bf[:, pieces[i]], in_=v_low[i][:], func=ACT.Copy)
-
-        def gather_low(g):
-            got = sbuf([P, K_PASS], BF16, "v_got_low%d" % g)
-            nc.scalar.activation(out=dealt(got), in_=v_low_bf[:, 0:reach(g)].indirect(listed(g)), func=ACT.Copy)
+        def token_row(pool_tile, entries, width, name, tag=None):
+            got = sbuf([P, width], F32, name, tag)
+            nc.scalar.activation(out=got[:], in_=pool_tile[:].indirect(entries), func=ACT.Copy)
             return got
 
-        def quantised(source, width, name, offset=None):
-            if offset is None:
-                codes = sbuf([P, width], U32, name + "_codes")
-            else:
-                codes = placed([P, width], U32, name + "_codes", offset)
+        def token_columns(row, name):
+            cols = sbuf([P, PACK], F32, name)
+            nc.sync.dma_start(out=cols[:], in_=row)
+            return cols
+
+        def weave(copy, woven, planes):
+            copy(out=woven.rearrange("p (c i) t -> p c t i", i=4), in_=planes.rearrange("p t (c i) -> p c t i", i=4))
+
+        kb_got = token_row(kb_pool, offsets[:], N, "kb_got")
+        vs_got = [token_row(vs_pool, listed(0), K_PASS, "vs_got0")]
+        q_bf = tiles(D_PASSES, [P, NQ, PACK], BF16, "q_bf")
+        for o in range(D_PASSES):
+            weave(nc.scalar.copy, q_bf[o][:], q_raw[o][:])
+        vs_got.append(token_row(vs_pool, listed(1), K_PASS, "vs_got1", "q_raw1"))
+        rows_a_quad = SCALE_ROWS // 4
+        for quad in range(4):
+            first = SCALE_BASE + quad * rows_a_quad
+            nc.sync.dma_start(out=k_planes[32 * quad:32 * quad + 4, :, :].bitcast(I32),
+                              in_=ks_got[first:first + rows_a_quad, :].bitcast(I32))
+        kb_cols = [token_columns(kb_got[LAST:P, g * K_PASS:(g + 1) * K_PASS], "kb_cols%d" % g) for g in range(SLOT_PASSES)]
+        v_pool = tiles(V_TILES, [P, T], F32, "v_pool")
+        for h in range(V_TILES):
+            nc.sync.dma_start(out=v_pool[h][:], in_=vT[h * P:(h + 1) * P, :])
+        vs_cols = [token_columns(vs_got[g][LAST:P, :], "vs_cols%d" % g) for g in range(SLOT_PASSES)]
+
+        def quantised(source, width, name, tag=None):
+            codes = sbuf([P, width], U32, name + "_codes", tag)
             plane = sbuf([P, width], U8, name + "_plane")
             nc.vector.quantize_mx(out=codes[:].bitcast(FP8X4), scales=plane[:], in_=source)
             return codes, plane
 
-        cast_low(0)
-        cast_low(1)
-        half_kb = sbuf([P, SLOT_PASSES * PACK], F32, "half_kb", "v_low0")
-        nc.scalar.activation(out=half_kb[:], in_=kb_cols, func=ACT.Copy, scale=0.5)
-        got_low = [gather_low(0)]
-        cast_low(2)
-        got_low.append(gather_low(1))
-        low_woven = [placed([P, P, PACK], BF16, "low_woven0", 8704)]
-        turn_values(got_low[0], 0, P, 6, low_woven[0][:])
-
         def gather_words(g):
             got = sbuf([P, K_PASS], U32, "kw_got%d" % g)
-            nc.vector.tensor_copy(out=got[:], in_=kw_pool[:, 0:reach(g)].bitcast(U32).indirect(listed(g)))
+            nc.vector.tensor_copy(out=got[:].rearrange("p (t m) -> p m t", t=PACK),
+                                  in_=kw_pool[:].bitcast(U32).indirect(listed(g)))
             return got
 
-        def part_words(got, codes):
-            nc.vector.tensor_copy(
-                out=codes[:].rearrange("p (o t b c) -> p b t o c", o=D_PASSES, t=PACK, c=RUN),
-                in_=got[:].bitcast(U16).rearrange("p (b t c o) -> p b t o c", o=D_PASSES, t=PACK, c=RUN))
+        def part_words(got, name, tag=None):
+            codes = sbuf([P, D_PASSES, K_PASS], U16, name, tag)
+            nc.vector.tensor_copy(out=codes[:], in_=got[:].bitcast(U16).rearrange("p (j o) -> p o j", o=D_PASSES))
             return codes
 
-        k_codes = [part_words(gather_words(g), sbuf([P, D_PASSES * K_PASS], U16, "k_codes%d" % g))
-                   for g in range(SLOT_PASSES)]
-        vs_got = token_row(vs_pool, "vs_got")
+        half_kb = sbuf([P, SLOT_PASSES, PACK], F32, "half_kb")
+        for g in range(SLOT_PASSES):
+            nc.scalar.activation(out=half_kb[:, g, :], in_=kb_cols[g][:], func=ACT.Copy, scale=0.5)
+
+        kw_got = [gather_words(g) for g in range(SLOT_PASSES)]
+        k_codes = [part_words(kw_got[0], "k_codes0")]
+        q_mx = [quantised(q_bf[0][:].rearrange("p q t -> p (q t)"), NQ, "q0")]
+        k_codes.append(part_words(kw_got[1], "k_codes1", "q_bf0"))
+        q_mx.append(quantised(q_bf[1][:].rearrange("p q t -> p (q t)"), NQ, "q1"))
+
+        v_got = tiles(V_TILES, [P, N], BF16, "v_got")
+        for h in range(V_TILES):
+            nc.vector.tensor_copy(out=v_got[h][:], in_=v_pool[h][:].indirect(offsets[:]))
 
         def capped_scores(g):
-            capped = placed([P, PACK * NQ], F32, "capped%d" % g, 12288 * g)
+            capped = sbuf([P, PACK, NQ], F32, "capped%d" % g)
             for t in range(PACK):
-                score = bank(((0, 1, 2, 3), (4, 7, 2, 3))[g][t], [P, NQ], F32, "score")
-                for qh in range(Q_TILES):
-                    for o in reversed(range(D_PASSES)):
-                        kc = o * K_PASS + t * P
-                        sc = (t * SLOT_PASSES + g) * P
-                        qc = o * NQ + qh * P
-                        nc.tensor.matmul_mx(
-                            out=score[:, qh * P:(qh + 1) * P],
-                            lhsT=k_codes[g][:, kc:kc + P].bitcast(FP4X4),
-                            lhsT_scale=k_plane[o][:, sc:sc + P],
-                            rhs=q_codes[:, qc:qc + P].bitcast(FP8X4),
-                            rhs_scale=q_plane[:, qc:qc + P],
-                            start=(o == D_PASSES - 1), stop=(o == 0))
-                col = g * PACK + t
-                nc.scalar.activation(out=capped[:, t * NQ:(t + 1) * NQ], in_=score[:], func=ACT.Tanh,
-                                     bias=half_kb[:, col:col + 1], scale=0.5)
+                score = bank(g * PACK + t, [P, NQ], F32, "score")
+                for o in range(D_PASSES):
+                    nc.tensor.matmul_mx(
+                        out=score[:],
+                        lhsT=k_codes[g][:, o, t * P:(t + 1) * P].bitcast(FP4X4),
+                        lhsT_scale=k_planes[:, o, (g * PACK + t) * P:(g * PACK + t + 1) * P],
+                        rhs=q_mx[o][0][:].bitcast(FP8X4), rhs_scale=q_mx[o][1][:],
+                        start=(o == 0), stop=(o == D_PASSES - 1))
+                nc.scalar.activation(out=capped[:, t, :], in_=score[:], func=ACT.Tanh,
+                                     bias=half_kb[:, g, t:t + 1], scale=0.5)
             return capped
 
         def sigmoid(capped, first, width, name):
             p = sbuf([P, width, PACK], F32, name)
-            rows = capped[:].rearrange("p (t q) -> p t q", t=PACK)[:, :, first:first + width]
             nc.scalar.activation(out=p[:].rearrange("p (c i) t -> p c t i", i=4),
-                                 in_=rows.rearrange("p t (c i) -> p c t i", i=4), func=ACT.Sigmoid, scale=2.0)
+                                 in_=capped[:, :, first:first + width].rearrange("p t (c i) -> p c t i", i=4),
+                                 func=ACT.Sigmoid, scale=2.0)
             return p
 
-        def weights(p, cols, width, name):
+        def weights(p, g, width, name):
             w = sbuf([P, width, PACK], BF16, name)
-            nc.vector.tensor_tensor(out=w[:], in0=p[:], in1=cols.unsqueeze(1).to_broadcast([P, width, PACK]),
+            nc.vector.tensor_tensor(out=w[:], in0=p[:], in1=vs_cols[g][:].unsqueeze(1).to_broadcast([P, width, PACK]),
                                     op=ALU.mult)
             return w[:].rearrange("p q t -> p (q t)")
+
+        def turned_values(h):
+            pairs = v_got[h][:].bitcast(F32)
+            turned = bank(h, [P, SLOT_PASSES, 2, P], F32, "v_turned")
+            for g in range(SLOT_PASSES):
+                for u in range(2):
+                    nc.tensor.transpose(turned[:, g, u, :], pairs[:, g * 2 * P + u:(g + 1) * 2 * P:2], ident[:])
+            woven = sbuf([P, SLOT_PASSES, P, 2], F32, "v_woven%d" % h)
+            nc.scalar.copy(out=woven[:], in_=turned[:].rearrange("p g u e -> p g e u"))
+            return woven[:].rearrange("p g e u -> p (g e u)").bitcast(BF16)
 
         capped0 = capped_scores(0)
         p0 = sigmoid(capped0, 0, NQ, "p0")
         capped1 = capped_scores(1)
-        low_woven.append(sbuf([P, P, PACK], BF16, "low_woven1"))
-        turn_values(got_low[1], 0, P, 0, low_woven[1][:])
-        vs_cols = columns(vs_got, 0, SLOT_PASSES * PACK, 1, "vs_turned")
+        v_woven = [turned_values(0)]
         p1 = [sigmoid(capped1, qh * P, P, "p1_%d" % qh) for qh in range(Q_TILES)]
+        v_woven.append(turned_values(1))
 
-        v_got_high = sbuf([P, N], BF16, "v_got_high")
-        nc.vector.tensor_copy(out=dealt(v_got_high), in_=v_high[:].indirect(offsets[:]))
-        high_woven = placed([P, SLOT_PASSES, P, PACK], BF16, "high_woven", 12288)
-        for g in range(SLOT_PASSES):
-            turn_values(v_got_high, g * P, SLOT_PASSES * P, (2, 3)[g], high_woven[:, g])
-
-        w0 = weights(p0, vs_cols[:, 0:PACK], NQ, "w0")
-        low_mx = [quantised(low_woven[g][:].rearrange("p e t -> p (e t)"), P, "v_low%d" % g, (1024, None)[g])
-                  for g in range(SLOT_PASSES)]
+        w0 = weights(p0, 0, NQ, "w0")
+        v_mx = [quantised(v_woven[0], SLOT_PASSES * P, "v0", "p0")]
         w0_mx = quantised(w0, NQ, "w0")
-        w1 = [weights(p1[qh], vs_cols[:, PACK:2 * PACK], P, "w1_%d" % qh) for qh in range(Q_TILES)]
+        w1 = [weights(p1[qh], 1, P, "w1_%d" % qh) for qh in range(Q_TILES)]
+        v_mx.append(quantised(v_woven[1], SLOT_PASSES * P, "v1", "p1_1"))
         w1_mx = [quantised(w1[qh], P, "w1_%d" % qh) for qh in range(Q_TILES)]
-        high_mx = [quantised(high_woven[:, g].rearrange("p e t -> p (e t)"), P, "v_high%d" % g)
-                   for g in range(SLOT_PASSES)]
 
         for qh in range(Q_TILES):
             cols = slice(qh * P, (qh + 1) * P)
-            y_bank = bank(4 * qh, [P, DV], F32, "y_bank")
-            for h in range(V_TILES):
-                for g in range(SLOT_PASSES):
+            y_bank = bank(2 + qh, [P, DV], F32, "y_bank")
+            for g in range(SLOT_PASSES):
+                for h in range(V_TILES):
                     w_codes, w_plane = (part[:, cols] for part in w0_mx) if g == 0 else (part[:] for part in w1_mx[qh])
-                    v_codes, v_plane = (part[:] for part in (low_mx, high_mx)[h][g])
+                    v_codes, v_plane = (part[:, g * P:(g + 1) * P] for part in v_mx[h])
                     nc.tensor.matmul_mx(out=y_bank[:, h * P:(h + 1) * P], lhsT=w_codes.bitcast(FP8X4),
                                         lhsT_scale=w_plane, rhs=v_codes.bitcast(FP8X4), rhs_scale=v_plane,
                                         start=(g == 0 and h == 0),
                                         stop=(g == SLOT_PASSES - 1 and h == V_TILES - 1))
             y = sbuf([P, DV], F32, "y%d" % qh)
-            if qh == 0:
-                nc.scalar.activation(out=y[:], in_=y_bank[:], func=ACT.Copy, scale=1.0 / 16.0)
-            else:
-                nc.vector.tensor_scalar_mul(y[:], y_bank[:], 1.0 / 16.0)
+            nc.scalar.activation(out=y[:], in_=y_bank[:], func=ACT.Copy, scale=1.0 / 16.0)
             nc.sync.dma_start(out=out[0, cols, :], in_=y[:])

@@ -26,6 +26,7 @@ LIST_COLS = K_PASS // 16
 LAST = P - 1
 SCALE_ROWS = 16 * D_PASSES
 SCALE_BASE = P - SCALE_ROWS
+HEAD = T - N + K_PASS
 
 FLOPS = 2 * NQ * N * (D + DV)
 BYTES = 4 * D * NQ + 4 * P * T + 32 * T + 4 * DV * T + 2 * 4 * T + 2 * P * N // 16 + 4 * NQ * DV
@@ -89,15 +90,13 @@ def tile_attend_sigm_cap_kb_srtq256n1024t2048_kernel(tc, qT, k_words, k_scales, 
         nc.vector.tensor_copy(out=ks_got[:].rearrange("p (g t m) -> p g m t", g=SLOT_PASSES, t=PACK),
                               in_=ks_pool[:].indirect(offsets[:]))
 
-        def token_row(pool_tile, entries, width, name, tag=None):
-            got = sbuf([P, width], F32, name, tag)
+        def token_row(pool_tile, entries, width, name):
+            got = sbuf([P, width], F32, name)
             nc.scalar.activation(out=got[:], in_=pool_tile[:].indirect(entries), func=ACT.Copy)
             return got
 
-        def token_columns(row, name):
-            cols = sbuf([P, PACK], F32, name)
-            nc.sync.dma_start(out=cols[:], in_=row)
-            return cols
+        def lay_out(cols, g, row):
+            nc.sync.dma_start(out=cols[:, g, 0:PACK], in_=row)
 
         def weave(copy, woven, planes):
             copy(out=woven.rearrange("p (c i) t -> p c t i", i=4), in_=planes.rearrange("p t (c i) -> p c t i", i=4))
@@ -107,17 +106,21 @@ def tile_attend_sigm_cap_kb_srtq256n1024t2048_kernel(tc, qT, k_words, k_scales, 
         q_bf = tiles(D_PASSES, [P, NQ, PACK], BF16, "q_bf")
         for o in range(D_PASSES):
             weave(nc.scalar.copy, q_bf[o][:], q_raw[o][:])
-        vs_got.append(token_row(vs_pool, listed(1), K_PASS, "vs_got1", "q_raw1"))
         rows_a_quad = SCALE_ROWS // 4
         for quad in range(4):
             first = SCALE_BASE + quad * rows_a_quad
             nc.sync.dma_start(out=k_planes[32 * quad:32 * quad + 4, :, :].bitcast(I32),
                               in_=ks_got[first:first + rows_a_quad, :].bitcast(I32))
-        kb_cols = [token_columns(kb_got[LAST:P, g * K_PASS:(g + 1) * K_PASS], "kb_cols%d" % g) for g in range(SLOT_PASSES)]
-        v_pool = tiles(V_TILES, [P, T], F32, "v_pool")
-        for h in range(V_TILES):
-            nc.sync.dma_start(out=v_pool[h][:], in_=vT[h * P:(h + 1) * P, :])
-        vs_cols = [token_columns(vs_got[g][LAST:P, :], "vs_cols%d" % g) for g in range(SLOT_PASSES)]
+        kb_cols = sbuf([P, SLOT_PASSES, 2 * PACK], F32, "kb_cols")
+        vs_cols = sbuf([P, SLOT_PASSES, 2 * PACK], F32, "vs_cols")
+        for g in range(SLOT_PASSES):
+            lay_out(kb_cols, g, kb_got[LAST:P, g * K_PASS:(g + 1) * K_PASS])
+        v_low = sbuf([P, T], F32, "v_low")
+        v_high = sbuf([P, T], F32, "v_high")
+        nc.sync.dma_start(out=v_low[:, 0:HEAD], in_=vT[0:P, 0:HEAD])
+        nc.sync.dma_start(out=v_low[:, HEAD:T], in_=vT[0:P, HEAD:T])
+        nc.sync.dma_start(out=v_high[:], in_=vT[P:2 * P, :])
+        lay_out(vs_cols, 0, vs_got[0][LAST:P, :])
 
         def quantised(source, width, name, tag=None):
             codes = sbuf([P, width], U32, name + "_codes", tag)
@@ -137,36 +140,41 @@ def tile_attend_sigm_cap_kb_srtq256n1024t2048_kernel(tc, qT, k_words, k_scales, 
             return codes
 
         half_kb = sbuf([P, SLOT_PASSES, PACK], F32, "half_kb")
-        for g in range(SLOT_PASSES):
-            nc.scalar.activation(out=half_kb[:, g, :], in_=kb_cols[g][:], func=ACT.Copy, scale=0.5)
+        nc.scalar.activation(out=half_kb[:], in_=kb_cols[:, :, 0:PACK], func=ACT.Copy, scale=0.5)
 
         kw_got = [gather_words(g) for g in range(SLOT_PASSES)]
         k_codes = [part_words(kw_got[0], "k_codes0")]
-        q_mx = [quantised(q_bf[0][:].rearrange("p q t -> p (q t)"), NQ, "q0")]
-        k_codes.append(part_words(kw_got[1], "k_codes1", "q_bf0"))
-        q_mx.append(quantised(q_bf[1][:].rearrange("p q t -> p (q t)"), NQ, "q1"))
+        q_mx = [quantised(q_bf[o][:].rearrange("p q t -> p (q t)"), NQ, "q%d" % o) for o in range(D_PASSES)]
+        k_codes.append(part_words(kw_got[1], "k_codes1", "q_bf1"))
+        vs_got.append(sbuf([P, K_PASS], F32, "vs_got1", "kw_got1"))
+        nc.vector.tensor_copy(out=vs_got[1][:], in_=vs_pool[:].indirect(listed(1)))
+        lay_out(vs_cols, 1, vs_got[1][LAST:P, :])
 
-        v_got = tiles(V_TILES, [P, N], BF16, "v_got")
-        for h in range(V_TILES):
-            nc.vector.tensor_copy(out=v_got[h][:], in_=v_pool[h][:].indirect(offsets[:]))
+        low_got = tiles(SLOT_PASSES, [P, K_PASS], BF16, "low_got")
+        high_got = tiles(SLOT_PASSES, [P, K_PASS], BF16, "high_got")
+        for g in range(SLOT_PASSES):
+            nc.vector.tensor_copy(out=low_got[g][:].rearrange("p (u m e) -> p m u e", u=2, e=2),
+                                  in_=v_low[:, 0:(HEAD, T)[g]].indirect(listed(g)))
+        for g in range(SLOT_PASSES):
+            nc.vector.tensor_copy(out=high_got[g][:], in_=v_high[:].indirect(listed(g)))
 
         def capped_scores(g):
             capped = sbuf([P, PACK, NQ], F32, "capped%d" % g)
             for t in range(PACK):
                 score = bank(g * PACK + t, [P, NQ], F32, "score")
-                for o in range(D_PASSES):
+                order = (range(D_PASSES), reversed(range(D_PASSES)))[g]
+                for step, o in enumerate(order):
                     nc.tensor.matmul_mx(
                         out=score[:],
                         lhsT=k_codes[g][:, o, t * P:(t + 1) * P].bitcast(FP4X4),
                         lhsT_scale=k_planes[:, o, (g * PACK + t) * P:(g * PACK + t + 1) * P],
                         rhs=q_mx[o][0][:].bitcast(FP8X4), rhs_scale=q_mx[o][1][:],
-                        start=(o == 0), stop=(o == D_PASSES - 1))
+                        start=(step == 0), stop=(step == D_PASSES - 1))
                 nc.scalar.activation(out=capped[:, t, :], in_=score[:], func=ACT.Tanh,
                                      bias=half_kb[:, g, t:t + 1], scale=0.5)
             return capped
 
-        def sigmoid(capped, first, width, name):
-            p = sbuf([P, width, PACK], F32, name)
+        def sigmoid(capped, first, width, p):
             nc.scalar.activation(out=p[:].rearrange("p (c i) t -> p c t i", i=4),
                                  in_=capped[:, :, first:first + width].rearrange("p t (c i) -> p c t i", i=4),
                                  func=ACT.Sigmoid, scale=2.0)
@@ -174,45 +182,44 @@ def tile_attend_sigm_cap_kb_srtq256n1024t2048_kernel(tc, qT, k_words, k_scales, 
 
         def weights(p, g, width, name):
             w = sbuf([P, width, PACK], BF16, name)
-            nc.vector.tensor_tensor(out=w[:], in0=p[:], in1=vs_cols[g][:].unsqueeze(1).to_broadcast([P, width, PACK]),
+            nc.vector.tensor_tensor(out=w[:], in0=p[:], in1=vs_cols[:, g, 0:PACK].unsqueeze(1).to_broadcast([P, width, PACK]),
                                     op=ALU.mult)
             return w[:].rearrange("p q t -> p (q t)")
 
-        def turned_values(h):
-            pairs = v_got[h][:].bitcast(F32)
-            turned = bank(h, [P, SLOT_PASSES, 2, P], F32, "v_turned")
-            for g in range(SLOT_PASSES):
-                for u in range(2):
-                    nc.tensor.transpose(turned[:, g, u, :], pairs[:, g * 2 * P + u:(g + 1) * 2 * P:2], ident[:])
-            woven = sbuf([P, SLOT_PASSES, P, 2], F32, "v_woven%d" % h)
-            nc.scalar.copy(out=woven[:], in_=turned[:].rearrange("p g u e -> p g e u"))
-            return woven[:].rearrange("p g e u -> p (g e u)").bitcast(BF16)
+        def turned_values(g):
+            turned = bank(g, [P, V_TILES, 2, P], F32, "v_turned")
+            for u in range(2):
+                nc.tensor.transpose(turned[:, 0, u, :], low_got[g][:].bitcast(F32)[:, u * P:(u + 1) * P], ident[:])
+            for u in range(2):
+                nc.tensor.transpose(turned[:, 1, u, :], high_got[g][:].bitcast(F32)[:, u:2 * P:2], ident[:])
+            woven = sbuf([P, V_TILES, P, 2], F32, "v_woven%d" % g)
+            nc.scalar.copy(out=woven[:], in_=turned[:].rearrange("p h u e -> p h e u"))
+            return woven[:].rearrange("p h e u -> p (h e u)").bitcast(BF16)
 
         capped0 = capped_scores(0)
-        p0 = sigmoid(capped0, 0, NQ, "p0")
+        p0 = sigmoid(capped0, 0, NQ, sbuf([P, NQ, PACK], F32, "p0"))
         capped1 = capped_scores(1)
         v_woven = [turned_values(0)]
-        p1 = [sigmoid(capped1, qh * P, P, "p1_%d" % qh) for qh in range(Q_TILES)]
+        p1 = [sigmoid(capped1, qh * P, P, sbuf([P, P, PACK], F32, "p1_%d" % qh)) for qh in range(Q_TILES)]
         v_woven.append(turned_values(1))
 
         w0 = weights(p0, 0, NQ, "w0")
-        v_mx = [quantised(v_woven[0], SLOT_PASSES * P, "v0", "p0")]
+        w1 = [weights(p1[0], 1, P, "w1_0")]
         w0_mx = quantised(w0, NQ, "w0")
-        w1 = [weights(p1[qh], 1, P, "w1_%d" % qh) for qh in range(Q_TILES)]
-        v_mx.append(quantised(v_woven[1], SLOT_PASSES * P, "v1", "p1_1"))
+        v_mx = [quantised(v_woven[0], DV, "v0", "p1_0")]
+        w1.append(weights(p1[1], 1, P, "w1_1"))
+        v_mx.append(quantised(v_woven[1], DV, "v1", "p1_1"))
         w1_mx = [quantised(w1[qh], P, "w1_%d" % qh) for qh in range(Q_TILES)]
 
         for qh in range(Q_TILES):
             cols = slice(qh * P, (qh + 1) * P)
             y_bank = bank(2 + qh, [P, DV], F32, "y_bank")
             for g in range(SLOT_PASSES):
-                for h in range(V_TILES):
-                    w_codes, w_plane = (part[:, cols] for part in w0_mx) if g == 0 else (part[:] for part in w1_mx[qh])
-                    v_codes, v_plane = (part[:, g * P:(g + 1) * P] for part in v_mx[h])
-                    nc.tensor.matmul_mx(out=y_bank[:, h * P:(h + 1) * P], lhsT=w_codes.bitcast(FP8X4),
-                                        lhsT_scale=w_plane, rhs=v_codes.bitcast(FP8X4), rhs_scale=v_plane,
-                                        start=(g == 0 and h == 0),
-                                        stop=(g == SLOT_PASSES - 1 and h == V_TILES - 1))
+                w_codes, w_plane = (part[:, cols] for part in w0_mx) if g == 0 else (part[:] for part in w1_mx[qh])
+                v_codes, v_plane = (part[:] for part in v_mx[g])
+                nc.tensor.matmul_mx(out=y_bank[:], lhsT=w_codes.bitcast(FP8X4), lhsT_scale=w_plane,
+                                    rhs=v_codes.bitcast(FP8X4), rhs_scale=v_plane,
+                                    start=(g == 0), stop=(g == SLOT_PASSES - 1))
             y = sbuf([P, DV], F32, "y%d" % qh)
             nc.scalar.activation(out=y[:], in_=y_bank[:], func=ACT.Copy, scale=1.0 / 16.0)
             nc.sync.dma_start(out=out[0, cols, :], in_=y[:])

@@ -26,7 +26,6 @@ LIST_COLS = K_PASS // 16
 LAST = P - 1
 SCALE_ROWS = 16 * D_PASSES
 SCALE_BASE = P - SCALE_ROWS
-HEAD = T - N + K_PASS
 
 FLOPS = 2 * NQ * N * (D + DV)
 BYTES = 4 * D * NQ + 4 * P * T + 32 * T + 4 * DV * T + 2 * 4 * T + 2 * P * N // 16 + 4 * NQ * DV
@@ -58,18 +57,16 @@ def tile_attend_sigm_cap_kb_srtq256n1024t2048_kernel(tc, qT, k_words, k_scales, 
         kw_pool = sbuf([P, T], I32, "kw_pool")
         k_planes = sbuf([P, D_PASSES, N], U8, "k_planes")
 
-        warm_in = sbuf([P, 1], F32, "warm_in", "vs_pool")
+        vs_pool = sbuf([P, T], F32, "vs_pool")
+
+        warm_in = sbuf([P, 1], F32, "warm_in")
         warm_out = sbuf([P, 1], F32, "warm_out")
         nc.gpsimd.memset(warm_in[:], 0.0)
-        nc.gpsimd.memset(ks_pool[0:SCALE_BASE, :].bitcast(I32), 0)
-        nc.vector.memset(kb_pool[0:LAST, :].bitcast(I32), 0)
-        nc.gpsimd.memset(k_planes[:].rearrange("p o n -> p (o n)").bitcast(I32), 0)
         nc.scalar.activation(out=warm_out[:], in_=warm_in[:], func=ACT.Sigmoid)
-
-        ident = sbuf([P, P], F32, "ident")
-        make_identity(nc, ident[:])
-        vs_pool = sbuf([P, T], F32, "vs_pool")
-        nc.gpsimd.memset(vs_pool[0:LAST, :].bitcast(I32), 0)
+        nc.gpsimd.memset(k_planes[:].rearrange("p o n -> p (o n)").bitcast(I32), 0)
+        nc.vector.memset(ks_pool[0:SCALE_BASE, :].bitcast(I32), 0)
+        nc.vector.memset(kb_pool[0:LAST, :].bitcast(I32), 0)
+        nc.vector.memset(vs_pool[0:LAST, :].bitcast(I32), 0)
 
         q_raw = tiles(D_PASSES, [P, PACK, NQ], F32, "q_raw")
 
@@ -81,46 +78,48 @@ def tile_attend_sigm_cap_kb_srtq256n1024t2048_kernel(tc, qT, k_words, k_scales, 
         nc.sync.dma_start(out=ks_pool[SCALE_BASE:P, :].bitcast(I32),
                           in_=k_scales.rearrange("o f t -> f o t").bitcast(I32))
         nc.sync.dma_start(out=kb_pool[LAST:P, :], in_=kb[LAST:P, :])
-        nc.sync.dma_start(out=kw_pool[:], in_=words)
         nc.sync.dma_start(out=vs_pool[LAST:P, :], in_=vs[LAST:P, :])
+        nc.sync.dma_start(out=kw_pool[:], in_=words)
         load_queries(0)
         load_queries(1)
 
         ks_got = sbuf([P, N], U8, "ks_got")
-        nc.vector.tensor_copy(out=ks_got[:].rearrange("p (g t m) -> p g m t", g=SLOT_PASSES, t=PACK),
-                              in_=ks_pool[:].indirect(offsets[:]))
-
-        def token_row(pool_tile, entries, width, name):
-            got = sbuf([P, width], F32, name)
-            nc.scalar.activation(out=got[:], in_=pool_tile[:].indirect(entries), func=ACT.Copy)
-            return got
+        ks_dealt = sbuf([P, N], U8, "ks_dealt")
+        nc.vector.tensor_copy(out=ks_got[:], in_=ks_pool[:].indirect(offsets[:]))
+        nc.vector.tensor_copy(out=ks_dealt[:].rearrange("p (t c i) -> p c t i", t=PACK, i=4),
+                              in_=ks_got[:].rearrange("p (c i t) -> p c t i", t=PACK, i=4))
 
         def lay_out(cols, g, row):
             nc.sync.dma_start(out=cols[:, g, 0:PACK], in_=row)
 
-        def weave(copy, woven, planes):
-            copy(out=woven.rearrange("p (c i) t -> p c t i", i=4), in_=planes.rearrange("p t (c i) -> p c t i", i=4))
+        def weave(woven, planes):
+            nc.scalar.copy(out=woven.rearrange("p (c i) t -> p c t i", i=4),
+                           in_=planes.rearrange("p t (c i) -> p c t i", i=4))
 
-        kb_got = token_row(kb_pool, offsets[:], N, "kb_got")
-        vs_got = [token_row(vs_pool, listed(0), K_PASS, "vs_got0")]
+        def gather_vs(g, tag=None):
+            got = sbuf([P, K_PASS], F32, "vs_got%d" % g, tag)
+            nc.vector.tensor_copy(out=got[:], in_=vs_pool[:].indirect(listed(g)))
+            return got
+
+        kb_got = sbuf([P, N], F32, "kb_got")
+        nc.scalar.activation(out=kb_got[:], in_=kb_pool[:].indirect(offsets[:]), func=ACT.Copy)
+        vs_first = gather_vs(0)
         q_bf = tiles(D_PASSES, [P, NQ, PACK], BF16, "q_bf")
         for o in range(D_PASSES):
-            weave(nc.scalar.copy, q_bf[o][:], q_raw[o][:])
+            weave(q_bf[o][:], q_raw[o][:])
         rows_a_quad = SCALE_ROWS // 4
         for quad in range(4):
             first = SCALE_BASE + quad * rows_a_quad
             nc.sync.dma_start(out=k_planes[32 * quad:32 * quad + 4, :, :].bitcast(I32),
-                              in_=ks_got[first:first + rows_a_quad, :].bitcast(I32))
+                              in_=ks_dealt[first:first + rows_a_quad, :].bitcast(I32))
         kb_cols = sbuf([P, SLOT_PASSES, 2 * PACK], F32, "kb_cols")
         vs_cols = sbuf([P, SLOT_PASSES, 2 * PACK], F32, "vs_cols")
-        for g in range(SLOT_PASSES):
-            lay_out(kb_cols, g, kb_got[LAST:P, g * K_PASS:(g + 1) * K_PASS])
-        v_low = sbuf([P, T], F32, "v_low")
-        v_high = sbuf([P, T], F32, "v_high")
-        nc.sync.dma_start(out=v_low[:, 0:HEAD], in_=vT[0:P, 0:HEAD])
-        nc.sync.dma_start(out=v_low[:, HEAD:T], in_=vT[0:P, HEAD:T])
-        nc.sync.dma_start(out=v_high[:], in_=vT[P:2 * P, :])
-        lay_out(vs_cols, 0, vs_got[0][LAST:P, :])
+        v_pool = tiles(V_TILES, [P, T], F32, "v_pool")
+        lay_out(kb_cols, 0, kb_got[LAST:P, 0:K_PASS])
+        lay_out(vs_cols, 0, vs_first[LAST:P, :])
+        nc.sync.dma_start(out=v_pool[0][:], in_=vT[0:P, :])
+        lay_out(kb_cols, 1, kb_got[LAST:P, K_PASS:N])
+        nc.sync.dma_start(out=v_pool[1][:], in_=vT[P:2 * P, :])
 
         def quantised(source, width, name, tag=None):
             codes = sbuf([P, width], U32, name + "_codes", tag)
@@ -130,35 +129,30 @@ def tile_attend_sigm_cap_kb_srtq256n1024t2048_kernel(tc, qT, k_words, k_scales, 
 
         def gather_words(g):
             got = sbuf([P, K_PASS], U32, "kw_got%d" % g)
-            nc.vector.tensor_copy(out=got[:].rearrange("p (t m) -> p m t", t=PACK),
-                                  in_=kw_pool[:].bitcast(U32).indirect(listed(g)))
+            nc.vector.tensor_copy(out=got[:], in_=kw_pool[:].bitcast(U32).indirect(listed(g)))
             return got
 
         def part_words(got, name, tag=None):
             codes = sbuf([P, D_PASSES, K_PASS], U16, name, tag)
-            nc.vector.tensor_copy(out=codes[:], in_=got[:].bitcast(U16).rearrange("p (j o) -> p o j", o=D_PASSES))
+            nc.vector.tensor_copy(out=codes[:].rearrange("p o (t c i) -> p o c t i", t=PACK, i=4),
+                                  in_=got[:].bitcast(U16).rearrange("p (c i t o) -> p o c t i", t=PACK, i=4, o=D_PASSES))
             return codes
-
-        half_kb = sbuf([P, SLOT_PASSES, PACK], F32, "half_kb")
-        nc.scalar.activation(out=half_kb[:], in_=kb_cols[:, :, 0:PACK], func=ACT.Copy, scale=0.5)
 
         kw_got = [gather_words(g) for g in range(SLOT_PASSES)]
         k_codes = [part_words(kw_got[0], "k_codes0")]
         q_mx = [quantised(q_bf[o][:].rearrange("p q t -> p (q t)"), NQ, "q%d" % o) for o in range(D_PASSES)]
         k_codes.append(part_words(kw_got[1], "k_codes1", "q_bf1"))
-        vs_got.append(sbuf([P, K_PASS], F32, "vs_got1", "kw_got1"))
-        nc.vector.tensor_copy(out=vs_got[1][:], in_=vs_pool[:].indirect(listed(1)))
-        lay_out(vs_cols, 1, vs_got[1][LAST:P, :])
+        lay_out(vs_cols, 1, gather_vs(1, "kw_got1")[LAST:P, :])
+        ident = sbuf([P, P], F32, "ident", "vs_pool")
+        make_identity(nc, ident[:])
 
-        low_got = tiles(SLOT_PASSES, [P, K_PASS], BF16, "low_got")
+        low_got = sbuf([P, N], BF16, "low_got")
         high_got = tiles(SLOT_PASSES, [P, K_PASS], BF16, "high_got")
-        for g in range(SLOT_PASSES):
-            nc.vector.tensor_copy(out=low_got[g][:].rearrange("p (u m e) -> p m u e", u=2, e=2),
-                                  in_=v_low[:, 0:(HEAD, T)[g]].indirect(listed(g)))
-        for g in range(SLOT_PASSES):
-            nc.vector.tensor_copy(out=high_got[g][:], in_=v_high[:].indirect(listed(g)))
+        nc.vector.tensor_copy(out=low_got[:], in_=v_pool[0][:].indirect(offsets[:]))
 
         def capped_scores(g):
+            half_kb = sbuf([P, PACK], F32, "half_kb%d" % g)
+            nc.scalar.activation(out=half_kb[:], in_=kb_cols[:, g, 0:PACK], func=ACT.Copy, scale=0.5)
             capped = sbuf([P, PACK, NQ], F32, "capped%d" % g)
             for t in range(PACK):
                 score = bank(g * PACK + t, [P, NQ], F32, "score")
@@ -167,11 +161,11 @@ def tile_attend_sigm_cap_kb_srtq256n1024t2048_kernel(tc, qT, k_words, k_scales, 
                     nc.tensor.matmul_mx(
                         out=score[:],
                         lhsT=k_codes[g][:, o, t * P:(t + 1) * P].bitcast(FP4X4),
-                        lhsT_scale=k_planes[:, o, (g * PACK + t) * P:(g * PACK + t + 1) * P],
+                        lhsT_scale=k_planes[:, o, (t * SLOT_PASSES + g) * P:(t * SLOT_PASSES + g + 1) * P],
                         rhs=q_mx[o][0][:].bitcast(FP8X4), rhs_scale=q_mx[o][1][:],
                         start=(step == 0), stop=(step == D_PASSES - 1))
                 nc.scalar.activation(out=capped[:, t, :], in_=score[:], func=ACT.Tanh,
-                                     bias=half_kb[:, g, t:t + 1], scale=0.5)
+                                     bias=half_kb[:, t:t + 1], scale=0.5)
             return capped
 
         def sigmoid(capped, first, width, p):
@@ -180,36 +174,36 @@ def tile_attend_sigm_cap_kb_srtq256n1024t2048_kernel(tc, qT, k_words, k_scales, 
                                  func=ACT.Sigmoid, scale=2.0)
             return p
 
-        def weights(p, g, width, name):
-            w = sbuf([P, width, PACK], BF16, name)
+        def weights(p, g, width, name, tag=None):
+            w = sbuf([P, width, PACK], BF16, name, tag)
             nc.vector.tensor_tensor(out=w[:], in0=p[:], in1=vs_cols[:, g, 0:PACK].unsqueeze(1).to_broadcast([P, width, PACK]),
                                     op=ALU.mult)
             return w[:].rearrange("p q t -> p (q t)")
 
         def turned_values(g):
             turned = bank(g, [P, V_TILES, 2, P], F32, "v_turned")
-            for u in range(2):
-                nc.tensor.transpose(turned[:, 0, u, :], low_got[g][:].bitcast(F32)[:, u * P:(u + 1) * P], ident[:])
-            for u in range(2):
-                nc.tensor.transpose(turned[:, 1, u, :], high_got[g][:].bitcast(F32)[:, u:2 * P:2], ident[:])
+            for h, got in enumerate((low_got[:, g * K_PASS:(g + 1) * K_PASS], high_got[g][:])):
+                for u in range(2):
+                    nc.tensor.transpose(turned[:, h, u, :], got.bitcast(F32)[:, u:2 * P:2], ident[:])
             woven = sbuf([P, V_TILES, P, 2], F32, "v_woven%d" % g)
             nc.scalar.copy(out=woven[:], in_=turned[:].rearrange("p h u e -> p h e u"))
             return woven[:].rearrange("p h e u -> p (h e u)").bitcast(BF16)
 
         capped0 = capped_scores(0)
         p0 = sigmoid(capped0, 0, NQ, sbuf([P, NQ, PACK], F32, "p0"))
+        w0 = weights(p0, 0, NQ, "w0", "v_pool0")
+        for g in range(SLOT_PASSES):
+            nc.vector.tensor_copy(out=high_got[g][:], in_=v_pool[1][:].indirect(listed(g)))
         capped1 = capped_scores(1)
-        v_woven = [turned_values(0)]
         p1 = [sigmoid(capped1, qh * P, P, sbuf([P, P, PACK], F32, "p1_%d" % qh)) for qh in range(Q_TILES)]
-        v_woven.append(turned_values(1))
+        v_woven = [turned_values(g) for g in range(SLOT_PASSES)]
 
-        w0 = weights(p0, 0, NQ, "w0")
+        w0_mx = quantised(w0, NQ, "w0", "v_pool1")
         w1 = [weights(p1[0], 1, P, "w1_0")]
-        w0_mx = quantised(w0, NQ, "w0")
-        v_mx = [quantised(v_woven[0], DV, "v0", "p1_0")]
-        w1.append(weights(p1[1], 1, P, "w1_1"))
-        v_mx.append(quantised(v_woven[1], DV, "v1", "p1_1"))
-        w1_mx = [quantised(w1[qh], P, "w1_%d" % qh) for qh in range(Q_TILES)]
+        v_mx = [quantised(v_woven[0], DV, "v0")]
+        w1.append(weights(p1[1], 1, P, "w1_1", "v_woven0"))
+        v_mx.append(quantised(v_woven[1], DV, "v1"))
+        w1_mx = [quantised(w1[0], P, "w1_0", "v_woven1"), quantised(w1[1], P, "w1_1")]
 
         for qh in range(Q_TILES):
             cols = slice(qh * P, (qh + 1) * P)

@@ -26,6 +26,7 @@ LIST_COLS = K_PASS // 16
 LAST = P - 1
 SCALE_ROWS = 16 * D_PASSES
 SCALE_BASE = P - SCALE_ROWS
+HEAD = T - N + K_PASS
 
 FLOPS = 2 * NQ * N * (D + DV)
 BYTES = 4 * D * NQ + 4 * P * T + 32 * T + 4 * DV * T + 2 * 4 * T + 2 * P * N // 16 + 4 * NQ * DV
@@ -79,15 +80,13 @@ def tile_attend_sigm_cap_kb_srtq256n1024t2048_kernel(tc, qT, k_words, k_scales, 
                           in_=k_scales.rearrange("o f t -> f o t").bitcast(I32))
         nc.sync.dma_start(out=kb_pool[LAST:P, :], in_=kb[LAST:P, :])
         nc.sync.dma_start(out=vs_pool[LAST:P, :], in_=vs[LAST:P, :])
-        nc.sync.dma_start(out=kw_pool[:], in_=words)
+        nc.sync.dma_start(out=kw_pool[:, 0:HEAD], in_=words[:, 0:HEAD])
         load_queries(0)
         load_queries(1)
+        nc.sync.dma_start(out=kw_pool[:, HEAD:T], in_=words[:, HEAD:T])
 
         ks_got = sbuf([P, N], U8, "ks_got")
-        ks_dealt = sbuf([P, N], U8, "ks_dealt")
-        nc.vector.tensor_copy(out=ks_got[:], in_=ks_pool[:].indirect(offsets[:]))
-        nc.vector.tensor_copy(out=ks_dealt[:].rearrange("p (t c i) -> p c t i", t=PACK, i=4),
-                              in_=ks_got[:].rearrange("p (c i t) -> p c t i", t=PACK, i=4))
+        nc.vector.tensor_copy(out=ks_got[:].rearrange("p (t m) -> p m t", t=PACK), in_=ks_pool[:].indirect(offsets[:]))
 
         def lay_out(cols, g, row):
             nc.sync.dma_start(out=cols[:, g, 0:PACK], in_=row)
@@ -96,30 +95,26 @@ def tile_attend_sigm_cap_kb_srtq256n1024t2048_kernel(tc, qT, k_words, k_scales, 
             nc.scalar.copy(out=woven.rearrange("p (c i) t -> p c t i", i=4),
                            in_=planes.rearrange("p t (c i) -> p c t i", i=4))
 
-        def gather_vs(g, tag=None):
-            got = sbuf([P, K_PASS], F32, "vs_got%d" % g, tag)
-            nc.vector.tensor_copy(out=got[:], in_=vs_pool[:].indirect(listed(g)))
-            return got
-
         kb_got = sbuf([P, N], F32, "kb_got")
         nc.scalar.activation(out=kb_got[:], in_=kb_pool[:].indirect(offsets[:]), func=ACT.Copy)
-        vs_first = gather_vs(0)
         q_bf = tiles(D_PASSES, [P, NQ, PACK], BF16, "q_bf")
         for o in range(D_PASSES):
             weave(q_bf[o][:], q_raw[o][:])
+        vs_got = [sbuf([P, K_PASS], F32, "vs_got0", "q_raw1")]
+        nc.scalar.activation(out=vs_got[0][:], in_=vs_pool[:].indirect(listed(0)), func=ACT.Copy)
         rows_a_quad = SCALE_ROWS // 4
         for quad in range(4):
             first = SCALE_BASE + quad * rows_a_quad
             nc.sync.dma_start(out=k_planes[32 * quad:32 * quad + 4, :, :].bitcast(I32),
-                              in_=ks_dealt[first:first + rows_a_quad, :].bitcast(I32))
+                              in_=ks_got[first:first + rows_a_quad, :].bitcast(I32))
         kb_cols = sbuf([P, SLOT_PASSES, 2 * PACK], F32, "kb_cols")
         vs_cols = sbuf([P, SLOT_PASSES, 2 * PACK], F32, "vs_cols")
         v_pool = tiles(V_TILES, [P, T], F32, "v_pool")
         lay_out(kb_cols, 0, kb_got[LAST:P, 0:K_PASS])
-        lay_out(vs_cols, 0, vs_first[LAST:P, :])
         nc.sync.dma_start(out=v_pool[0][:], in_=vT[0:P, :])
         lay_out(kb_cols, 1, kb_got[LAST:P, K_PASS:N])
         nc.sync.dma_start(out=v_pool[1][:], in_=vT[P:2 * P, :])
+        lay_out(vs_cols, 0, vs_got[0][LAST:P, :])
 
         def quantised(source, width, name, tag=None):
             codes = sbuf([P, width], U32, name + "_codes", tag)
@@ -129,7 +124,7 @@ def tile_attend_sigm_cap_kb_srtq256n1024t2048_kernel(tc, qT, k_words, k_scales, 
 
         def gather_words(g):
             got = sbuf([P, K_PASS], U32, "kw_got%d" % g)
-            nc.vector.tensor_copy(out=got[:], in_=kw_pool[:].bitcast(U32).indirect(listed(g)))
+            nc.vector.tensor_copy(out=got[:], in_=kw_pool[:, 0:(HEAD, T)[g]].bitcast(U32).indirect(listed(g)))
             return got
 
         def part_words(got, name, tag=None):
@@ -138,17 +133,22 @@ def tile_attend_sigm_cap_kb_srtq256n1024t2048_kernel(tc, qT, k_words, k_scales, 
                                   in_=got[:].bitcast(U16).rearrange("p (c i t o) -> p o c t i", t=PACK, i=4, o=D_PASSES))
             return codes
 
-        kw_got = [gather_words(g) for g in range(SLOT_PASSES)]
-        k_codes = [part_words(kw_got[0], "k_codes0")]
-        q_mx = [quantised(q_bf[o][:].rearrange("p q t -> p (q t)"), NQ, "q%d" % o) for o in range(D_PASSES)]
-        k_codes.append(part_words(kw_got[1], "k_codes1", "q_bf1"))
-        lay_out(vs_cols, 1, gather_vs(1, "kw_got1")[LAST:P, :])
+        k_codes = [part_words(gather_words(0), "k_codes0")]
+        q_mx = [quantised(q_bf[0][:].rearrange("p q t -> p (q t)"), NQ, "q0")]
+        last_words = gather_words(1)
+        q_mx.append(quantised(q_bf[1][:].rearrange("p q t -> p (q t)"), NQ, "q1"))
+        k_codes.append(part_words(last_words, "k_codes1", "q_bf1"))
+        vs_got.append(sbuf([P, K_PASS], F32, "vs_got1", "kw_got1"))
+        nc.vector.tensor_copy(out=vs_got[1][:], in_=vs_pool[:].indirect(listed(1)))
+        lay_out(vs_cols, 1, vs_got[1][LAST:P, :])
         ident = sbuf([P, P], F32, "ident", "vs_pool")
         make_identity(nc, ident[:])
 
         low_got = sbuf([P, N], BF16, "low_got")
         high_got = tiles(SLOT_PASSES, [P, K_PASS], BF16, "high_got")
         nc.vector.tensor_copy(out=low_got[:], in_=v_pool[0][:].indirect(offsets[:]))
+        for g in range(SLOT_PASSES):
+            nc.vector.tensor_copy(out=high_got[g][:], in_=v_pool[1][:].indirect(listed(g)))
 
         def capped_scores(g):
             half_kb = sbuf([P, PACK], F32, "half_kb%d" % g)
@@ -191,15 +191,15 @@ def tile_attend_sigm_cap_kb_srtq256n1024t2048_kernel(tc, qT, k_words, k_scales, 
 
         capped0 = capped_scores(0)
         p0 = sigmoid(capped0, 0, NQ, sbuf([P, NQ, PACK], F32, "p0"))
-        w0 = weights(p0, 0, NQ, "w0", "v_pool0")
-        for g in range(SLOT_PASSES):
-            nc.vector.tensor_copy(out=high_got[g][:], in_=v_pool[1][:].indirect(listed(g)))
         capped1 = capped_scores(1)
-        p1 = [sigmoid(capped1, qh * P, P, sbuf([P, P, PACK], F32, "p1_%d" % qh)) for qh in range(Q_TILES)]
-        v_woven = [turned_values(g) for g in range(SLOT_PASSES)]
+        p1 = [sigmoid(capped1, 0, P, sbuf([P, P, PACK], F32, "p1_0"))]
+        v_woven = [turned_values(0)]
+        p1.append(sigmoid(capped1, P, P, sbuf([P, P, PACK], F32, "p1_1", "high_got0")))
+        v_woven.append(turned_values(1))
 
-        w0_mx = quantised(w0, NQ, "w0", "v_pool1")
+        w0 = weights(p0, 0, NQ, "w0")
         w1 = [weights(p1[0], 1, P, "w1_0")]
+        w0_mx = quantised(w0, NQ, "w0")
         v_mx = [quantised(v_woven[0], DV, "v0")]
         w1.append(weights(p1[1], 1, P, "w1_1", "v_woven0"))
         v_mx.append(quantised(v_woven[1], DV, "v1"))

@@ -36,6 +36,7 @@ def tile_attend_sigm_cap_kb_srtq256n1024t2048_kernel(tc, qT, k_words, k_scales, 
     nc = tc.nc
     with ExitStack() as ctx:
         sb = ctx.enter_context(tc.tile_pool(name="sb", bufs=1))
+        shared = ctx.enter_context(tc.tile_pool(name="shared", bufs=1))
         ps = ctx.enter_context(tc.psum_pool(name="ps", bufs=1))
 
         def sbuf(shape, dtype, name, tag=None):
@@ -43,6 +44,9 @@ def tile_attend_sigm_cap_kb_srtq256n1024t2048_kernel(tc, qT, k_words, k_scales, 
 
         def tiles(count, shape, dtype, name):
             return [sbuf(shape, dtype, "%s%d" % (name, i)) for i in range(count)]
+
+        def placed(shape, dtype, name, offset):
+            return shared.tile(shape, dtype, name=name, align_bytes=64, offset=offset)
 
         def bank(index, shape, dtype, name):
             return ps.tile(shape, dtype, name=name, tag="bank%d" % index)
@@ -58,18 +62,18 @@ def tile_attend_sigm_cap_kb_srtq256n1024t2048_kernel(tc, qT, k_words, k_scales, 
         kw_pool = sbuf([P, T], I32, "kw_pool")
         k_planes = sbuf([P, D_PASSES, N], U8, "k_planes")
 
-        vs_pool = sbuf([P, T], F32, "vs_pool")
 
         warm_in = sbuf([P, 1], F32, "warm_in")
         warm_out = sbuf([P, 1], F32, "warm_out")
         nc.gpsimd.memset(warm_in[:], 0.0)
         nc.scalar.activation(out=warm_out[:], in_=warm_in[:], func=ACT.Sigmoid)
+        ident = sbuf([P, P], F32, "ident")
+        make_identity(nc, ident[:])
         nc.gpsimd.memset(k_planes[:].rearrange("p o n -> p (o n)").bitcast(I32), 0)
         nc.vector.memset(ks_pool[0:SCALE_BASE, :].bitcast(I32), 0)
         nc.vector.memset(kb_pool[0:LAST, :].bitcast(I32), 0)
-        nc.vector.memset(vs_pool[0:LAST, :].bitcast(I32), 0)
 
-        q_raw = tiles(D_PASSES, [P, PACK, NQ], F32, "q_raw")
+        q_raw = [sbuf([P, PACK, NQ], F32, "q_raw0"), placed([P, PACK, NQ], F32, "q_raw1", 0)]
 
         def load_queries(o):
             rows = qT[0, o * K_PASS:(o + 1) * K_PASS, :]
@@ -79,7 +83,6 @@ def tile_attend_sigm_cap_kb_srtq256n1024t2048_kernel(tc, qT, k_words, k_scales, 
         nc.sync.dma_start(out=ks_pool[SCALE_BASE:P, :].bitcast(I32),
                           in_=k_scales.rearrange("o f t -> f o t").bitcast(I32))
         nc.sync.dma_start(out=kb_pool[LAST:P, :], in_=kb[LAST:P, :])
-        nc.sync.dma_start(out=vs_pool[LAST:P, :], in_=vs[LAST:P, :])
         nc.sync.dma_start(out=kw_pool[:, 0:HEAD], in_=words[:, 0:HEAD])
         load_queries(0)
         load_queries(1)
@@ -87,6 +90,9 @@ def tile_attend_sigm_cap_kb_srtq256n1024t2048_kernel(tc, qT, k_words, k_scales, 
 
         ks_got = sbuf([P, N], U8, "ks_got")
         nc.vector.tensor_copy(out=ks_got[:].rearrange("p (t m) -> p m t", t=PACK), in_=ks_pool[:].indirect(offsets[:]))
+        vs_pool = sbuf([P, T], F32, "vs_pool", "ks_pool")
+        nc.vector.memset(vs_pool[0:LAST, :].bitcast(I32), 0)
+        nc.sync.dma_start(out=vs_pool[LAST:P, :], in_=vs[LAST:P, :])
 
         def lay_out(cols, g, row):
             nc.sync.dma_start(out=cols[:, g, 0:PACK], in_=row)
@@ -100,19 +106,23 @@ def tile_attend_sigm_cap_kb_srtq256n1024t2048_kernel(tc, qT, k_words, k_scales, 
         q_bf = tiles(D_PASSES, [P, NQ, PACK], BF16, "q_bf")
         for o in range(D_PASSES):
             weave(q_bf[o][:], q_raw[o][:])
-        vs_got = [sbuf([P, K_PASS], F32, "vs_got0", "q_raw1")]
+        vs_got = [placed([P, K_PASS], F32, "vs_got0", 0)]
         nc.scalar.activation(out=vs_got[0][:], in_=vs_pool[:].indirect(listed(0)), func=ACT.Copy)
+        tiles_in_all = SLOT_PASSES * PACK
+        kb_turned = bank(7, [P, P + tiles_in_all - 1], F32, "kb_turned")
+        for j in reversed(range(tiles_in_all)):
+            g, t = divmod(j, PACK)
+            nc.tensor.transpose(kb_turned[:, j:j + P], kb_got[:, g * K_PASS + t:(g + 1) * K_PASS:PACK], ident[:])
+        half_kb = placed([P, tiles_in_all], F32, "half_kb", 4 * K_PASS)
+        nc.scalar.activation(out=half_kb[:], in_=kb_turned[:, LAST:LAST + tiles_in_all], func=ACT.Copy, scale=0.5)
         rows_a_quad = SCALE_ROWS // 4
         for quad in range(4):
             first = SCALE_BASE + quad * rows_a_quad
             nc.sync.dma_start(out=k_planes[32 * quad:32 * quad + 4, :, :].bitcast(I32),
                               in_=ks_got[first:first + rows_a_quad, :].bitcast(I32))
-        kb_cols = sbuf([P, SLOT_PASSES, 2 * PACK], F32, "kb_cols")
         vs_cols = sbuf([P, SLOT_PASSES, 2 * PACK], F32, "vs_cols")
         v_pool = tiles(V_TILES, [P, T], F32, "v_pool")
-        lay_out(kb_cols, 0, kb_got[LAST:P, 0:K_PASS])
         nc.sync.dma_start(out=v_pool[0][:], in_=vT[0:P, :])
-        lay_out(kb_cols, 1, kb_got[LAST:P, K_PASS:N])
         nc.sync.dma_start(out=v_pool[1][:], in_=vT[P:2 * P, :])
         lay_out(vs_cols, 0, vs_got[0][LAST:P, :])
 
@@ -141,8 +151,6 @@ def tile_attend_sigm_cap_kb_srtq256n1024t2048_kernel(tc, qT, k_words, k_scales, 
         vs_got.append(sbuf([P, K_PASS], F32, "vs_got1", "kw_got1"))
         nc.vector.tensor_copy(out=vs_got[1][:], in_=vs_pool[:].indirect(listed(1)))
         lay_out(vs_cols, 1, vs_got[1][LAST:P, :])
-        ident = sbuf([P, P], F32, "ident", "vs_pool")
-        make_identity(nc, ident[:])
 
         low_got = sbuf([P, N], BF16, "low_got")
         high_got = tiles(SLOT_PASSES, [P, K_PASS], BF16, "high_got")
@@ -151,8 +159,6 @@ def tile_attend_sigm_cap_kb_srtq256n1024t2048_kernel(tc, qT, k_words, k_scales, 
             nc.vector.tensor_copy(out=high_got[g][:], in_=v_pool[1][:].indirect(listed(g)))
 
         def capped_scores(g):
-            half_kb = sbuf([P, PACK], F32, "half_kb%d" % g)
-            nc.scalar.activation(out=half_kb[:], in_=kb_cols[:, g, 0:PACK], func=ACT.Copy, scale=0.5)
             capped = sbuf([P, PACK, NQ], F32, "capped%d" % g)
             for t in range(PACK):
                 score = bank(g * PACK + t, [P, NQ], F32, "score")
@@ -165,19 +171,18 @@ def tile_attend_sigm_cap_kb_srtq256n1024t2048_kernel(tc, qT, k_words, k_scales, 
                         rhs=q_mx[o][0][:].bitcast(FP8X4), rhs_scale=q_mx[o][1][:],
                         start=(step == 0), stop=(step == D_PASSES - 1))
                 nc.scalar.activation(out=capped[:, t, :], in_=score[:], func=ACT.Tanh,
-                                     bias=half_kb[:, t:t + 1], scale=0.5)
+                                     bias=half_kb[:, g * PACK + t:g * PACK + t + 1], scale=0.5)
             return capped
 
         def sigmoid(capped, first, width, p):
-            nc.scalar.activation(out=p[:].rearrange("p (c i) t -> p c t i", i=4),
-                                 in_=capped[:, :, first:first + width].rearrange("p t (c i) -> p c t i", i=4),
-                                 func=ACT.Sigmoid, scale=2.0)
+            nc.scalar.activation(out=p[:], in_=capped[:, :, first:first + width], func=ACT.Sigmoid, scale=2.0)
             return p
 
         def weights(p, g, width, name, tag=None):
             w = sbuf([P, width, PACK], BF16, name, tag)
-            nc.vector.tensor_tensor(out=w[:], in0=p[:], in1=vs_cols[:, g, 0:PACK].unsqueeze(1).to_broadcast([P, width, PACK]),
-                                    op=ALU.mult)
+            scales = vs_cols[:, g, 0:PACK].unsqueeze(1).unsqueeze(3).to_broadcast([P, width // 4, PACK, 4])
+            nc.vector.tensor_tensor(out=w[:].rearrange("p (c i) t -> p c t i", i=4),
+                                    in0=p[:].rearrange("p t (c i) -> p c t i", i=4), in1=scales, op=ALU.mult)
             return w[:].rearrange("p q t -> p (q t)")
 
         def turned_values(g):
@@ -190,11 +195,11 @@ def tile_attend_sigm_cap_kb_srtq256n1024t2048_kernel(tc, qT, k_words, k_scales, 
             return woven[:].rearrange("p h e u -> p (h e u)").bitcast(BF16)
 
         capped0 = capped_scores(0)
-        p0 = sigmoid(capped0, 0, NQ, sbuf([P, NQ, PACK], F32, "p0"))
+        p0 = sigmoid(capped0, 0, NQ, sbuf([P, PACK, NQ], F32, "p0"))
         capped1 = capped_scores(1)
-        p1 = [sigmoid(capped1, 0, P, sbuf([P, P, PACK], F32, "p1_0"))]
+        p1 = [sigmoid(capped1, 0, P, sbuf([P, PACK, P], F32, "p1_0"))]
         v_woven = [turned_values(0)]
-        p1.append(sigmoid(capped1, P, P, sbuf([P, P, PACK], F32, "p1_1", "high_got0")))
+        p1.append(sigmoid(capped1, P, P, sbuf([P, PACK, P], F32, "p1_1", "high_got0")))
         v_woven.append(turned_values(1))
 
         w0 = weights(p0, 0, NQ, "w0")

@@ -70,8 +70,10 @@ def tile_attend_sigm_cap_kb_srtq256n1024t2048_kernel(tc, qT, k_words, k_scales, 
         ident = sbuf([P, P], F32, "ident")
         make_identity(nc, ident[:])
         nc.gpsimd.memset(k_planes[:].rearrange("p o n -> p (o n)").bitcast(I32), 0)
-        nc.vector.memset(ks_pool[0:SCALE_BASE, :].bitcast(I32), 0)
+        vs_pool = sbuf([P, T], F32, "vs_pool")
         nc.vector.memset(kb_pool[0:LAST, :].bitcast(I32), 0)
+        nc.vector.memset(ks_pool[0:SCALE_BASE, :].bitcast(I32), 0)
+        nc.vector.memset(vs_pool[0:LAST, :].bitcast(I32), 0)
 
         q_raw = [sbuf([P, PACK, NQ], F32, "q_raw0"), placed([P, PACK, NQ], F32, "q_raw1", 0)]
 
@@ -80,9 +82,10 @@ def tile_attend_sigm_cap_kb_srtq256n1024t2048_kernel(tc, qT, k_words, k_scales, 
             nc.sync.dma_start(out=q_raw[o][:], in_=rows.rearrange("(p t) q -> p t q", t=PACK))
 
         words = k_words[0].rearrange("p t b -> p (t b)").bitcast(I32)
+        nc.sync.dma_start(out=kb_pool[LAST:P, :], in_=kb[LAST:P, :])
+        nc.sync.dma_start(out=vs_pool[LAST:P, :], in_=vs[LAST:P, :])
         nc.sync.dma_start(out=ks_pool[SCALE_BASE:P, :].bitcast(I32),
                           in_=k_scales.rearrange("o f t -> f o t").bitcast(I32))
-        nc.sync.dma_start(out=kb_pool[LAST:P, :], in_=kb[LAST:P, :])
         nc.sync.dma_start(out=kw_pool[:, 0:HEAD], in_=words[:, 0:HEAD])
         load_queries(0)
         load_queries(1)
@@ -90,9 +93,6 @@ def tile_attend_sigm_cap_kb_srtq256n1024t2048_kernel(tc, qT, k_words, k_scales, 
 
         ks_got = sbuf([P, N], U8, "ks_got")
         nc.vector.tensor_copy(out=ks_got[:].rearrange("p (t m) -> p m t", t=PACK), in_=ks_pool[:].indirect(offsets[:]))
-        vs_pool = sbuf([P, T], F32, "vs_pool", "ks_pool")
-        nc.vector.memset(vs_pool[0:LAST, :].bitcast(I32), 0)
-        nc.sync.dma_start(out=vs_pool[LAST:P, :], in_=vs[LAST:P, :])
 
         def lay_out(cols, g, row):
             nc.sync.dma_start(out=cols[:, g, 0:PACK], in_=row)
@@ -103,11 +103,13 @@ def tile_attend_sigm_cap_kb_srtq256n1024t2048_kernel(tc, qT, k_words, k_scales, 
 
         kb_got = sbuf([P, N], F32, "kb_got")
         nc.scalar.activation(out=kb_got[:], in_=kb_pool[:].indirect(offsets[:]), func=ACT.Copy)
+        vs_got = [sbuf([P, K_PASS], F32, "vs_got0")]
+        nc.scalar.activation(out=vs_got[0][:], in_=vs_pool[:].indirect(listed(0)), func=ACT.Copy)
         q_bf = tiles(D_PASSES, [P, NQ, PACK], BF16, "q_bf")
         for o in range(D_PASSES):
             weave(q_bf[o][:], q_raw[o][:])
-        vs_got = [placed([P, K_PASS], F32, "vs_got0", 0)]
-        nc.scalar.activation(out=vs_got[0][:], in_=vs_pool[:].indirect(listed(0)), func=ACT.Copy)
+        vs_got.append(placed([P, K_PASS], F32, "vs_got1", 0))
+        nc.scalar.activation(out=vs_got[1][:], in_=vs_pool[:].indirect(listed(1)), func=ACT.Copy)
         tiles_in_all = SLOT_PASSES * PACK
         kb_turned = bank(7, [P, P + tiles_in_all - 1], F32, "kb_turned")
         for j in reversed(range(tiles_in_all)):
@@ -122,9 +124,11 @@ def tile_attend_sigm_cap_kb_srtq256n1024t2048_kernel(tc, qT, k_words, k_scales, 
                               in_=ks_got[first:first + rows_a_quad, :].bitcast(I32))
         vs_cols = sbuf([P, SLOT_PASSES, 2 * PACK], F32, "vs_cols")
         v_pool = tiles(V_TILES, [P, T], F32, "v_pool")
-        nc.sync.dma_start(out=v_pool[0][:], in_=vT[0:P, :])
-        nc.sync.dma_start(out=v_pool[1][:], in_=vT[P:2 * P, :])
-        lay_out(vs_cols, 0, vs_got[0][LAST:P, :])
+        for h in range(V_TILES):
+            for cols in (slice(0, HEAD), slice(HEAD, T)):
+                nc.sync.dma_start(out=v_pool[h][:, cols], in_=vT[h * P:(h + 1) * P, cols])
+        for g in range(SLOT_PASSES):
+            lay_out(vs_cols, g, vs_got[g][LAST:P, :])
 
         def quantised(source, width, name, tag=None):
             codes = sbuf([P, width], U32, name + "_codes", tag)
@@ -148,30 +152,33 @@ def tile_attend_sigm_cap_kb_srtq256n1024t2048_kernel(tc, qT, k_words, k_scales, 
         last_words = gather_words(1)
         q_mx.append(quantised(q_bf[1][:].rearrange("p q t -> p (q t)"), NQ, "q1"))
         k_codes.append(part_words(last_words, "k_codes1", "q_bf1"))
-        vs_got.append(sbuf([P, K_PASS], F32, "vs_got1", "kw_got1"))
-        nc.vector.tensor_copy(out=vs_got[1][:], in_=vs_pool[:].indirect(listed(1)))
-        lay_out(vs_cols, 1, vs_got[1][LAST:P, :])
 
-        low_got = sbuf([P, N], BF16, "low_got")
-        high_got = tiles(SLOT_PASSES, [P, K_PASS], BF16, "high_got")
-        nc.vector.tensor_copy(out=low_got[:], in_=v_pool[0][:].indirect(offsets[:]))
-        for g in range(SLOT_PASSES):
-            nc.vector.tensor_copy(out=high_got[g][:], in_=v_pool[1][:].indirect(listed(g)))
+        first_got = tiles(V_TILES, [P, 2, P, 2], BF16, "first_got")
+        last_got = tiles(V_TILES, [P, K_PASS], BF16, "last_got")
+        for h in range(V_TILES):
+            nc.vector.tensor_copy(out=first_got[h][:].rearrange("p u m e -> p m u e"),
+                                  in_=v_pool[h][:, 0:HEAD].indirect(listed(0)))
+            nc.vector.tensor_copy(out=last_got[h][:], in_=v_pool[h][:].indirect(listed(1)))
+
+        def value_pairs(g, h, u):
+            if g == 0:
+                return first_got[h][:, u, :, :].rearrange("p m e -> p (m e)").bitcast(F32)
+            return last_got[h][:].bitcast(F32)[:, u:2 * P:2]
 
         def capped_scores(g):
             capped = sbuf([P, PACK, NQ], F32, "capped%d" % g)
-            for t in range(PACK):
-                score = bank(g * PACK + t, [P, NQ], F32, "score")
-                order = (range(D_PASSES), reversed(range(D_PASSES)))[g]
-                for step, o in enumerate(order):
-                    nc.tensor.matmul_mx(
-                        out=score[:],
-                        lhsT=k_codes[g][:, o, t * P:(t + 1) * P].bitcast(FP4X4),
-                        lhsT_scale=k_planes[:, o, (t * SLOT_PASSES + g) * P:(t * SLOT_PASSES + g + 1) * P],
-                        rhs=q_mx[o][0][:].bitcast(FP8X4), rhs_scale=q_mx[o][1][:],
-                        start=(step == 0), stop=(step == D_PASSES - 1))
-                nc.scalar.activation(out=capped[:, t, :], in_=score[:], func=ACT.Tanh,
-                                     bias=half_kb[:, g * PACK + t:g * PACK + t + 1], scale=0.5)
+            scores = [bank(g * PACK + t, [P, NQ], F32, "score") for t in range(PACK)]
+            steps = [(t, o) for o in range(D_PASSES) for t in range(PACK)]
+            for t, o in (steps, sorted(steps))[g]:
+                nc.tensor.matmul_mx(
+                    out=scores[t][:],
+                    lhsT=k_codes[g][:, o, t * P:(t + 1) * P].bitcast(FP4X4),
+                    lhsT_scale=k_planes[:, o, (t * SLOT_PASSES + g) * P:(t * SLOT_PASSES + g + 1) * P],
+                    rhs=q_mx[o][0][:].bitcast(FP8X4), rhs_scale=q_mx[o][1][:],
+                    start=(o == 0), stop=(o == D_PASSES - 1))
+                if o == D_PASSES - 1:
+                    nc.scalar.activation(out=capped[:, t, :], in_=scores[t][:], func=ACT.Tanh,
+                                         bias=half_kb[:, g * PACK + t:g * PACK + t + 1], scale=0.5)
             return capped
 
         def sigmoid(capped, first, width, p):
@@ -187,9 +194,9 @@ def tile_attend_sigm_cap_kb_srtq256n1024t2048_kernel(tc, qT, k_words, k_scales, 
 
         def turned_values(g):
             turned = bank(g, [P, V_TILES, 2, P], F32, "v_turned")
-            for h, got in enumerate((low_got[:, g * K_PASS:(g + 1) * K_PASS], high_got[g][:])):
+            for h in range(V_TILES):
                 for u in range(2):
-                    nc.tensor.transpose(turned[:, h, u, :], got.bitcast(F32)[:, u:2 * P:2], ident[:])
+                    nc.tensor.transpose(turned[:, h, u, :], value_pairs(g, h, u), ident[:])
             woven = sbuf([P, V_TILES, P, 2], F32, "v_woven%d" % g)
             nc.scalar.copy(out=woven[:], in_=turned[:].rearrange("p h u e -> p h e u"))
             return woven[:].rearrange("p h e u -> p (h e u)").bitcast(BF16)
@@ -199,7 +206,7 @@ def tile_attend_sigm_cap_kb_srtq256n1024t2048_kernel(tc, qT, k_words, k_scales, 
         capped1 = capped_scores(1)
         p1 = [sigmoid(capped1, 0, P, sbuf([P, PACK, P], F32, "p1_0"))]
         v_woven = [turned_values(0)]
-        p1.append(sigmoid(capped1, P, P, sbuf([P, PACK, P], F32, "p1_1", "high_got0")))
+        p1.append(sigmoid(capped1, P, P, sbuf([P, PACK, P], F32, "p1_1", "first_got1")))
         v_woven.append(turned_values(1))
 
         w0 = weights(p0, 0, NQ, "w0")

@@ -101,8 +101,9 @@ def tile_attend_sigm_cap_kb_srtq256n1024t2048_kernel(tc, qT, k_words, k_scales, 
             nc.scalar.copy(out=woven.rearrange("p (c i) t -> p c t i", i=4),
                            in_=planes.rearrange("p t (c i) -> p c t i", i=4))
 
-        kb_got = sbuf([P, N], F32, "kb_got")
-        nc.scalar.activation(out=kb_got[:], in_=kb_pool[:].indirect(offsets[:]), func=ACT.Copy)
+        kb_got = tiles(SLOT_PASSES, [P, K_PASS], F32, "kb_got")
+        for g in range(SLOT_PASSES):
+            nc.scalar.activation(out=kb_got[g][:], in_=kb_pool[:].indirect(listed(g)), func=ACT.Copy)
         vs_got = [sbuf([P, K_PASS], F32, "vs_got0")]
         nc.scalar.activation(out=vs_got[0][:], in_=vs_pool[:].indirect(listed(0)), func=ACT.Copy)
         q_bf = tiles(D_PASSES, [P, NQ, PACK], BF16, "q_bf")
@@ -110,18 +111,18 @@ def tile_attend_sigm_cap_kb_srtq256n1024t2048_kernel(tc, qT, k_words, k_scales, 
             weave(q_bf[o][:], q_raw[o][:])
         vs_got.append(placed([P, K_PASS], F32, "vs_got1", 0))
         nc.scalar.activation(out=vs_got[1][:], in_=vs_pool[:].indirect(listed(1)), func=ACT.Copy)
-        tiles_in_all = SLOT_PASSES * PACK
-        kb_turned = bank(7, [P, P + tiles_in_all - 1], F32, "kb_turned")
-        for j in reversed(range(tiles_in_all)):
-            g, t = divmod(j, PACK)
-            nc.tensor.transpose(kb_turned[:, j:j + P], kb_got[:, g * K_PASS + t:(g + 1) * K_PASS:PACK], ident[:])
-        half_kb = placed([P, tiles_in_all], F32, "half_kb", 4 * K_PASS)
-        nc.scalar.activation(out=half_kb[:], in_=kb_turned[:, LAST:LAST + tiles_in_all], func=ACT.Copy, scale=0.5)
+        kb_turned = bank(7, [P, P + PACK - 1], F32, "kb_turned")
+        for t in reversed(range(PACK)):
+            nc.tensor.transpose(kb_turned[:, t:t + P], kb_got[0][:, t:K_PASS:PACK], ident[:])
+        half_kb = [placed([P, PACK], F32, "half_kb0", 4 * K_PASS), sbuf([P, PACK], F32, "half_kb1")]
+        nc.scalar.activation(out=half_kb[0][:], in_=kb_turned[:, LAST:LAST + PACK], func=ACT.Copy, scale=0.5)
         rows_a_quad = SCALE_ROWS // 4
         for quad in range(4):
             first = SCALE_BASE + quad * rows_a_quad
             nc.sync.dma_start(out=k_planes[32 * quad:32 * quad + 4, :, :].bitcast(I32),
                               in_=ks_got[first:first + rows_a_quad, :].bitcast(I32))
+        kb_cols = sbuf([P, PACK], F32, "kb_cols")
+        nc.sync.dma_start(out=kb_cols[:], in_=kb_got[1][LAST:P, :])
         vs_cols = sbuf([P, SLOT_PASSES, 2 * PACK], F32, "vs_cols")
         v_pool = tiles(V_TILES, [P, T], F32, "v_pool")
         for h in range(V_TILES):
@@ -152,6 +153,7 @@ def tile_attend_sigm_cap_kb_srtq256n1024t2048_kernel(tc, qT, k_words, k_scales, 
         last_words = gather_words(1)
         q_mx.append(quantised(q_bf[1][:].rearrange("p q t -> p (q t)"), NQ, "q1"))
         k_codes.append(part_words(last_words, "k_codes1", "q_bf1"))
+        nc.vector.tensor_scalar(out=half_kb[1][:], in0=kb_cols[:], scalar1=0.5, scalar2=None, op0=ALU.mult)
 
         first_got = tiles(V_TILES, [P, 2, P, 2], BF16, "first_got")
         last_got = tiles(V_TILES, [P, K_PASS], BF16, "last_got")
@@ -178,7 +180,7 @@ def tile_attend_sigm_cap_kb_srtq256n1024t2048_kernel(tc, qT, k_words, k_scales, 
                     start=(o == 0), stop=(o == D_PASSES - 1))
                 if o == D_PASSES - 1:
                     nc.scalar.activation(out=capped[:, t, :], in_=scores[t][:], func=ACT.Tanh,
-                                         bias=half_kb[:, g * PACK + t:g * PACK + t + 1], scale=0.5)
+                                         bias=half_kb[g][:, t:t + 1], scale=0.5)
             return capped
 
         def sigmoid(capped, first, width, p):

@@ -63,6 +63,9 @@ def tile_attend_sigm_cap_kb_srtq256n1024t2048_kernel(tc, qT, k_words, k_scales, 
         k_planes = sbuf([P, D_PASSES, N], U8, "k_planes")
 
 
+        vs_pool = sbuf([P, T], F32, "vs_pool")
+        nc.scalar.dma_start(out=kb_pool[LAST:P, :], in_=kb[LAST:P, :])
+        nc.scalar.dma_start(out=vs_pool[LAST:P, :], in_=vs[LAST:P, :])
         warm_in = sbuf([P, 1], F32, "warm_in")
         warm_out = sbuf([P, 1], F32, "warm_out")
         nc.gpsimd.memset(warm_in[:], 0.0)
@@ -70,7 +73,6 @@ def tile_attend_sigm_cap_kb_srtq256n1024t2048_kernel(tc, qT, k_words, k_scales, 
         ident = sbuf([P, P], F32, "ident")
         make_identity(nc, ident[:])
         nc.gpsimd.memset(k_planes[:].rearrange("p o n -> p (o n)").bitcast(I32), 0)
-        vs_pool = sbuf([P, T], F32, "vs_pool")
         nc.vector.memset(kb_pool[0:LAST, :].bitcast(I32), 0)
         nc.vector.memset(ks_pool[0:SCALE_BASE, :].bitcast(I32), 0)
         nc.vector.memset(vs_pool[0:LAST, :].bitcast(I32), 0)
@@ -82,8 +84,6 @@ def tile_attend_sigm_cap_kb_srtq256n1024t2048_kernel(tc, qT, k_words, k_scales, 
             nc.sync.dma_start(out=q_raw[o][:], in_=rows.rearrange("(p t) q -> p t q", t=PACK))
 
         words = k_words[0].rearrange("p t b -> p (t b)").bitcast(I32)
-        nc.sync.dma_start(out=kb_pool[LAST:P, :], in_=kb[LAST:P, :])
-        nc.sync.dma_start(out=vs_pool[LAST:P, :], in_=vs[LAST:P, :])
         nc.sync.dma_start(out=ks_pool[SCALE_BASE:P, :].bitcast(I32),
                           in_=k_scales.rearrange("o f t -> f o t").bitcast(I32))
         nc.sync.dma_start(out=kw_pool[:, 0:HEAD], in_=words[:, 0:HEAD])
@@ -138,7 +138,7 @@ def tile_attend_sigm_cap_kb_srtq256n1024t2048_kernel(tc, qT, k_words, k_scales, 
             return codes, plane
 
         def gather_words(g):
-            got = sbuf([P, K_PASS], U32, "kw_got%d" % g)
+            got = sbuf([P, K_PASS], U32, "kw_got%d" % g, ("kw_got0", "q_bf0")[g])
             nc.vector.tensor_copy(out=got[:], in_=kw_pool[:, 0:(HEAD, T)[g]].bitcast(U32).indirect(listed(g)))
             return got
 

@@ -27,6 +27,8 @@ LAST = P - 1
 SCALE_ROWS = 16 * D_PASSES
 SCALE_BASE = P - SCALE_ROWS
 HEAD = T - N + K_PASS
+HELD = 8192
+P_BYTES = 4 * PACK * P
 
 FLOPS = 2 * NQ * N * (D + DV)
 BYTES = 4 * D * NQ + 4 * P * T + 32 * T + 4 * DV * T + 2 * 4 * T + 2 * P * N // 16 + 4 * NQ * DV
@@ -155,7 +157,7 @@ def tile_attend_sigm_cap_kb_srtq256n1024t2048_kernel(tc, qT, k_words, k_scales, 
         k_codes.append(part_words(last_words, "k_codes1", "q_bf1"))
         nc.vector.tensor_scalar(out=half_kb[1][:], in0=kb_cols[:], scalar1=0.5, scalar2=None, op0=ALU.mult)
 
-        first_got = tiles(V_TILES, [P, 2, P, 2], BF16, "first_got")
+        first_got = [sbuf([P, 2, P, 2], BF16, "first_got0"), placed([P, 2, P, 2], BF16, "first_got1", HELD - K_PASS)]
         last_got = tiles(V_TILES, [P, K_PASS], BF16, "last_got")
         for h in range(V_TILES):
             nc.vector.tensor_copy(out=first_got[h][:].rearrange("p u m e -> p m u e"),
@@ -206,16 +208,15 @@ def tile_attend_sigm_cap_kb_srtq256n1024t2048_kernel(tc, qT, k_words, k_scales, 
         capped0 = capped_scores(0)
         p0 = sigmoid(capped0, 0, NQ, sbuf([P, PACK, NQ], F32, "p0"))
         capped1 = capped_scores(1)
-        p1 = [sigmoid(capped1, 0, P, sbuf([P, PACK, P], F32, "p1_0"))]
         v_woven = [turned_values(0)]
-        p1.append(sigmoid(capped1, P, P, sbuf([P, PACK, P], F32, "p1_1", "first_got1")))
+        p1 = [sigmoid(capped1, qh * P, P, placed([P, PACK, P], F32, "p1_%d" % qh, HELD + (qh - 1) * P_BYTES))
+              for qh in range(Q_TILES)]
         v_woven.append(turned_values(1))
 
         w0 = weights(p0, 0, NQ, "w0")
-        w1 = [weights(p1[0], 1, P, "w1_0")]
+        v_mx = [quantised(v_woven[0], DV, "v0", "p0")]
         w0_mx = quantised(w0, NQ, "w0")
-        v_mx = [quantised(v_woven[0], DV, "v0")]
-        w1.append(weights(p1[1], 1, P, "w1_1", "v_woven0"))
+        w1 = [weights(p1[0], 1, P, "w1_0", "v_woven0"), weights(p1[1], 1, P, "w1_1")]
         v_mx.append(quantised(v_woven[1], DV, "v1"))
         w1_mx = [quantised(w1[0], P, "w1_0", "v_woven1"), quantised(w1[1], P, "w1_1")]
 

@@ -103,6 +103,9 @@ def tile_attend_sigm_cap_kb_srtq256n1024t2048_kernel(tc, qT, k_words, k_scales, 
             nc.scalar.copy(out=woven.rearrange("p (c i) t -> p c t i", i=4),
                            in_=planes.rearrange("p t (c i) -> p c t i", i=4))
 
+        def bias_column(g, t):
+            return (SLOT_PASSES - 1 - g) * PACK + t
+
         kb_got = tiles(SLOT_PASSES, [P, K_PASS], F32, "kb_got")
         for g in range(SLOT_PASSES):
             nc.scalar.activation(out=kb_got[g][:], in_=kb_pool[:].indirect(listed(g)), func=ACT.Copy)
@@ -113,23 +116,24 @@ def tile_attend_sigm_cap_kb_srtq256n1024t2048_kernel(tc, qT, k_words, k_scales, 
             weave(q_bf[o][:], q_raw[o][:])
         vs_got.append(placed([P, K_PASS], F32, "vs_got1", 0))
         nc.scalar.activation(out=vs_got[1][:], in_=vs_pool[:].indirect(listed(1)), func=ACT.Copy)
-        kb_turned = bank(7, [P, P + PACK - 1], F32, "kb_turned")
-        for t in reversed(range(PACK)):
-            nc.tensor.transpose(kb_turned[:, t:t + P], kb_got[0][:, t:K_PASS:PACK], ident[:])
-        half_kb = [placed([P, PACK], F32, "half_kb0", 4 * K_PASS), sbuf([P, PACK], F32, "half_kb1")]
-        nc.scalar.activation(out=half_kb[0][:], in_=kb_turned[:, LAST:LAST + PACK], func=ACT.Copy, scale=0.5)
+        kb_turned = bank(7, [P, P + SLOT_PASSES * PACK - 1], F32, "kb_turned")
+
+        def turn_bias(g, place):
+            for t in reversed(range(PACK)):
+                j = bias_column(g, t)
+                nc.tensor.transpose(kb_turned[:, j:j + P], place(t), ident[:])
+
+        turn_bias(0, lambda t: kb_got[0][:, t:K_PASS:PACK])
         rows_a_quad = SCALE_ROWS // 4
         for quad in range(4):
             first = SCALE_BASE + quad * rows_a_quad
             nc.sync.dma_start(out=k_planes[32 * quad:32 * quad + 4, :, :].bitcast(I32),
                               in_=ks_got[first:first + rows_a_quad, :].bitcast(I32))
-        kb_cols = sbuf([P, PACK], F32, "kb_cols")
-        nc.sync.dma_start(out=kb_cols[:], in_=kb_got[1][LAST:P, :])
         vs_cols = sbuf([P, SLOT_PASSES, 2 * PACK], F32, "vs_cols")
         v_pool = tiles(V_TILES, [P, T], F32, "v_pool")
-        for h in range(V_TILES):
-            for cols in (slice(0, HEAD), slice(HEAD, T)):
-                nc.sync.dma_start(out=v_pool[h][:, cols], in_=vT[h * P:(h + 1) * P, cols])
+        nc.sync.dma_start(out=v_pool[0][:], in_=vT[0:P, :])
+        for cols in (slice(0, HEAD), slice(HEAD, T)):
+            nc.sync.dma_start(out=v_pool[1][:, cols], in_=vT[P:DV, cols])
         for g in range(SLOT_PASSES):
             lay_out(vs_cols, g, vs_got[g][LAST:P, :])
 
@@ -151,23 +155,30 @@ def tile_attend_sigm_cap_kb_srtq256n1024t2048_kernel(tc, qT, k_words, k_scales, 
             return codes
 
         k_codes = [part_words(gather_words(0), "k_codes0")]
+        kb_dealt = sbuf([P, PACK, P], F32, "kb_dealt", "kw_got0")
+        nc.vector.tensor_copy(out=kb_dealt[:].rearrange("p t m -> p m t"),
+                              in_=kb_got[1][:].rearrange("p (m t) -> p m t", t=PACK))
+        turn_bias(1, lambda t: kb_dealt[:, t, :])
+        half_kb = placed([P, SLOT_PASSES * PACK], F32, "half_kb", 4 * K_PASS)
+        nc.scalar.activation(out=half_kb[:], in_=kb_turned[:, LAST:LAST + SLOT_PASSES * PACK], func=ACT.Copy, scale=0.5)
         q_mx = [quantised(q_bf[0][:].rearrange("p q t -> p (q t)"), NQ, "q0")]
         last_words = gather_words(1)
         q_mx.append(quantised(q_bf[1][:].rearrange("p q t -> p (q t)"), NQ, "q1"))
         k_codes.append(part_words(last_words, "k_codes1", "q_bf1"))
-        nc.vector.tensor_scalar(out=half_kb[1][:], in0=kb_cols[:], scalar1=0.5, scalar2=None, op0=ALU.mult)
 
-        first_got = [sbuf([P, 2, P, 2], BF16, "first_got0"), placed([P, 2, P, 2], BF16, "first_got1", HELD - K_PASS)]
-        last_got = tiles(V_TILES, [P, K_PASS], BF16, "last_got")
-        for h in range(V_TILES):
-            nc.vector.tensor_copy(out=first_got[h][:].rearrange("p u m e -> p m u e"),
-                                  in_=v_pool[h][:, 0:HEAD].indirect(listed(0)))
-            nc.vector.tensor_copy(out=last_got[h][:], in_=v_pool[h][:].indirect(listed(1)))
+        low_got = sbuf([P, N], BF16, "low_got")
+        high_dealt = placed([P, 2, P, 2], BF16, "high_dealt", HELD - K_PASS)
+        high_got = sbuf([P, K_PASS], BF16, "high_got")
+        nc.vector.tensor_copy(out=low_got[:], in_=v_pool[0][:].indirect(offsets[:]))
+        nc.vector.tensor_copy(out=high_dealt[:].rearrange("p u m e -> p m u e"),
+                              in_=v_pool[1][:, 0:HEAD].indirect(listed(0)))
+        nc.vector.tensor_copy(out=high_got[:], in_=v_pool[1][:].indirect(listed(1)))
 
         def value_pairs(g, h, u):
-            if g == 0:
-                return first_got[h][:, u, :, :].rearrange("p m e -> p (m e)").bitcast(F32)
-            return last_got[h][:].bitcast(F32)[:, u:2 * P:2]
+            if (g, h) == (0, 1):
+                return high_dealt[:, u, :, :].rearrange("p m e -> p (m e)").bitcast(F32)
+            got = low_got[:, g * K_PASS:(g + 1) * K_PASS] if h == 0 else high_got[:]
+            return got.bitcast(F32)[:, u:2 * P:2]
 
         def capped_scores(g):
             capped = sbuf([P, PACK, NQ], F32, "capped%d" % g)
@@ -182,7 +193,7 @@ def tile_attend_sigm_cap_kb_srtq256n1024t2048_kernel(tc, qT, k_words, k_scales, 
                     start=(o == 0), stop=(o == D_PASSES - 1))
                 if o == D_PASSES - 1:
                     nc.scalar.activation(out=capped[:, t, :], in_=scores[t][:], func=ACT.Tanh,
-                                         bias=half_kb[g][:, t:t + 1], scale=0.5)
+                                         bias=half_kb[:, bias_column(g, t):bias_column(g, t) + 1], scale=0.5)
             return capped
 
         def sigmoid(capped, first, width, p):

@@ -131,9 +131,9 @@ def tile_attend_sigm_cap_kb_srtq256n1024t2048_kernel(tc, qT, k_words, k_scales, 
                               in_=ks_got[first:first + rows_a_quad, :].bitcast(I32))
         vs_cols = sbuf([P, SLOT_PASSES, 2 * PACK], F32, "vs_cols")
         v_pool = tiles(V_TILES, [P, T], F32, "v_pool")
-        nc.sync.dma_start(out=v_pool[0][:], in_=vT[0:P, :])
-        for cols in (slice(0, HEAD), slice(HEAD, T)):
-            nc.sync.dma_start(out=v_pool[1][:, cols], in_=vT[P:DV, cols])
+        for h in range(V_TILES):
+            for cols in (slice(0, HEAD), slice(HEAD, T)):
+                nc.sync.dma_start(out=v_pool[h][:, cols], in_=vT[h * P:(h + 1) * P, cols])
         for g in range(SLOT_PASSES):
             lay_out(vs_cols, g, vs_got[g][LAST:P, :])
 
@@ -166,19 +166,17 @@ def tile_attend_sigm_cap_kb_srtq256n1024t2048_kernel(tc, qT, k_words, k_scales, 
         q_mx.append(quantised(q_bf[1][:].rearrange("p q t -> p (q t)"), NQ, "q1"))
         k_codes.append(part_words(last_words, "k_codes1", "q_bf1"))
 
-        low_got = sbuf([P, N], BF16, "low_got")
-        high_dealt = placed([P, 2, P, 2], BF16, "high_dealt", HELD - K_PASS)
-        high_got = sbuf([P, K_PASS], BF16, "high_got")
-        nc.vector.tensor_copy(out=low_got[:], in_=v_pool[0][:].indirect(offsets[:]))
-        nc.vector.tensor_copy(out=high_dealt[:].rearrange("p u m e -> p m u e"),
-                              in_=v_pool[1][:, 0:HEAD].indirect(listed(0)))
-        nc.vector.tensor_copy(out=high_got[:], in_=v_pool[1][:].indirect(listed(1)))
+        first_got = [sbuf([P, 2, P, 2], BF16, "first_got0"), placed([P, 2, P, 2], BF16, "first_got1", HELD - K_PASS)]
+        last_got = tiles(V_TILES, [P, K_PASS], BF16, "last_got")
+        for h in range(V_TILES):
+            nc.vector.tensor_copy(out=first_got[h][:].rearrange("p u m e -> p m u e"),
+                                  in_=v_pool[h][:, 0:HEAD].indirect(listed(0)))
+            nc.vector.tensor_copy(out=last_got[h][:], in_=v_pool[h][:].indirect(listed(1)))
 
         def value_pairs(g, h, u):
-            if (g, h) == (0, 1):
-                return high_dealt[:, u, :, :].rearrange("p m e -> p (m e)").bitcast(F32)
-            got = low_got[:, g * K_PASS:(g + 1) * K_PASS] if h == 0 else high_got[:]
-            return got.bitcast(F32)[:, u:2 * P:2]
+            if g == 0:
+                return first_got[h][:, u, :, :].rearrange("p m e -> p (m e)").bitcast(F32)
+            return last_got[h][:].bitcast(F32)[:, u:2 * P:2]
 
         def capped_scores(g):
             capped = sbuf([P, PACK, NQ], F32, "capped%d" % g)

@@ -88,8 +88,8 @@ def tile_attend_sigm_cap_kb_srtq256n1024t2048_kernel(tc, qT, k_words, k_scales, 
         words = k_words[0].rearrange("p t b -> p (t b)").bitcast(I32)
         nc.sync.dma_start(out=ks_pool[SCALE_BASE:P, :].bitcast(I32),
                           in_=k_scales.rearrange("o f t -> f o t").bitcast(I32))
-        nc.sync.dma_start(out=kw_pool[:, 0:HEAD], in_=words[:, 0:HEAD])
         load_queries(0)
+        nc.sync.dma_start(out=kw_pool[:, 0:HEAD], in_=words[:, 0:HEAD])
         load_queries(1)
         nc.sync.dma_start(out=kw_pool[:, HEAD:T], in_=words[:, HEAD:T])
 
@@ -109,13 +109,11 @@ def tile_attend_sigm_cap_kb_srtq256n1024t2048_kernel(tc, qT, k_words, k_scales, 
         kb_got = tiles(SLOT_PASSES, [P, K_PASS], F32, "kb_got")
         for g in range(SLOT_PASSES):
             nc.scalar.activation(out=kb_got[g][:], in_=kb_pool[:].indirect(listed(g)), func=ACT.Copy)
-        vs_got = [sbuf([P, K_PASS], F32, "vs_got0")]
-        nc.scalar.activation(out=vs_got[0][:], in_=vs_pool[:].indirect(listed(0)), func=ACT.Copy)
         q_bf = tiles(D_PASSES, [P, NQ, PACK], BF16, "q_bf")
-        for o in range(D_PASSES):
-            weave(q_bf[o][:], q_raw[o][:])
-        vs_got.append(placed([P, K_PASS], F32, "vs_got1", 0))
-        nc.scalar.activation(out=vs_got[1][:], in_=vs_pool[:].indirect(listed(1)), func=ACT.Copy)
+        vs_got = [sbuf([P, K_PASS], F32, "vs_got0"), placed([P, K_PASS], F32, "vs_got1", 0)]
+        for i in range(2):
+            weave(q_bf[i][:], q_raw[i][:])
+            nc.scalar.activation(out=vs_got[i][:], in_=vs_pool[:].indirect(listed(i)), func=ACT.Copy)
         kb_turned = bank(7, [P, P + SLOT_PASSES * PACK - 1], F32, "kb_turned")
 
         def turn_bias(g, place):
@@ -144,7 +142,7 @@ def tile_attend_sigm_cap_kb_srtq256n1024t2048_kernel(tc, qT, k_words, k_scales, 
             return codes, plane
 
         def gather_words(g):
-            got = sbuf([P, K_PASS], U32, "kw_got%d" % g, ("kw_got0", "q_bf0")[g])
+            got = sbuf([P, K_PASS], U32, "kw_got%d" % g, "kw_got")
             nc.vector.tensor_copy(out=got[:], in_=kw_pool[:, 0:(HEAD, T)[g]].bitcast(U32).indirect(listed(g)))
             return got
 
@@ -154,14 +152,15 @@ def tile_attend_sigm_cap_kb_srtq256n1024t2048_kernel(tc, qT, k_words, k_scales, 
                                   in_=got[:].bitcast(U16).rearrange("p (c i t o) -> p o c t i", t=PACK, i=4, o=D_PASSES))
             return codes
 
-        k_codes = [part_words(gather_words(0), "k_codes0")]
-        kb_dealt = sbuf([P, PACK, P], F32, "kb_dealt", "kw_got0")
+        first_words = gather_words(0)
+        q_mx = [quantised(q_bf[0][:].rearrange("p q t -> p (q t)"), NQ, "q0")]
+        kb_dealt = sbuf([P, PACK, P], F32, "kb_dealt", "q_bf0")
         nc.vector.tensor_copy(out=kb_dealt[:].rearrange("p t m -> p m t"),
                               in_=kb_got[1][:].rearrange("p (m t) -> p m t", t=PACK))
         turn_bias(1, lambda t: kb_dealt[:, t, :])
         half_kb = placed([P, SLOT_PASSES * PACK], F32, "half_kb", 4 * K_PASS)
         nc.scalar.activation(out=half_kb[:], in_=kb_turned[:, LAST:LAST + SLOT_PASSES * PACK], func=ACT.Copy, scale=0.5)
-        q_mx = [quantised(q_bf[0][:].rearrange("p q t -> p (q t)"), NQ, "q0")]
+        k_codes = [part_words(first_words, "k_codes0", "kb_got1")]
         last_words = gather_words(1)
         q_mx.append(quantised(q_bf[1][:].rearrange("p q t -> p (q t)"), NQ, "q1"))
         k_codes.append(part_words(last_words, "k_codes1", "q_bf1"))

@@ -27,7 +27,13 @@ LAST = P - 1
 SCALE_ROWS = 16 * D_PASSES
 SCALE_BASE = P - SCALE_ROWS
 HEAD = T - N + K_PASS
-HELD = 8192
+SCALAR_QUERIES = 88
+ALIGN = 256
+EARLY_ZEROS = 256
+Q0_AT = 0
+KW_AT = Q0_AT + 3 * PACK * NQ
+Q1_AT = KW_AT + 4 * T
+P1_AT = Q1_AT + 4 * PACK * NQ
 P_BYTES = 4 * PACK * P
 
 FLOPS = 2 * NQ * N * (D + DV)
@@ -42,13 +48,13 @@ def tile_attend_sigm_cap_kb_srtq256n1024t2048_kernel(tc, qT, k_words, k_scales, 
         ps = ctx.enter_context(tc.psum_pool(name="ps", bufs=1))
 
         def sbuf(shape, dtype, name, tag=None):
-            return sb.tile(shape, dtype, name=name, tag=tag or name, align_bytes=64)
+            return sb.tile(shape, dtype, name=name, tag=tag or name, align_bytes=ALIGN)
 
         def tiles(count, shape, dtype, name):
             return [sbuf(shape, dtype, "%s%d" % (name, i)) for i in range(count)]
 
         def placed(shape, dtype, name, offset):
-            return shared.tile(shape, dtype, name=name, align_bytes=64, offset=offset)
+            return shared.tile(shape, dtype, name=name, align_bytes=ALIGN, offset=offset)
 
         def bank(index, shape, dtype, name):
             return ps.tile(shape, dtype, name=name, tag="bank%d" % index)
@@ -61,12 +67,9 @@ def tile_attend_sigm_cap_kb_srtq256n1024t2048_kernel(tc, qT, k_words, k_scales, 
 
         ks_pool = sbuf([P, T], U8, "ks_pool")
         kb_pool = sbuf([P, T], F32, "kb_pool")
-        kw_pool = sbuf([P, T], I32, "kw_pool")
         k_planes = sbuf([P, D_PASSES, N], U8, "k_planes")
-
-
-        vs_pool = sbuf([P, T], F32, "vs_pool")
         nc.scalar.dma_start(out=kb_pool[LAST:P, :], in_=kb[LAST:P, :])
+        vs_pool = sbuf([P, T], F32, "vs_pool")
         nc.scalar.dma_start(out=vs_pool[LAST:P, :], in_=vs[LAST:P, :])
         warm_in = sbuf([P, 1], F32, "warm_in")
         warm_out = sbuf([P, 1], F32, "warm_out")
@@ -74,66 +77,63 @@ def tile_attend_sigm_cap_kb_srtq256n1024t2048_kernel(tc, qT, k_words, k_scales, 
         nc.scalar.activation(out=warm_out[:], in_=warm_in[:], func=ACT.Sigmoid)
         ident = sbuf([P, P], F32, "ident")
         make_identity(nc, ident[:])
-        nc.gpsimd.memset(k_planes[:].rearrange("p o n -> p (o n)").bitcast(I32), 0)
-        nc.vector.memset(kb_pool[0:LAST, :].bitcast(I32), 0)
         nc.vector.memset(ks_pool[0:SCALE_BASE, :].bitcast(I32), 0)
-        nc.vector.memset(vs_pool[0:LAST, :].bitcast(I32), 0)
+        nc.vector.memset(k_planes[:].rearrange("p o n -> p (o n)").bitcast(I32), 0)
+        nc.vector.memset(kb_pool[0:LAST, :].bitcast(I32), 0)
+        nc.vector.memset(vs_pool[0:LAST, 0:EARLY_ZEROS].bitcast(I32), 0)
 
-        q_raw = [sbuf([P, PACK, NQ], F32, "q_raw0"), placed([P, PACK, NQ], F32, "q_raw1", 0)]
+        q_raw = [sbuf([P, PACK, NQ], F32, "q_raw0"), placed([P, PACK, NQ], F32, "q_raw1", Q1_AT)]
 
         def load_queries(o):
             rows = qT[0, o * K_PASS:(o + 1) * K_PASS, :]
             nc.sync.dma_start(out=q_raw[o][:], in_=rows.rearrange("(p t) q -> p t q", t=PACK))
 
+        kw_pool = placed([P, T], I32, "kw_pool", KW_AT)
         words = k_words[0].rearrange("p t b -> p (t b)").bitcast(I32)
         nc.sync.dma_start(out=ks_pool[SCALE_BASE:P, :].bitcast(I32),
                           in_=k_scales.rearrange("o f t -> f o t").bitcast(I32))
         load_queries(0)
         nc.sync.dma_start(out=kw_pool[:, 0:HEAD], in_=words[:, 0:HEAD])
         load_queries(1)
-        nc.sync.dma_start(out=kw_pool[:, HEAD:T], in_=words[:, HEAD:T])
 
         ks_got = sbuf([P, N], U8, "ks_got")
         nc.vector.tensor_copy(out=ks_got[:].rearrange("p (t m) -> p m t", t=PACK), in_=ks_pool[:].indirect(offsets[:]))
-
-        def lay_out(cols, g, row):
-            nc.sync.dma_start(out=cols[:, g, 0:PACK], in_=row)
-
-        def weave(woven, planes):
-            nc.scalar.copy(out=woven.rearrange("p (c i) t -> p c t i", i=4),
-                           in_=planes.rearrange("p t (c i) -> p c t i", i=4))
-
-        def bias_column(g, t):
-            return (SLOT_PASSES - 1 - g) * PACK + t
-
-        kb_got = tiles(SLOT_PASSES, [P, K_PASS], F32, "kb_got")
-        for g in range(SLOT_PASSES):
-            nc.scalar.activation(out=kb_got[g][:], in_=kb_pool[:].indirect(listed(g)), func=ACT.Copy)
-        q_bf = tiles(D_PASSES, [P, NQ, PACK], BF16, "q_bf")
-        vs_got = [sbuf([P, K_PASS], F32, "vs_got0"), placed([P, K_PASS], F32, "vs_got1", 0)]
-        for i in range(2):
-            weave(q_bf[i][:], q_raw[i][:])
-            nc.scalar.activation(out=vs_got[i][:], in_=vs_pool[:].indirect(listed(i)), func=ACT.Copy)
-        kb_turned = bank(7, [P, P + SLOT_PASSES * PACK - 1], F32, "kb_turned")
-
-        def turn_bias(g, place):
-            for t in reversed(range(PACK)):
-                j = bias_column(g, t)
-                nc.tensor.transpose(kb_turned[:, j:j + P], place(t), ident[:])
-
-        turn_bias(0, lambda t: kb_got[0][:, t:K_PASS:PACK])
+        nc.vector.memset(vs_pool[0:LAST, EARLY_ZEROS:T].bitcast(I32), 0)
         rows_a_quad = SCALE_ROWS // 4
         for quad in range(4):
             first = SCALE_BASE + quad * rows_a_quad
             nc.sync.dma_start(out=k_planes[32 * quad:32 * quad + 4, :, :].bitcast(I32),
                               in_=ks_got[first:first + rows_a_quad, :].bitcast(I32))
-        vs_cols = sbuf([P, SLOT_PASSES, 2 * PACK], F32, "vs_cols")
+        nc.sync.dma_start(out=kw_pool[:, HEAD:T], in_=words[:, HEAD:T])
         v_pool = tiles(V_TILES, [P, T], F32, "v_pool")
         for h in range(V_TILES):
             for cols in (slice(0, HEAD), slice(HEAD, T)):
                 nc.sync.dma_start(out=v_pool[h][:, cols], in_=vT[h * P:(h + 1) * P, cols])
+
+        def woven_views(woven, planes, queries):
+            return (woven[:, queries, :].rearrange("p (c i) t -> p c t i", i=4),
+                    planes[:, :, queries].rearrange("p t (c i) -> p c t i", i=4))
+
+        kb_got = tiles(SLOT_PASSES, [P, K_PASS], F32, "kb_got")
         for g in range(SLOT_PASSES):
-            lay_out(vs_cols, g, vs_got[g][LAST:P, :])
+            nc.scalar.activation(out=kb_got[g][:], in_=kb_pool[:].indirect(listed(g)), func=ACT.Copy)
+        q_bf = [placed([P, NQ, PACK], BF16, "q_bf%d" % o, Q0_AT + o * PACK * NQ) for o in range(D_PASSES)]
+        vs_got = [sbuf([P, K_PASS], F32, "vs_got0"), placed([P, K_PASS], F32, "vs_got1", Q1_AT)]
+        nc.scalar.copy(*woven_views(q_bf[0], q_raw[0], slice(0, NQ)))
+        nc.scalar.activation(out=vs_got[0][:], in_=vs_pool[:].indirect(listed(0)), func=ACT.Copy)
+        nc.scalar.copy(*woven_views(q_bf[1], q_raw[1], slice(0, SCALAR_QUERIES)))
+
+        def turned_bias(g, place):
+            turned = bank(7 - g, [P, P + PACK - 1], F32, "kb_turned")
+            for t in reversed(range(PACK)):
+                nc.tensor.transpose(turned[:, t:t + P], place(t), ident[:])
+            return turned
+
+        def halved(turned, half):
+            nc.scalar.activation(out=half[:], in_=turned[:, LAST:LAST + PACK], func=ACT.Copy, scale=0.5)
+            return half
+
+        kb_turned0 = turned_bias(0, lambda t: kb_got[0][:, t:K_PASS:PACK])
 
         def quantised(source, width, name, tag=None):
             codes = sbuf([P, width], U32, name + "_codes", tag)
@@ -141,31 +141,38 @@ def tile_attend_sigm_cap_kb_srtq256n1024t2048_kernel(tc, qT, k_words, k_scales, 
             nc.vector.quantize_mx(out=codes[:].bitcast(FP8X4), scales=plane[:], in_=source)
             return codes, plane
 
-        def gather_words(g):
-            got = sbuf([P, K_PASS], U32, "kw_got%d" % g, "kw_got")
+        def gather_words(g, got):
             nc.vector.tensor_copy(out=got[:], in_=kw_pool[:, 0:(HEAD, T)[g]].bitcast(U32).indirect(listed(g)))
-            return got
+            return got[:].bitcast(U16).rearrange("p (c i t o) -> p o c t i", t=PACK, i=4, o=D_PASSES)
 
-        def part_words(got, name, tag=None):
-            codes = sbuf([P, D_PASSES, K_PASS], U16, name, tag)
-            nc.vector.tensor_copy(out=codes[:].rearrange("p o (t c i) -> p o c t i", t=PACK, i=4),
-                                  in_=got[:].bitcast(U16).rearrange("p (c i t o) -> p o c t i", t=PACK, i=4, o=D_PASSES))
-            return codes
-
-        first_words = gather_words(0)
+        first_words = gather_words(0, sbuf([P, K_PASS], U32, "kw_got0"))
         q_mx = [quantised(q_bf[0][:].rearrange("p q t -> p (q t)"), NQ, "q0")]
-        kb_dealt = sbuf([P, PACK, P], F32, "kb_dealt", "q_bf0")
+        first_codes = [placed([P, K_PASS], U16, "k_codes00", Q0_AT), placed([P, K_PASS], U16, "k_codes01", Q1_AT + 6 * K_PASS)]
+
+        def part_first(o):
+            nc.vector.tensor_copy(out=first_codes[o][:].rearrange("p (t c i) -> p c t i", t=PACK, i=4),
+                                  in_=first_words[:, o])
+
+        part_first(0)
+        nc.vector.tensor_copy(*woven_views(q_bf[1], q_raw[1], slice(SCALAR_QUERIES, NQ)))
+        part_first(1)
+        q_mx.append(quantised(q_bf[1][:].rearrange("p q t -> p (q t)"), NQ, "q1"))
+        nc.scalar.activation(out=vs_got[1][:], in_=vs_pool[:].indirect(listed(1)), func=ACT.Copy)
+        half_kb = [halved(kb_turned0, placed([P, PACK], F32, "half_kb0", Q1_AT + 4 * K_PASS))]
+        vs_cols = sbuf([P, SLOT_PASSES, 2 * PACK], F32, "vs_cols")
+        for g in range(SLOT_PASSES):
+            nc.sync.dma_start(out=vs_cols[:, g, 0:PACK], in_=vs_got[g][LAST:P, :])
+
+        last_words = gather_words(1, placed([P, K_PASS], U32, "kw_got1", Q0_AT + PACK * NQ))
+        kb_dealt = placed([P, PACK, P], F32, "kb_dealt", KW_AT)
         nc.vector.tensor_copy(out=kb_dealt[:].rearrange("p t m -> p m t"),
                               in_=kb_got[1][:].rearrange("p (m t) -> p m t", t=PACK))
-        turn_bias(1, lambda t: kb_dealt[:, t, :])
-        half_kb = placed([P, SLOT_PASSES * PACK], F32, "half_kb", 4 * K_PASS)
-        nc.scalar.activation(out=half_kb[:], in_=kb_turned[:, LAST:LAST + SLOT_PASSES * PACK], func=ACT.Copy, scale=0.5)
-        k_codes = [part_words(first_words, "k_codes0", "kb_got1")]
-        last_words = gather_words(1)
-        q_mx.append(quantised(q_bf[1][:].rearrange("p q t -> p (q t)"), NQ, "q1"))
-        k_codes.append(part_words(last_words, "k_codes1", "q_bf1"))
+        last_codes = sbuf([P, D_PASSES, K_PASS], U16, "k_codes1")
+        nc.vector.tensor_copy(out=last_codes[:].rearrange("p o (t c i) -> p o c t i", t=PACK, i=4), in_=last_words)
+        k_codes = [[first_codes[o][:] for o in range(D_PASSES)], [last_codes[:, o, :] for o in range(D_PASSES)]]
 
-        first_got = [sbuf([P, 2, P, 2], BF16, "first_got0"), placed([P, 2, P, 2], BF16, "first_got1", HELD - K_PASS)]
+        first_got = [sbuf([P, 2, P, 2], BF16, "first_got0"),
+                     placed([P, 2, P, 2], BF16, "first_got1", P1_AT + P_BYTES - K_PASS)]
         last_got = tiles(V_TILES, [P, K_PASS], BF16, "last_got")
         for h in range(V_TILES):
             nc.vector.tensor_copy(out=first_got[h][:].rearrange("p u m e -> p m u e"),
@@ -184,13 +191,13 @@ def tile_attend_sigm_cap_kb_srtq256n1024t2048_kernel(tc, qT, k_words, k_scales, 
             for t, o in (steps, sorted(steps))[g]:
                 nc.tensor.matmul_mx(
                     out=scores[t][:],
-                    lhsT=k_codes[g][:, o, t * P:(t + 1) * P].bitcast(FP4X4),
+                    lhsT=k_codes[g][o][:, t * P:(t + 1) * P].bitcast(FP4X4),
                     lhsT_scale=k_planes[:, o, (t * SLOT_PASSES + g) * P:(t * SLOT_PASSES + g + 1) * P],
                     rhs=q_mx[o][0][:].bitcast(FP8X4), rhs_scale=q_mx[o][1][:],
                     start=(o == 0), stop=(o == D_PASSES - 1))
                 if o == D_PASSES - 1:
                     nc.scalar.activation(out=capped[:, t, :], in_=scores[t][:], func=ACT.Tanh,
-                                         bias=half_kb[:, bias_column(g, t):bias_column(g, t) + 1], scale=0.5)
+                                         bias=half_kb[g][:, t:t + 1], scale=0.5)
             return capped
 
         def sigmoid(capped, first, width, p):
@@ -214,10 +221,11 @@ def tile_attend_sigm_cap_kb_srtq256n1024t2048_kernel(tc, qT, k_words, k_scales, 
             return woven[:].rearrange("p h e u -> p (h e u)").bitcast(BF16)
 
         capped0 = capped_scores(0)
+        half_kb.append(halved(turned_bias(1, lambda t: kb_dealt[:, t, :]), sbuf([P, PACK], F32, "half_kb1")))
         p0 = sigmoid(capped0, 0, NQ, sbuf([P, PACK, NQ], F32, "p0"))
         capped1 = capped_scores(1)
         v_woven = [turned_values(0)]
-        p1 = [sigmoid(capped1, qh * P, P, placed([P, PACK, P], F32, "p1_%d" % qh, HELD + (qh - 1) * P_BYTES))
+        p1 = [sigmoid(capped1, qh * P, P, placed([P, PACK, P], F32, "p1_%d" % qh, P1_AT + qh * P_BYTES))
               for qh in range(Q_TILES)]
         v_woven.append(turned_values(1))
 

@@ -25,15 +25,18 @@ V_TILES = DV // P
 LIST_COLS = K_PASS // 16
 LAST = P - 1
 SCALE_ROWS = 16 * D_PASSES
-SCALE_BASE = P - SCALE_ROWS
+SCALE_BASE = 32
 HEAD = T - N + K_PASS
-SCALAR_QUERIES = 88
+SCALAR_QUERIES = 136
 ALIGN = 256
 EARLY_ZEROS = 256
 Q0_AT = 0
 KW_AT = Q0_AT + 3 * PACK * NQ
-Q1_AT = KW_AT + 4 * T
-P1_AT = Q1_AT + 4 * PACK * NQ
+CODES_AT = KW_AT + 4 * T
+Q1_AT = CODES_AT + 2 * K_PASS - ALIGN
+VS_AT = Q1_AT + ALIGN
+KB_AT = VS_AT + 4 * K_PASS
+P1_AT = KB_AT + 4 * K_PASS
 P_BYTES = 4 * PACK * P
 
 FLOPS = 2 * NQ * N * (D + DV)
@@ -67,18 +70,18 @@ def tile_attend_sigm_cap_kb_srtq256n1024t2048_kernel(tc, qT, k_words, k_scales, 
 
         ks_pool = sbuf([P, T], U8, "ks_pool")
         kb_pool = sbuf([P, T], F32, "kb_pool")
-        k_planes = sbuf([P, D_PASSES, N], U8, "k_planes")
         nc.scalar.dma_start(out=kb_pool[LAST:P, :], in_=kb[LAST:P, :])
         vs_pool = sbuf([P, T], F32, "vs_pool")
         nc.scalar.dma_start(out=vs_pool[LAST:P, :], in_=vs[LAST:P, :])
         warm_in = sbuf([P, 1], F32, "warm_in")
         warm_out = sbuf([P, 1], F32, "warm_out")
-        nc.gpsimd.memset(warm_in[:], 0.0)
+        nc.vector.memset(warm_in[:], 0.0)
         nc.scalar.activation(out=warm_out[:], in_=warm_in[:], func=ACT.Sigmoid)
         ident = sbuf([P, P], F32, "ident")
-        make_identity(nc, ident[:])
+        nc.vector.memset(ident[:], 0.0)
+        make_identity(nc, ident[:], nomemset=True)
         nc.vector.memset(ks_pool[0:SCALE_BASE, :].bitcast(I32), 0)
-        nc.vector.memset(k_planes[:].rearrange("p o n -> p (o n)").bitcast(I32), 0)
+        nc.vector.memset(ks_pool[SCALE_BASE + SCALE_ROWS:P, :].bitcast(I32), 0)
         nc.vector.memset(kb_pool[0:LAST, :].bitcast(I32), 0)
         nc.vector.memset(vs_pool[0:LAST, 0:EARLY_ZEROS].bitcast(I32), 0)
 
@@ -90,7 +93,7 @@ def tile_attend_sigm_cap_kb_srtq256n1024t2048_kernel(tc, qT, k_words, k_scales, 
 
         kw_pool = placed([P, T], I32, "kw_pool", KW_AT)
         words = k_words[0].rearrange("p t b -> p (t b)").bitcast(I32)
-        nc.sync.dma_start(out=ks_pool[SCALE_BASE:P, :].bitcast(I32),
+        nc.sync.dma_start(out=ks_pool[SCALE_BASE:SCALE_BASE + SCALE_ROWS, :].bitcast(I32),
                           in_=k_scales.rearrange("o f t -> f o t").bitcast(I32))
         load_queries(0)
         nc.sync.dma_start(out=kw_pool[:, 0:HEAD], in_=words[:, 0:HEAD])
@@ -99,6 +102,7 @@ def tile_attend_sigm_cap_kb_srtq256n1024t2048_kernel(tc, qT, k_words, k_scales, 
         ks_got = sbuf([P, N], U8, "ks_got")
         nc.vector.tensor_copy(out=ks_got[:].rearrange("p (t m) -> p m t", t=PACK), in_=ks_pool[:].indirect(offsets[:]))
         nc.vector.memset(vs_pool[0:LAST, EARLY_ZEROS:T].bitcast(I32), 0)
+        k_planes = sbuf([P, D_PASSES, N], U8, "k_planes", "ks_pool")
         rows_a_quad = SCALE_ROWS // 4
         for quad in range(4):
             first = SCALE_BASE + quad * rows_a_quad
@@ -118,7 +122,7 @@ def tile_attend_sigm_cap_kb_srtq256n1024t2048_kernel(tc, qT, k_words, k_scales, 
         for g in range(SLOT_PASSES):
             nc.scalar.activation(out=kb_got[g][:], in_=kb_pool[:].indirect(listed(g)), func=ACT.Copy)
         q_bf = [placed([P, NQ, PACK], BF16, "q_bf%d" % o, Q0_AT + o * PACK * NQ) for o in range(D_PASSES)]
-        vs_got = [sbuf([P, K_PASS], F32, "vs_got0"), placed([P, K_PASS], F32, "vs_got1", Q1_AT)]
+        vs_got = [sbuf([P, K_PASS], F32, "vs_got0"), placed([P, K_PASS], F32, "vs_got1", VS_AT)]
         nc.scalar.copy(*woven_views(q_bf[0], q_raw[0], slice(0, NQ)))
         nc.scalar.activation(out=vs_got[0][:], in_=vs_pool[:].indirect(listed(0)), func=ACT.Copy)
         nc.scalar.copy(*woven_views(q_bf[1], q_raw[1], slice(0, SCALAR_QUERIES)))
@@ -141,13 +145,13 @@ def tile_attend_sigm_cap_kb_srtq256n1024t2048_kernel(tc, qT, k_words, k_scales, 
             nc.vector.quantize_mx(out=codes[:].bitcast(FP8X4), scales=plane[:], in_=source)
             return codes, plane
 
-        def gather_words(g, got):
-            nc.vector.tensor_copy(out=got[:], in_=kw_pool[:, 0:(HEAD, T)[g]].bitcast(U32).indirect(listed(g)))
+        def gather_words(entries, reach, got):
+            nc.vector.tensor_copy(out=got[:], in_=kw_pool[:, 0:reach].bitcast(U32).indirect(entries))
             return got[:].bitcast(U16).rearrange("p (c i t o) -> p o c t i", t=PACK, i=4, o=D_PASSES)
 
-        first_words = gather_words(0, sbuf([P, K_PASS], U32, "kw_got0"))
+        first_words = gather_words(listed(0), HEAD, sbuf([P, K_PASS], U32, "kw_got0"))
         q_mx = [quantised(q_bf[0][:].rearrange("p q t -> p (q t)"), NQ, "q0")]
-        first_codes = [placed([P, K_PASS], U16, "k_codes00", Q0_AT), placed([P, K_PASS], U16, "k_codes01", Q1_AT + 6 * K_PASS)]
+        first_codes = [placed([P, K_PASS], U16, "k_codes00", Q0_AT), placed([P, K_PASS], U16, "k_codes01", CODES_AT)]
 
         def part_first(o):
             nc.vector.tensor_copy(out=first_codes[o][:].rearrange("p (t c i) -> p c t i", t=PACK, i=4),
@@ -158,17 +162,22 @@ def tile_attend_sigm_cap_kb_srtq256n1024t2048_kernel(tc, qT, k_words, k_scales, 
         part_first(1)
         q_mx.append(quantised(q_bf[1][:].rearrange("p q t -> p (q t)"), NQ, "q1"))
         nc.scalar.activation(out=vs_got[1][:], in_=vs_pool[:].indirect(listed(1)), func=ACT.Copy)
-        half_kb = [halved(kb_turned0, placed([P, PACK], F32, "half_kb0", Q1_AT + 4 * K_PASS))]
+        half_kb = [halved(kb_turned0, sbuf([P, PACK], F32, "half_kb0"))]
+        kb_dealt = placed([P, PACK, P], F32, "kb_dealt", KB_AT)
+        nc.scalar.copy(out=kb_dealt[:].rearrange("p t m -> p m t"),
+                       in_=kb_got[1][:].rearrange("p (m t) -> p m t", t=PACK))
         vs_cols = sbuf([P, SLOT_PASSES, 2 * PACK], F32, "vs_cols")
         for g in range(SLOT_PASSES):
             nc.sync.dma_start(out=vs_cols[:, g, 0:PACK], in_=vs_got[g][LAST:P, :])
 
-        last_words = gather_words(1, placed([P, K_PASS], U32, "kw_got1", Q0_AT + PACK * NQ))
-        kb_dealt = placed([P, PACK, P], F32, "kb_dealt", KW_AT)
-        nc.vector.tensor_copy(out=kb_dealt[:].rearrange("p t m -> p m t"),
-                              in_=kb_got[1][:].rearrange("p (m t) -> p m t", t=PACK))
+        half = LIST_COLS // 2
+        last_words = [gather_words(listed(1)[:, a * half:(a + 1) * half], T,
+                                   placed([P, K_PASS // 2], U32, "kw_got1%d" % a, Q0_AT + (1 + a) * PACK * NQ))
+                      for a in range(2)]
         last_codes = sbuf([P, D_PASSES, K_PASS], U16, "k_codes1")
-        nc.vector.tensor_copy(out=last_codes[:].rearrange("p o (t c i) -> p o c t i", t=PACK, i=4), in_=last_words)
+        for a in range(2):
+            nc.vector.tensor_copy(out=last_codes[:].rearrange("p o (t a c i) -> p a o c t i", t=PACK, a=2, i=4)[:, a],
+                                  in_=last_words[a])
         k_codes = [[first_codes[o][:] for o in range(D_PASSES)], [last_codes[:, o, :] for o in range(D_PASSES)]]
 
         first_got = [sbuf([P, 2, P, 2], BF16, "first_got0"),

@@ -30,14 +30,14 @@ HEAD = T - N + K_PASS
 SCALAR_QUERIES = 136
 ALIGN = 256
 EARLY_ZEROS = 256
-Q0_AT = 0
-KW_AT = Q0_AT + 3 * PACK * NQ
+KW_AT = 0
 CODES_AT = KW_AT + 4 * T
 Q1_AT = CODES_AT + 2 * K_PASS - ALIGN
 VS_AT = Q1_AT + ALIGN
-KB_AT = VS_AT + 4 * K_PASS
-P1_AT = KB_AT + 4 * K_PASS
+P1_AT = Q1_AT + 4 * PACK * NQ
+KB_AT = P1_AT + 4 * PACK * NQ
 P_BYTES = 4 * PACK * P
+Q0_AT = KB_AT
 
 FLOPS = 2 * NQ * N * (D + DV)
 BYTES = 4 * D * NQ + 4 * P * T + 32 * T + 4 * DV * T + 2 * 4 * T + 2 * P * N // 16 + 4 * NQ * DV
@@ -69,10 +69,15 @@ def tile_attend_sigm_cap_kb_srtq256n1024t2048_kernel(tc, qT, k_words, k_scales, 
             return offsets[:, g * LIST_COLS:(g + 1) * LIST_COLS]
 
         ks_pool = sbuf([P, T], U8, "ks_pool")
-        kb_pool = sbuf([P, T], F32, "kb_pool")
-        nc.scalar.dma_start(out=kb_pool[LAST:P, :], in_=kb[LAST:P, :])
+        kb_pool = placed([P, T], F32, "kb_pool", KB_AT)
         vs_pool = sbuf([P, T], F32, "vs_pool")
-        nc.scalar.dma_start(out=vs_pool[LAST:P, :], in_=vs[LAST:P, :])
+        q_raw = [sbuf([P, PACK, NQ], F32, "q_raw0"), placed([P, PACK, NQ], F32, "q_raw1", Q1_AT)]
+
+        def load_queries(o):
+            rows = qT[0, o * K_PASS:(o + 1) * K_PASS, :]
+            nc.sync.dma_start(out=q_raw[o][:], in_=rows.rearrange("(p t) q -> p t q", t=PACK))
+
+        nc.scalar.dma_start(out=kb_pool[LAST:P, :], in_=kb[LAST:P, :])
         warm_in = sbuf([P, 1], F32, "warm_in")
         warm_out = sbuf([P, 1], F32, "warm_out")
         nc.vector.memset(warm_in[:], 0.0)
@@ -85,18 +90,13 @@ def tile_attend_sigm_cap_kb_srtq256n1024t2048_kernel(tc, qT, k_words, k_scales, 
         nc.vector.memset(kb_pool[0:LAST, :].bitcast(I32), 0)
         nc.vector.memset(vs_pool[0:LAST, 0:EARLY_ZEROS].bitcast(I32), 0)
 
-        q_raw = [sbuf([P, PACK, NQ], F32, "q_raw0"), placed([P, PACK, NQ], F32, "q_raw1", Q1_AT)]
-
-        def load_queries(o):
-            rows = qT[0, o * K_PASS:(o + 1) * K_PASS, :]
-            nc.sync.dma_start(out=q_raw[o][:], in_=rows.rearrange("(p t) q -> p t q", t=PACK))
-
         kw_pool = placed([P, T], I32, "kw_pool", KW_AT)
         words = k_words[0].rearrange("p t b -> p (t b)").bitcast(I32)
         nc.sync.dma_start(out=ks_pool[SCALE_BASE:SCALE_BASE + SCALE_ROWS, :].bitcast(I32),
                           in_=k_scales.rearrange("o f t -> f o t").bitcast(I32))
         load_queries(0)
         nc.sync.dma_start(out=kw_pool[:, 0:HEAD], in_=words[:, 0:HEAD])
+        nc.sync.dma_start(out=vs_pool[LAST:P, :], in_=vs[LAST:P, :])
         load_queries(1)
 
         ks_got = sbuf([P, N], U8, "ks_got")
@@ -108,11 +108,6 @@ def tile_attend_sigm_cap_kb_srtq256n1024t2048_kernel(tc, qT, k_words, k_scales, 
             first = SCALE_BASE + quad * rows_a_quad
             nc.sync.dma_start(out=k_planes[32 * quad:32 * quad + 4, :, :].bitcast(I32),
                               in_=ks_got[first:first + rows_a_quad, :].bitcast(I32))
-        nc.sync.dma_start(out=kw_pool[:, HEAD:T], in_=words[:, HEAD:T])
-        v_pool = tiles(V_TILES, [P, T], F32, "v_pool")
-        for h in range(V_TILES):
-            for cols in (slice(0, HEAD), slice(HEAD, T)):
-                nc.sync.dma_start(out=v_pool[h][:, cols], in_=vT[h * P:(h + 1) * P, cols])
 
         def woven_views(woven, planes, queries):
             return (woven[:, queries, :].rearrange("p (c i) t -> p c t i", i=4),
@@ -121,23 +116,26 @@ def tile_attend_sigm_cap_kb_srtq256n1024t2048_kernel(tc, qT, k_words, k_scales, 
         kb_got = tiles(SLOT_PASSES, [P, K_PASS], F32, "kb_got")
         for g in range(SLOT_PASSES):
             nc.scalar.activation(out=kb_got[g][:], in_=kb_pool[:].indirect(listed(g)), func=ACT.Copy)
+        kb_cols = sbuf([P, 2 * PACK], F32, "kb_cols")
+        nc.sync.dma_start(out=kb_cols[:, 0:PACK], in_=kb_got[1][LAST:P, :])
+        nc.sync.dma_start(out=kw_pool[:, HEAD:T], in_=words[:, HEAD:T])
+        v_pool = tiles(V_TILES, [P, T], F32, "v_pool")
+        for h in range(V_TILES):
+            for cols in (slice(0, HEAD), slice(HEAD, T)):
+                nc.sync.dma_start(out=v_pool[h][:, cols], in_=vT[h * P:(h + 1) * P, cols])
         q_bf = [placed([P, NQ, PACK], BF16, "q_bf%d" % o, Q0_AT + o * PACK * NQ) for o in range(D_PASSES)]
         vs_got = [sbuf([P, K_PASS], F32, "vs_got0"), placed([P, K_PASS], F32, "vs_got1", VS_AT)]
         nc.scalar.copy(*woven_views(q_bf[0], q_raw[0], slice(0, NQ)))
         nc.scalar.activation(out=vs_got[0][:], in_=vs_pool[:].indirect(listed(0)), func=ACT.Copy)
         nc.scalar.copy(*woven_views(q_bf[1], q_raw[1], slice(0, SCALAR_QUERIES)))
 
-        def turned_bias(g, place):
-            turned = bank(7 - g, [P, P + PACK - 1], F32, "kb_turned")
-            for t in reversed(range(PACK)):
-                nc.tensor.transpose(turned[:, t:t + P], place(t), ident[:])
-            return turned
+        kb_turned = bank(7, [P, P + PACK - 1], F32, "kb_turned")
+        for t in reversed(range(PACK)):
+            nc.tensor.transpose(kb_turned[:, t:t + P], kb_got[0][:, t:K_PASS:PACK], ident[:])
 
-        def halved(turned, half):
-            nc.scalar.activation(out=half[:], in_=turned[:, LAST:LAST + PACK], func=ACT.Copy, scale=0.5)
+        def halved(columns, half):
+            nc.scalar.activation(out=half[:], in_=columns, func=ACT.Copy, scale=0.5)
             return half
-
-        kb_turned0 = turned_bias(0, lambda t: kb_got[0][:, t:K_PASS:PACK])
 
         def quantised(source, width, name, tag=None):
             codes = sbuf([P, width], U32, name + "_codes", tag)
@@ -162,10 +160,7 @@ def tile_attend_sigm_cap_kb_srtq256n1024t2048_kernel(tc, qT, k_words, k_scales, 
         part_first(1)
         q_mx.append(quantised(q_bf[1][:].rearrange("p q t -> p (q t)"), NQ, "q1"))
         nc.scalar.activation(out=vs_got[1][:], in_=vs_pool[:].indirect(listed(1)), func=ACT.Copy)
-        half_kb = [halved(kb_turned0, sbuf([P, PACK], F32, "half_kb0"))]
-        kb_dealt = placed([P, PACK, P], F32, "kb_dealt", KB_AT)
-        nc.scalar.copy(out=kb_dealt[:].rearrange("p t m -> p m t"),
-                       in_=kb_got[1][:].rearrange("p (m t) -> p m t", t=PACK))
+        half_kb = [halved(kb_turned[:, LAST:LAST + PACK], placed([P, PACK], F32, "half_kb0", VS_AT + 4 * K_PASS))]
         vs_cols = sbuf([P, SLOT_PASSES, 2 * PACK], F32, "vs_cols")
         for g in range(SLOT_PASSES):
             nc.sync.dma_start(out=vs_cols[:, g, 0:PACK], in_=vs_got[g][LAST:P, :])
@@ -230,7 +225,7 @@ def tile_attend_sigm_cap_kb_srtq256n1024t2048_kernel(tc, qT, k_words, k_scales, 
             return woven[:].rearrange("p h e u -> p (h e u)").bitcast(BF16)
 
         capped0 = capped_scores(0)
-        half_kb.append(halved(turned_bias(1, lambda t: kb_dealt[:, t, :]), sbuf([P, PACK], F32, "half_kb1")))
+        half_kb.append(halved(kb_cols[:, 0:PACK], sbuf([P, PACK], F32, "half_kb1")))
         p0 = sigmoid(capped0, 0, NQ, sbuf([P, PACK, NQ], F32, "p0"))
         capped1 = capped_scores(1)
         v_woven = [turned_values(0)]

@@ -29,15 +29,16 @@ SCALE_BASE = 32
 HEAD = T - N + K_PASS
 SCALAR_QUERIES = 136
 ALIGN = 256
+DEALT = 2
 EARLY_ZEROS = 256
-KW_AT = 0
-CODES_AT = KW_AT + 4 * T
-Q1_AT = CODES_AT + 2 * K_PASS - ALIGN
-VS_AT = Q1_AT + ALIGN
-P1_AT = Q1_AT + 4 * PACK * NQ
-KB_AT = P1_AT + 4 * PACK * NQ
+EARLY_VS = 512
+CODES_AT = 0
+PLANE_AT = CODES_AT + 2 * K_PASS
+HALF_AT = PLANE_AT + NQ
+DEALT_AT = HALF_AT + ALIGN
+VS_AT = DEALT_AT + 4 * DEALT * P
+P1_AT = VS_AT + 4 * K_PASS
 P_BYTES = 4 * PACK * P
-Q0_AT = KB_AT
 
 FLOPS = 2 * NQ * N * (D + DV)
 BYTES = 4 * D * NQ + 4 * P * T + 32 * T + 4 * DV * T + 2 * 4 * T + 2 * P * N // 16 + 4 * NQ * DV
@@ -69,15 +70,16 @@ def tile_attend_sigm_cap_kb_srtq256n1024t2048_kernel(tc, qT, k_words, k_scales, 
             return offsets[:, g * LIST_COLS:(g + 1) * LIST_COLS]
 
         ks_pool = sbuf([P, T], U8, "ks_pool")
-        kb_pool = placed([P, T], F32, "kb_pool", KB_AT)
+        kb_pool = sbuf([P, T], F32, "kb_pool")
         vs_pool = sbuf([P, T], F32, "vs_pool")
-        q_raw = [sbuf([P, PACK, NQ], F32, "q_raw0"), placed([P, PACK, NQ], F32, "q_raw1", Q1_AT)]
+        q_raw = tiles(D_PASSES, [P, PACK, NQ], F32, "q_raw")
 
         def load_queries(o):
             rows = qT[0, o * K_PASS:(o + 1) * K_PASS, :]
             nc.sync.dma_start(out=q_raw[o][:], in_=rows.rearrange("(p t) q -> p t q", t=PACK))
 
         nc.scalar.dma_start(out=kb_pool[LAST:P, :], in_=kb[LAST:P, :])
+        nc.scalar.dma_start(out=vs_pool[LAST:P, 0:EARLY_VS], in_=vs[LAST:P, 0:EARLY_VS])
         warm_in = sbuf([P, 1], F32, "warm_in")
         warm_out = sbuf([P, 1], F32, "warm_out")
         nc.vector.memset(warm_in[:], 0.0)
@@ -90,24 +92,24 @@ def tile_attend_sigm_cap_kb_srtq256n1024t2048_kernel(tc, qT, k_words, k_scales, 
         nc.vector.memset(kb_pool[0:LAST, :].bitcast(I32), 0)
         nc.vector.memset(vs_pool[0:LAST, 0:EARLY_ZEROS].bitcast(I32), 0)
 
-        kw_pool = placed([P, T], I32, "kw_pool", KW_AT)
+        kw_pool = sbuf([P, T], I32, "kw_pool")
         words = k_words[0].rearrange("p t b -> p (t b)").bitcast(I32)
         nc.sync.dma_start(out=ks_pool[SCALE_BASE:SCALE_BASE + SCALE_ROWS, :].bitcast(I32),
                           in_=k_scales.rearrange("o f t -> f o t").bitcast(I32))
         load_queries(0)
         nc.sync.dma_start(out=kw_pool[:, 0:HEAD], in_=words[:, 0:HEAD])
-        nc.sync.dma_start(out=vs_pool[LAST:P, :], in_=vs[LAST:P, :])
+        nc.sync.dma_start(out=vs_pool[LAST:P, EARLY_VS:T], in_=vs[LAST:P, EARLY_VS:T])
         load_queries(1)
 
-        ks_got = sbuf([P, N], U8, "ks_got")
-        nc.vector.tensor_copy(out=ks_got[:].rearrange("p (t m) -> p m t", t=PACK), in_=ks_pool[:].indirect(offsets[:]))
+        ks_got = placed([P, P1_AT], U8, "ks_got", 0)
+        nc.vector.tensor_copy(out=ks_got[:, 0:N].rearrange("p (t m) -> p m t", t=PACK), in_=ks_pool[:].indirect(offsets[:]))
         nc.vector.memset(vs_pool[0:LAST, EARLY_ZEROS:T].bitcast(I32), 0)
         k_planes = sbuf([P, D_PASSES, N], U8, "k_planes", "ks_pool")
         rows_a_quad = SCALE_ROWS // 4
-        for quad in range(4):
+        for quad in (0, 2, 1, 3):
             first = SCALE_BASE + quad * rows_a_quad
             nc.sync.dma_start(out=k_planes[32 * quad:32 * quad + 4, :, :].bitcast(I32),
-                              in_=ks_got[first:first + rows_a_quad, :].bitcast(I32))
+                              in_=ks_got[first:first + rows_a_quad, 0:N].bitcast(I32))
 
         def woven_views(woven, planes, queries):
             return (woven[:, queries, :].rearrange("p (c i) t -> p c t i", i=4),
@@ -116,30 +118,34 @@ def tile_attend_sigm_cap_kb_srtq256n1024t2048_kernel(tc, qT, k_words, k_scales, 
         kb_got = tiles(SLOT_PASSES, [P, K_PASS], F32, "kb_got")
         for g in range(SLOT_PASSES):
             nc.scalar.activation(out=kb_got[g][:], in_=kb_pool[:].indirect(listed(g)), func=ACT.Copy)
-        kb_cols = sbuf([P, 2 * PACK], F32, "kb_cols")
-        nc.sync.dma_start(out=kb_cols[:, 0:PACK], in_=kb_got[1][LAST:P, :])
         nc.sync.dma_start(out=kw_pool[:, HEAD:T], in_=words[:, HEAD:T])
         v_pool = tiles(V_TILES, [P, T], F32, "v_pool")
         for h in range(V_TILES):
             for cols in (slice(0, HEAD), slice(HEAD, T)):
                 nc.sync.dma_start(out=v_pool[h][:, cols], in_=vT[h * P:(h + 1) * P, cols])
-        q_bf = [placed([P, NQ, PACK], BF16, "q_bf%d" % o, Q0_AT + o * PACK * NQ) for o in range(D_PASSES)]
+        q_bf = tiles(D_PASSES, [P, NQ, PACK], BF16, "q_bf")
         vs_got = [sbuf([P, K_PASS], F32, "vs_got0"), placed([P, K_PASS], F32, "vs_got1", VS_AT)]
         nc.scalar.copy(*woven_views(q_bf[0], q_raw[0], slice(0, NQ)))
         nc.scalar.activation(out=vs_got[0][:], in_=vs_pool[:].indirect(listed(0)), func=ACT.Copy)
         nc.scalar.copy(*woven_views(q_bf[1], q_raw[1], slice(0, SCALAR_QUERIES)))
 
-        kb_turned = bank(7, [P, P + PACK - 1], F32, "kb_turned")
-        for t in reversed(range(PACK)):
-            nc.tensor.transpose(kb_turned[:, t:t + P], kb_got[0][:, t:K_PASS:PACK], ident[:])
+        kb_turned = [bank(7 - g, [P, P + PACK - 1], F32, "kb_turned") for g in range(SLOT_PASSES)]
+
+        def turn_bias(g, t, place):
+            nc.tensor.transpose(kb_turned[g][:, t:t + P], place, ident[:])
+
+        for g, first in ((0, 0), (1, DEALT)):
+            for t in reversed(range(first, PACK)):
+                turn_bias(g, t, kb_got[g][:, t:K_PASS:PACK])
 
         def halved(columns, half):
             nc.scalar.activation(out=half[:], in_=columns, func=ACT.Copy, scale=0.5)
             return half
 
-        def quantised(source, width, name, tag=None):
+        def quantised(source, width, name, tag=None, plane=None):
             codes = sbuf([P, width], U32, name + "_codes", tag)
-            plane = sbuf([P, width], U8, name + "_plane")
+            if plane is None:
+                plane = sbuf([P, width], U8, name + "_plane")
             nc.vector.quantize_mx(out=codes[:].bitcast(FP8X4), scales=plane[:], in_=source)
             return codes, plane
 
@@ -149,7 +155,7 @@ def tile_attend_sigm_cap_kb_srtq256n1024t2048_kernel(tc, qT, k_words, k_scales, 
 
         first_words = gather_words(listed(0), HEAD, sbuf([P, K_PASS], U32, "kw_got0"))
         q_mx = [quantised(q_bf[0][:].rearrange("p q t -> p (q t)"), NQ, "q0")]
-        first_codes = [placed([P, K_PASS], U16, "k_codes00", Q0_AT), placed([P, K_PASS], U16, "k_codes01", CODES_AT)]
+        first_codes = [sbuf([P, K_PASS], U16, "k_codes00", "q_raw0"), placed([P, K_PASS], U16, "k_codes01", CODES_AT)]
 
         def part_first(o):
             nc.vector.tensor_copy(out=first_codes[o][:].rearrange("p (t c i) -> p c t i", t=PACK, i=4),
@@ -158,16 +164,19 @@ def tile_attend_sigm_cap_kb_srtq256n1024t2048_kernel(tc, qT, k_words, k_scales, 
         part_first(0)
         nc.vector.tensor_copy(*woven_views(q_bf[1], q_raw[1], slice(SCALAR_QUERIES, NQ)))
         part_first(1)
-        q_mx.append(quantised(q_bf[1][:].rearrange("p q t -> p (q t)"), NQ, "q1"))
+        q_mx.append(quantised(q_bf[1][:].rearrange("p q t -> p (q t)"), NQ, "q1",
+                              plane=placed([P, NQ], U8, "q1_plane", PLANE_AT)))
         nc.scalar.activation(out=vs_got[1][:], in_=vs_pool[:].indirect(listed(1)), func=ACT.Copy)
-        half_kb = [halved(kb_turned[:, LAST:LAST + PACK], placed([P, PACK], F32, "half_kb0", VS_AT + 4 * K_PASS))]
+        half_kb = [halved(kb_turned[0][:, LAST:LAST + PACK], placed([P, PACK], F32, "half_kb0", HALF_AT))]
+        kb_dealt = placed([P, DEALT, P], F32, "kb_dealt", DEALT_AT)
+        nc.scalar.copy(out=kb_dealt[:].rearrange("p t m -> p m t"),
+                       in_=kb_got[1][:].rearrange("p (m t) -> p m t", t=PACK)[:, :, 0:DEALT])
         vs_cols = sbuf([P, SLOT_PASSES, 2 * PACK], F32, "vs_cols")
         for g in range(SLOT_PASSES):
             nc.sync.dma_start(out=vs_cols[:, g, 0:PACK], in_=vs_got[g][LAST:P, :])
 
         half = LIST_COLS // 2
-        last_words = [gather_words(listed(1)[:, a * half:(a + 1) * half], T,
-                                   placed([P, K_PASS // 2], U32, "kw_got1%d" % a, Q0_AT + (1 + a) * PACK * NQ))
+        last_words = [gather_words(listed(1)[:, a * half:(a + 1) * half], T, sbuf([P, K_PASS // 2], U32, "kw_got1%d" % a))
                       for a in range(2)]
         last_codes = sbuf([P, D_PASSES, K_PASS], U16, "k_codes1")
         for a in range(2):
@@ -208,47 +217,55 @@ def tile_attend_sigm_cap_kb_srtq256n1024t2048_kernel(tc, qT, k_words, k_scales, 
             nc.scalar.activation(out=p[:], in_=capped[:, :, first:first + width], func=ACT.Sigmoid, scale=2.0)
             return p
 
-        def weights(p, g, width, name, tag=None):
-            w = sbuf([P, width, PACK], BF16, name, tag)
-            scales = vs_cols[:, g, 0:PACK].unsqueeze(1).unsqueeze(3).to_broadcast([P, width // 4, PACK, 4])
-            nc.vector.tensor_tensor(out=w[:].rearrange("p (c i) t -> p c t i", i=4),
+        def weights(p, g, w):
+            scales = vs_cols[:, g, 0:PACK].unsqueeze(1).unsqueeze(3).to_broadcast([P, P // 4, PACK, 4])
+            nc.vector.tensor_tensor(out=w.rearrange("p (c i) t -> p c t i", i=4),
                                     in0=p[:].rearrange("p t (c i) -> p c t i", i=4), in1=scales, op=ALU.mult)
-            return w[:].rearrange("p q t -> p (q t)")
+            return w.rearrange("p q t -> p (q t)")
 
-        def turned_values(g):
-            turned = bank(g, [P, V_TILES, 2, P], F32, "v_turned")
-            for h in range(V_TILES):
+        def turned_values(g, planes, index, woven):
+            turned = bank(index, [P, len(planes), 2, P], F32, "v_turned")
+            for i, h in enumerate(planes):
                 for u in range(2):
-                    nc.tensor.transpose(turned[:, h, u, :], value_pairs(g, h, u), ident[:])
-            woven = sbuf([P, V_TILES, P, 2], F32, "v_woven%d" % g)
+                    nc.tensor.transpose(turned[:, i, u, :], value_pairs(g, h, u), ident[:])
             nc.scalar.copy(out=woven[:], in_=turned[:].rearrange("p h u e -> p h e u"))
             return woven[:].rearrange("p h e u -> p (h e u)").bitcast(BF16)
 
         capped0 = capped_scores(0)
-        half_kb.append(halved(kb_cols[:, 0:PACK], sbuf([P, PACK], F32, "half_kb1")))
-        p0 = sigmoid(capped0, 0, NQ, sbuf([P, PACK, NQ], F32, "p0"))
+        for t in reversed(range(DEALT)):
+            turn_bias(1, t, kb_dealt[:, t, :])
+        half_kb.append(halved(kb_turned[1][:, LAST:LAST + PACK], sbuf([P, PACK], F32, "half_kb1")))
+        p0 = [sigmoid(capped0, qh * P, P, sbuf([P, PACK, P], F32, "p0_%d" % qh)) for qh in range(Q_TILES)]
         capped1 = capped_scores(1)
-        v_woven = [turned_values(0)]
+        first_woven = turned_values(0, range(V_TILES), 0, sbuf([P, V_TILES, P, 2], F32, "v_woven0"))
         p1 = [sigmoid(capped1, qh * P, P, placed([P, PACK, P], F32, "p1_%d" % qh, P1_AT + qh * P_BYTES))
               for qh in range(Q_TILES)]
-        v_woven.append(turned_values(1))
+        last_woven = [turned_values(1, [h], h, sbuf([P, 1, P, 2], F32, "v_woven1%d" % h)) for h in range(V_TILES)]
 
-        w0 = weights(p0, 0, NQ, "w0")
-        v_mx = [quantised(v_woven[0], DV, "v0", "p0")]
-        w0_mx = quantised(w0, NQ, "w0")
-        w1 = [weights(p1[0], 1, P, "w1_0", "v_woven0"), weights(p1[1], 1, P, "w1_1")]
-        v_mx.append(quantised(v_woven[1], DV, "v1"))
-        w1_mx = [quantised(w1[0], P, "w1_0", "v_woven1"), quantised(w1[1], P, "w1_1")]
-
+        w0 = sbuf([P, NQ, PACK], BF16, "w0")
         for qh in range(Q_TILES):
-            cols = slice(qh * P, (qh + 1) * P)
-            y_bank = bank(2 + qh, [P, DV], F32, "y_bank")
-            for g in range(SLOT_PASSES):
-                w_codes, w_plane = (part[:, cols] for part in w0_mx) if g == 0 else (part[:] for part in w1_mx[qh])
-                v_codes, v_plane = (part[:] for part in v_mx[g])
-                nc.tensor.matmul_mx(out=y_bank[:], lhsT=w_codes.bitcast(FP8X4), lhsT_scale=w_plane,
+            weights(p0[qh], 0, w0[:, qh * P:(qh + 1) * P, :])
+        first_v = quantised(first_woven, DV, "v0", "p0_0")
+        w0_mx = quantised(w0[:].rearrange("p q t -> p (q t)"), NQ, "w0")
+        w1 = [weights(p1[qh], 1, sbuf([P, P, PACK], BF16, "w1_%d" % qh, ("v_woven0", None)[qh])[:])
+              for qh in range(Q_TILES)]
+        w1_mx = [quantised(w1[qh], P, "w1_%d" % qh) for qh in range(Q_TILES)]
+        last_v = [quantised(last_woven[h], P, "v1%d" % h) for h in range(V_TILES)]
+
+        pieces = [(qh, h) for h in range(V_TILES) for qh in range(Q_TILES)]
+        y_banks = [bank(2 + i, [P, P], F32, "y_bank") for i in range(len(pieces))]
+        for g in range(SLOT_PASSES):
+            for i, (qh, h) in enumerate(pieces):
+                rows, features = slice(qh * P, (qh + 1) * P), slice(h * P, (h + 1) * P)
+                w_codes, w_plane = (part[:, rows] for part in w0_mx) if g == 0 else (part[:] for part in w1_mx[qh])
+                v_codes, v_plane = (part[:, features] for part in first_v) if g == 0 else (part[:] for part in last_v[h])
+                nc.tensor.matmul_mx(out=y_banks[i][:], lhsT=w_codes.bitcast(FP8X4), lhsT_scale=w_plane,
                                     rhs=v_codes.bitcast(FP8X4), rhs_scale=v_plane,
                                     start=(g == 0), stop=(g == SLOT_PASSES - 1))
-            y = sbuf([P, DV], F32, "y%d" % qh)
-            nc.scalar.activation(out=y[:], in_=y_bank[:], func=ACT.Copy, scale=1.0 / 16.0)
-            nc.sync.dma_start(out=out[0, cols, :], in_=y[:])
+        for i, (qh, h) in enumerate(pieces):
+            y = sbuf([P, P], F32, "y%d" % i)
+            if i != 2:
+                nc.scalar.activation(out=y[:], in_=y_banks[i][:], func=ACT.Copy, scale=1.0 / 16.0)
+            else:
+                nc.vector.tensor_scalar_mul(y[:], y_banks[i][:], 1.0 / 16.0)
+            nc.sync.dma_start(out=out[0, qh * P:(qh + 1) * P, h * P:(h + 1) * P], in_=y[:])

@@ -29,16 +29,14 @@ SCALE_BASE = 32
 HEAD = T - N + K_PASS
 SCALAR_QUERIES = 136
 ALIGN = 256
-DEALT = 2
+VECTOR_COLS = 16
 EARLY_ZEROS = 256
 EARLY_VS = 512
 CODES_AT = 0
 PLANE_AT = CODES_AT + 2 * K_PASS
 HALF_AT = PLANE_AT + NQ
-DEALT_AT = HALF_AT + ALIGN
-VS_AT = DEALT_AT + 4 * DEALT * P
-P1_AT = VS_AT + 4 * K_PASS
-P_BYTES = 4 * PACK * P
+VS_AT = HALF_AT + ALIGN
+V1_AT = VS_AT + 4 * K_PASS
 
 FLOPS = 2 * NQ * N * (D + DV)
 BYTES = 4 * D * NQ + 4 * P * T + 32 * T + 4 * DV * T + 2 * 4 * T + 2 * P * N // 16 + 4 * NQ * DV
@@ -101,7 +99,7 @@ def tile_attend_sigm_cap_kb_srtq256n1024t2048_kernel(tc, qT, k_words, k_scales, 
         nc.sync.dma_start(out=vs_pool[LAST:P, EARLY_VS:T], in_=vs[LAST:P, EARLY_VS:T])
         load_queries(1)
 
-        ks_got = placed([P, P1_AT], U8, "ks_got", 0)
+        ks_got = placed([P, V1_AT], U8, "ks_got", 0)
         nc.vector.tensor_copy(out=ks_got[:, 0:N].rearrange("p (t m) -> p m t", t=PACK), in_=ks_pool[:].indirect(offsets[:]))
         nc.vector.memset(vs_pool[0:LAST, EARLY_ZEROS:T].bitcast(I32), 0)
         k_planes = sbuf([P, D_PASSES, N], U8, "k_planes", "ks_pool")
@@ -119,28 +117,28 @@ def tile_attend_sigm_cap_kb_srtq256n1024t2048_kernel(tc, qT, k_words, k_scales, 
         for g in range(SLOT_PASSES):
             nc.scalar.activation(out=kb_got[g][:], in_=kb_pool[:].indirect(listed(g)), func=ACT.Copy)
         nc.sync.dma_start(out=kw_pool[:, HEAD:T], in_=words[:, HEAD:T])
-        v_pool = tiles(V_TILES, [P, T], F32, "v_pool")
+        v_pool = [sbuf([P, T], F32, "v_pool0"), placed([P, T], F32, "v_pool1", V1_AT)]
         for h in range(V_TILES):
             for cols in (slice(0, HEAD), slice(HEAD, T)):
                 nc.sync.dma_start(out=v_pool[h][:, cols], in_=vT[h * P:(h + 1) * P, cols])
         q_bf = tiles(D_PASSES, [P, NQ, PACK], BF16, "q_bf")
         vs_got = [sbuf([P, K_PASS], F32, "vs_got0"), placed([P, K_PASS], F32, "vs_got1", VS_AT)]
         nc.scalar.copy(*woven_views(q_bf[0], q_raw[0], slice(0, NQ)))
+        kb_dealt = sbuf([P, PACK, P], F32, "kb_dealt")
+        nc.vector.tensor_copy(out=kb_dealt[:].rearrange("p t m -> p m t"),
+                              in_=kb_got[1][:].rearrange("p (m t) -> p m t", t=PACK))
         nc.scalar.activation(out=vs_got[0][:], in_=vs_pool[:].indirect(listed(0)), func=ACT.Copy)
         nc.scalar.copy(*woven_views(q_bf[1], q_raw[1], slice(0, SCALAR_QUERIES)))
 
-        kb_turned = [bank(7 - g, [P, P + PACK - 1], F32, "kb_turned") for g in range(SLOT_PASSES)]
+        def bias_column(g, t):
+            return (SLOT_PASSES - 1 - g) * PACK + t
 
-        def turn_bias(g, t, place):
-            nc.tensor.transpose(kb_turned[g][:, t:t + P], place, ident[:])
-
-        for g, first in ((0, 0), (1, DEALT)):
-            for t in reversed(range(first, PACK)):
-                turn_bias(g, t, kb_got[g][:, t:K_PASS:PACK])
-
-        def halved(columns, half):
-            nc.scalar.activation(out=half[:], in_=columns, func=ACT.Copy, scale=0.5)
-            return half
+        kb_turned = bank(7, [P, P + SLOT_PASSES * PACK - 1], F32, "kb_turned")
+        for g in range(SLOT_PASSES):
+            for t in reversed(range(PACK)):
+                j = bias_column(g, t)
+                place = kb_got[0][:, t:K_PASS:PACK] if g == 0 else kb_dealt[:, t, :]
+                nc.tensor.transpose(kb_turned[:, j:j + P], place, ident[:])
 
         def quantised(source, width, name, tag=None, plane=None):
             codes = sbuf([P, width], U32, name + "_codes", tag)
@@ -167,10 +165,8 @@ def tile_attend_sigm_cap_kb_srtq256n1024t2048_kernel(tc, qT, k_words, k_scales, 
         q_mx.append(quantised(q_bf[1][:].rearrange("p q t -> p (q t)"), NQ, "q1",
                               plane=placed([P, NQ], U8, "q1_plane", PLANE_AT)))
         nc.scalar.activation(out=vs_got[1][:], in_=vs_pool[:].indirect(listed(1)), func=ACT.Copy)
-        half_kb = [halved(kb_turned[0][:, LAST:LAST + PACK], placed([P, PACK], F32, "half_kb0", HALF_AT))]
-        kb_dealt = placed([P, DEALT, P], F32, "kb_dealt", DEALT_AT)
-        nc.scalar.copy(out=kb_dealt[:].rearrange("p t m -> p m t"),
-                       in_=kb_got[1][:].rearrange("p (m t) -> p m t", t=PACK)[:, :, 0:DEALT])
+        half_kb = placed([P, SLOT_PASSES * PACK], F32, "half_kb", HALF_AT)
+        nc.scalar.activation(out=half_kb[:], in_=kb_turned[:, LAST:LAST + SLOT_PASSES * PACK], func=ACT.Copy, scale=0.5)
         vs_cols = sbuf([P, SLOT_PASSES, 2 * PACK], F32, "vs_cols")
         for g in range(SLOT_PASSES):
             nc.sync.dma_start(out=vs_cols[:, g, 0:PACK], in_=vs_got[g][LAST:P, :])
@@ -184,13 +180,13 @@ def tile_attend_sigm_cap_kb_srtq256n1024t2048_kernel(tc, qT, k_words, k_scales, 
                                   in_=last_words[a])
         k_codes = [[first_codes[o][:] for o in range(D_PASSES)], [last_codes[:, o, :] for o in range(D_PASSES)]]
 
-        first_got = [sbuf([P, 2, P, 2], BF16, "first_got0"),
-                     placed([P, 2, P, 2], BF16, "first_got1", P1_AT + P_BYTES - K_PASS)]
+        first_got = tiles(V_TILES, [P, 2, P, 2], BF16, "first_got")
         last_got = tiles(V_TILES, [P, K_PASS], BF16, "last_got")
         for h in range(V_TILES):
             nc.vector.tensor_copy(out=first_got[h][:].rearrange("p u m e -> p m u e"),
                                   in_=v_pool[h][:, 0:HEAD].indirect(listed(0)))
-            nc.vector.tensor_copy(out=last_got[h][:], in_=v_pool[h][:].indirect(listed(1)))
+            reach = (LIST_COLS, VECTOR_COLS)[h]
+            nc.vector.tensor_copy(out=last_got[h][:, 0:16 * reach], in_=v_pool[h][:].indirect(listed(1)[:, 0:reach]))
 
         def value_pairs(g, h, u):
             if g == 0:
@@ -210,17 +206,17 @@ def tile_attend_sigm_cap_kb_srtq256n1024t2048_kernel(tc, qT, k_words, k_scales, 
                     start=(o == 0), stop=(o == D_PASSES - 1))
                 if o == D_PASSES - 1:
                     nc.scalar.activation(out=capped[:, t, :], in_=scores[t][:], func=ACT.Tanh,
-                                         bias=half_kb[g][:, t:t + 1], scale=0.5)
+                                         bias=half_kb[:, bias_column(g, t):bias_column(g, t) + 1], scale=0.5)
             return capped
 
-        def sigmoid(capped, first, width, p):
-            nc.scalar.activation(out=p[:], in_=capped[:, :, first:first + width], func=ACT.Sigmoid, scale=2.0)
+        def sigmoid(p, capped):
+            nc.scalar.activation(out=p, in_=capped, func=ACT.Sigmoid, scale=2.0)
             return p
 
         def weights(p, g, w):
-            scales = vs_cols[:, g, 0:PACK].unsqueeze(1).unsqueeze(3).to_broadcast([P, P // 4, PACK, 4])
+            scales = vs_cols[:, g, 0:PACK].unsqueeze(1).unsqueeze(3).to_broadcast([P, w.shape[1] // 4, PACK, 4])
             nc.vector.tensor_tensor(out=w.rearrange("p (c i) t -> p c t i", i=4),
-                                    in0=p[:].rearrange("p t (c i) -> p c t i", i=4), in1=scales, op=ALU.mult)
+                                    in0=p.rearrange("p t (c i) -> p c t i", i=4), in1=scales, op=ALU.mult)
             return w.rearrange("p q t -> p (q t)")
 
         def turned_values(g, planes, index, woven):
@@ -232,28 +228,31 @@ def tile_attend_sigm_cap_kb_srtq256n1024t2048_kernel(tc, qT, k_words, k_scales, 
             return woven[:].rearrange("p h e u -> p (h e u)").bitcast(BF16)
 
         capped0 = capped_scores(0)
-        for t in reversed(range(DEALT)):
-            turn_bias(1, t, kb_dealt[:, t, :])
-        half_kb.append(halved(kb_turned[1][:, LAST:LAST + PACK], sbuf([P, PACK], F32, "half_kb1")))
-        p0 = [sigmoid(capped0, qh * P, P, sbuf([P, PACK, P], F32, "p0_%d" % qh)) for qh in range(Q_TILES)]
+        p0 = sbuf([P, PACK, NQ], F32, "p0")
+        for places in (slice(0, 2), slice(2, PACK)):
+            sigmoid(p0[:, places, :], capped0[:, places, :])
         capped1 = capped_scores(1)
+        last_woven = [turned_values(1, [0], 1, sbuf([P, 1, P, 2], F32, "v_woven10"))]
+        p1 = [sigmoid(sbuf([P, PACK, P], F32, "p1_0")[:], capped1[:, :, 0:P])]
+        nc.scalar.activation(out=last_got[1][:, 16 * VECTOR_COLS:K_PASS],
+                             in_=v_pool[1][:].indirect(listed(1)[:, VECTOR_COLS:LIST_COLS]), func=ACT.Copy)
         first_woven = turned_values(0, range(V_TILES), 0, sbuf([P, V_TILES, P, 2], F32, "v_woven0"))
-        p1 = [sigmoid(capped1, qh * P, P, placed([P, PACK, P], F32, "p1_%d" % qh, P1_AT + qh * P_BYTES))
-              for qh in range(Q_TILES)]
-        last_woven = [turned_values(1, [h], h, sbuf([P, 1, P, 2], F32, "v_woven1%d" % h)) for h in range(V_TILES)]
+        p1.append(sigmoid(placed([P, PACK, P], F32, "p1_1", V1_AT)[:], capped1[:, :, P:NQ]))
+        last_woven.append(turned_values(1, [1], 2, sbuf([P, 1, P, 2], F32, "v_woven11")))
 
         w0 = sbuf([P, NQ, PACK], BF16, "w0")
-        for qh in range(Q_TILES):
-            weights(p0[qh], 0, w0[:, qh * P:(qh + 1) * P, :])
-        first_v = quantised(first_woven, DV, "v0", "p0_0")
+        weights(p0[:], 0, w0[:])
+        w1 = [weights(p1[0], 1, sbuf([P, P, PACK], BF16, "w1_0")[:])]
         w0_mx = quantised(w0[:].rearrange("p q t -> p (q t)"), NQ, "w0")
-        w1 = [weights(p1[qh], 1, sbuf([P, P, PACK], BF16, "w1_%d" % qh, ("v_woven0", None)[qh])[:])
-              for qh in range(Q_TILES)]
-        w1_mx = [quantised(w1[qh], P, "w1_%d" % qh) for qh in range(Q_TILES)]
-        last_v = [quantised(last_woven[h], P, "v1%d" % h) for h in range(V_TILES)]
+        last_v = [quantised(last_woven[0], P, "v10", "p0")]
+        w1_mx = [quantised(w1[0], P, "w1_0")]
+        first_v = quantised(first_woven, DV, "v0")
+        w1.append(weights(p1[1], 1, sbuf([P, P, PACK], BF16, "w1_1")[:]))
+        last_v.append(quantised(last_woven[1], P, "v11"))
+        w1_mx.append(quantised(w1[1], P, "w1_1"))
 
-        pieces = [(qh, h) for h in range(V_TILES) for qh in range(Q_TILES)]
-        y_banks = [bank(2 + i, [P, P], F32, "y_bank") for i in range(len(pieces))]
+        pieces = [(qh, h) for qh in range(Q_TILES) for h in range(V_TILES)]
+        y_banks = [bank(3 + i, [P, P], F32, "y_bank") for i in range(len(pieces))]
         for g in range(SLOT_PASSES):
             for i, (qh, h) in enumerate(pieces):
                 rows, features = slice(qh * P, (qh + 1) * P), slice(h * P, (h + 1) * P)

@@ -29,7 +29,7 @@ SCALE_BASE = 32
 HEAD = T - N + K_PASS
 SCALAR_QUERIES = 136
 ALIGN = 256
-VECTOR_COLS = 16
+VECTOR_COLS = 22
 EARLY_ZEROS = 256
 EARLY_VS = 512
 CODES_AT = 0

from contextlib import ExitStack

import concourse.mybir as mybir
from concourse.masks import make_identity

F32 = mybir.dt.float32
BF16 = mybir.dt.bfloat16
I32 = mybir.dt.int32
U32 = mybir.dt.uint32
U16 = mybir.dt.uint16
U8 = mybir.dt.uint8
FP8X4 = mybir.dt.float8_e4m3fn_x4
FP4X4 = mybir.dt.float4_e2m1fn_x4
ACT = mybir.ActivationFunctionType
ALU = mybir.AluOpType

P = 128
NQ, N, T, D, DV = 256, 1024, 2048, 1024, 256
PACK = 4
K_PASS = P * PACK
SLOT_PASSES = N // K_PASS
D_PASSES = D // K_PASS
Q_TILES = NQ // P
V_TILES = DV // P
LIST_COLS = K_PASS // 16
LAST = P - 1
SCALE_ROWS = 16 * D_PASSES
SCALE_BASE = 32
HEAD = T - N + K_PASS
SCALAR_QUERIES = 136
ALIGN = 256
VECTOR_COLS = 22
EARLY_ZEROS = 256
EARLY_VS = 512
CODES_AT = 0
PLANE_AT = CODES_AT + 2 * K_PASS
HALF_AT = PLANE_AT + NQ
VS_AT = HALF_AT + ALIGN
V1_AT = VS_AT + 4 * K_PASS

FLOPS = 2 * NQ * N * (D + DV)
BYTES = 4 * D * NQ + 4 * P * T + 32 * T + 4 * DV * T + 2 * 4 * T + 2 * P * N // 16 + 4 * NQ * DV


def tile_attend_sigm_cap_kb_srtq256n1024t2048_kernel(tc, qT, k_words, k_scales, vT, vs, kb, offs, out):
    nc = tc.nc
    with ExitStack() as ctx:
        sb = ctx.enter_context(tc.tile_pool(name="sb", bufs=1))
        shared = ctx.enter_context(tc.tile_pool(name="shared", bufs=1))
        ps = ctx.enter_context(tc.psum_pool(name="ps", bufs=1))

        def sbuf(shape, dtype, name, tag=None):
            return sb.tile(shape, dtype, name=name, tag=tag or name, align_bytes=ALIGN)

        def tiles(count, shape, dtype, name):
            return [sbuf(shape, dtype, "%s%d" % (name, i)) for i in range(count)]

        def placed(shape, dtype, name, offset):
            return shared.tile(shape, dtype, name=name, align_bytes=ALIGN, offset=offset)

        def bank(index, shape, dtype, name):
            return ps.tile(shape, dtype, name=name, tag="bank%d" % index)

        offsets = sb.tile([P, N // 16], U16, name="offsets")
        nc.sync.dma_start(offsets[:], offs)

        def listed(g):
            return offsets[:, g * LIST_COLS:(g + 1) * LIST_COLS]

        ks_pool = sbuf([P, T], U8, "ks_pool")
        kb_pool = sbuf([P, T], F32, "kb_pool")
        vs_pool = sbuf([P, T], F32, "vs_pool")
        q_raw = tiles(D_PASSES, [P, PACK, NQ], F32, "q_raw")

        def load_queries(o):
            rows = qT[0, o * K_PASS:(o + 1) * K_PASS, :]
            nc.sync.dma_start(out=q_raw[o][:], in_=rows.rearrange("(p t) q -> p t q", t=PACK))

        nc.scalar.dma_start(out=kb_pool[LAST:P, :], in_=kb[LAST:P, :])
        nc.scalar.dma_start(out=vs_pool[LAST:P, 0:EARLY_VS], in_=vs[LAST:P, 0:EARLY_VS])
        warm_in = sbuf([P, 1], F32, "warm_in")
        warm_out = sbuf([P, 1], F32, "warm_out")
        nc.vector.memset(warm_in[:], 0.0)
        nc.scalar.activation(out=warm_out[:], in_=warm_in[:], func=ACT.Sigmoid)
        ident = sbuf([P, P], F32, "ident")
        nc.vector.memset(ident[:], 0.0)
        make_identity(nc, ident[:], nomemset=True)
        nc.vector.memset(ks_pool[0:SCALE_BASE, :].bitcast(I32), 0)
        nc.vector.memset(ks_pool[SCALE_BASE + SCALE_ROWS:P, :].bitcast(I32), 0)
        nc.vector.memset(kb_pool[0:LAST, :].bitcast(I32), 0)
        nc.vector.memset(vs_pool[0:LAST, 0:EARLY_ZEROS].bitcast(I32), 0)

        kw_pool = sbuf([P, T], I32, "kw_pool")
        words = k_words[0].rearrange("p t b -> p (t b)").bitcast(I32)
        nc.sync.dma_start(out=ks_pool[SCALE_BASE:SCALE_BASE + SCALE_ROWS, :].bitcast(I32),
                          in_=k_scales.rearrange("o f t -> f o t").bitcast(I32))
        load_queries(0)
        nc.sync.dma_start(out=kw_pool[:, 0:HEAD], in_=words[:, 0:HEAD])
        nc.sync.dma_start(out=vs_pool[LAST:P, EARLY_VS:T], in_=vs[LAST:P, EARLY_VS:T])
        load_queries(1)

        ks_got = placed([P, V1_AT], U8, "ks_got", 0)
        nc.vector.tensor_copy(out=ks_got[:, 0:N].rearrange("p (t m) -> p m t", t=PACK), in_=ks_pool[:].indirect(offsets[:]))
        nc.vector.memset(vs_pool[0:LAST, EARLY_ZEROS:T].bitcast(I32), 0)
        k_planes = sbuf([P, D_PASSES, N], U8, "k_planes", "ks_pool")
        rows_a_quad = SCALE_ROWS // 4
        for quad in (0, 2, 1, 3):
            first = SCALE_BASE + quad * rows_a_quad
            nc.sync.dma_start(out=k_planes[32 * quad:32 * quad + 4, :, :].bitcast(I32),
                              in_=ks_got[first:first + rows_a_quad, 0:N].bitcast(I32))

        def woven_views(woven, planes, queries):
            return (woven[:, queries, :].rearrange("p (c i) t -> p c t i", i=4),
                    planes[:, :, queries].rearrange("p t (c i) -> p c t i", i=4))

        kb_got = tiles(SLOT_PASSES, [P, K_PASS], F32, "kb_got")
        for g in range(SLOT_PASSES):
            nc.scalar.activation(out=kb_got[g][:], in_=kb_pool[:].indirect(listed(g)), func=ACT.Copy)
        nc.sync.dma_start(out=kw_pool[:, HEAD:T], in_=words[:, HEAD:T])
        v_pool = [sbuf([P, T], F32, "v_pool0"), placed([P, T], F32, "v_pool1", V1_AT)]
        for h in range(V_TILES):
            for cols in (slice(0, HEAD), slice(HEAD, T)):
                nc.sync.dma_start(out=v_pool[h][:, cols], in_=vT[h * P:(h + 1) * P, cols])
        q_bf = tiles(D_PASSES, [P, NQ, PACK], BF16, "q_bf")
        vs_got = [sbuf([P, K_PASS], F32, "vs_got0"), placed([P, K_PASS], F32, "vs_got1", VS_AT)]
        nc.scalar.copy(*woven_views(q_bf[0], q_raw[0], slice(0, NQ)))
        kb_dealt = sbuf([P, PACK, P], F32, "kb_dealt")
        nc.vector.tensor_copy(out=kb_dealt[:].rearrange("p t m -> p m t"),
                              in_=kb_got[1][:].rearrange("p (m t) -> p m t", t=PACK))
        nc.scalar.activation(out=vs_got[0][:], in_=vs_pool[:].indirect(listed(0)), func=ACT.Copy)
        nc.scalar.copy(*woven_views(q_bf[1], q_raw[1], slice(0, SCALAR_QUERIES)))

        def bias_column(g, t):
            return (SLOT_PASSES - 1 - g) * PACK + t

        kb_turned = bank(7, [P, P + SLOT_PASSES * PACK - 1], F32, "kb_turned")
        for g in range(SLOT_PASSES):
            for t in reversed(range(PACK)):
                j = bias_column(g, t)
                place = kb_got[0][:, t:K_PASS:PACK] if g == 0 else kb_dealt[:, t, :]
                nc.tensor.transpose(kb_turned[:, j:j + P], place, ident[:])

        def quantised(source, width, name, tag=None, plane=None):
            codes = sbuf([P, width], U32, name + "_codes", tag)
            if plane is None:
                plane = sbuf([P, width], U8, name + "_plane")
            nc.vector.quantize_mx(out=codes[:].bitcast(FP8X4), scales=plane[:], in_=source)
            return codes, plane

        def gather_words(entries, reach, got):
            nc.vector.tensor_copy(out=got[:], in_=kw_pool[:, 0:reach].bitcast(U32).indirect(entries))
            return got[:].bitcast(U16).rearrange("p (c i t o) -> p o c t i", t=PACK, i=4, o=D_PASSES)

        first_words = gather_words(listed(0), HEAD, sbuf([P, K_PASS], U32, "kw_got0"))
        q_mx = [quantised(q_bf[0][:].rearrange("p q t -> p (q t)"), NQ, "q0")]
        first_codes = [sbuf([P, K_PASS], U16, "k_codes00", "q_raw0"), placed([P, K_PASS], U16, "k_codes01", CODES_AT)]

        def part_first(o):
            nc.vector.tensor_copy(out=first_codes[o][:].rearrange("p (t c i) -> p c t i", t=PACK, i=4),
                                  in_=first_words[:, o])

        part_first(0)
        nc.vector.tensor_copy(*woven_views(q_bf[1], q_raw[1], slice(SCALAR_QUERIES, NQ)))
        part_first(1)
        q_mx.append(quantised(q_bf[1][:].rearrange("p q t -> p (q t)"), NQ, "q1",
                              plane=placed([P, NQ], U8, "q1_plane", PLANE_AT)))
        nc.scalar.activation(out=vs_got[1][:], in_=vs_pool[:].indirect(listed(1)), func=ACT.Copy)
        half_kb = placed([P, SLOT_PASSES * PACK], F32, "half_kb", HALF_AT)
        nc.scalar.activation(out=half_kb[:], in_=kb_turned[:, LAST:LAST + SLOT_PASSES * PACK], func=ACT.Copy, scale=0.5)
        vs_cols = sbuf([P, SLOT_PASSES, 2 * PACK], F32, "vs_cols")
        for g in range(SLOT_PASSES):
            nc.sync.dma_start(out=vs_cols[:, g, 0:PACK], in_=vs_got[g][LAST:P, :])

        half = LIST_COLS // 2
        last_words = [gather_words(listed(1)[:, a * half:(a + 1) * half], T, sbuf([P, K_PASS // 2], U32, "kw_got1%d" % a))
                      for a in range(2)]
        last_codes = sbuf([P, D_PASSES, K_PASS], U16, "k_codes1")
        for a in range(2):
            nc.vector.tensor_copy(out=last_codes[:].rearrange("p o (t a c i) -> p a o c t i", t=PACK, a=2, i=4)[:, a],
                                  in_=last_words[a])
        k_codes = [[first_codes[o][:] for o in range(D_PASSES)], [last_codes[:, o, :] for o in range(D_PASSES)]]

        first_got = tiles(V_TILES, [P, 2, P, 2], BF16, "first_got")
        last_got = tiles(V_TILES, [P, K_PASS], BF16, "last_got")
        for h in range(V_TILES):
            nc.vector.tensor_copy(out=first_got[h][:].rearrange("p u m e -> p m u e"),
                                  in_=v_pool[h][:, 0:HEAD].indirect(listed(0)))
            reach = (LIST_COLS, VECTOR_COLS)[h]
            nc.vector.tensor_copy(out=last_got[h][:, 0:16 * reach], in_=v_pool[h][:].indirect(listed(1)[:, 0:reach]))

        def value_pairs(g, h, u):
            if g == 0:
                return first_got[h][:, u, :, :].rearrange("p m e -> p (m e)").bitcast(F32)
            return last_got[h][:].bitcast(F32)[:, u:2 * P:2]

        def capped_scores(g):
            capped = sbuf([P, PACK, NQ], F32, "capped%d" % g)
            scores = [bank(g * PACK + t, [P, NQ], F32, "score") for t in range(PACK)]
            steps = [(t, o) for o in range(D_PASSES) for t in range(PACK)]
            for t, o in (steps, sorted(steps))[g]:
                nc.tensor.matmul_mx(
                    out=scores[t][:],
                    lhsT=k_codes[g][o][:, t * P:(t + 1) * P].bitcast(FP4X4),
                    lhsT_scale=k_planes[:, o, (t * SLOT_PASSES + g) * P:(t * SLOT_PASSES + g + 1) * P],
                    rhs=q_mx[o][0][:].bitcast(FP8X4), rhs_scale=q_mx[o][1][:],
                    start=(o == 0), stop=(o == D_PASSES - 1))
                if o == D_PASSES - 1:
                    nc.scalar.activation(out=capped[:, t, :], in_=scores[t][:], func=ACT.Tanh,
                                         bias=half_kb[:, bias_column(g, t):bias_column(g, t) + 1], scale=0.5)
            return capped

        def sigmoid(p, capped):
            nc.scalar.activation(out=p, in_=capped, func=ACT.Sigmoid, scale=2.0)
            return p

        def weights(p, g, w):
            scales = vs_cols[:, g, 0:PACK].unsqueeze(1).unsqueeze(3).to_broadcast([P, w.shape[1] // 4, PACK, 4])
            nc.vector.tensor_tensor(out=w.rearrange("p (c i) t -> p c t i", i=4),
                                    in0=p.rearrange("p t (c i) -> p c t i", i=4), in1=scales, op=ALU.mult)
            return w.rearrange("p q t -> p (q t)")

        def turned_values(g, planes, index, woven):
            turned = bank(index, [P, len(planes), 2, P], F32, "v_turned")
            for i, h in enumerate(planes):
                for u in range(2):
                    nc.tensor.transpose(turned[:, i, u, :], value_pairs(g, h, u), ident[:])
            nc.scalar.copy(out=woven[:], in_=turned[:].rearrange("p h u e -> p h e u"))
            return woven[:].rearrange("p h e u -> p (h e u)").bitcast(BF16)

        capped0 = capped_scores(0)
        p0 = sbuf([P, PACK, NQ], F32, "p0")
        for places in (slice(0, 2), slice(2, PACK)):
            sigmoid(p0[:, places, :], capped0[:, places, :])
        capped1 = capped_scores(1)
        last_woven = [turned_values(1, [0], 1, sbuf([P, 1, P, 2], F32, "v_woven10"))]
        p1 = [sigmoid(sbuf([P, PACK, P], F32, "p1_0")[:], capped1[:, :, 0:P])]
        nc.scalar.activation(out=last_got[1][:, 16 * VECTOR_COLS:K_PASS],
                             in_=v_pool[1][:].indirect(listed(1)[:, VECTOR_COLS:LIST_COLS]), func=ACT.Copy)
        first_woven = turned_values(0, range(V_TILES), 0, sbuf([P, V_TILES, P, 2], F32, "v_woven0"))
        p1.append(sigmoid(placed([P, PACK, P], F32, "p1_1", V1_AT)[:], capped1[:, :, P:NQ]))
        last_woven.append(turned_values(1, [1], 2, sbuf([P, 1, P, 2], F32, "v_woven11")))

        w0 = sbuf([P, NQ, PACK], BF16, "w0")
        weights(p0[:], 0, w0[:])
        w1 = [weights(p1[0], 1, sbuf([P, P, PACK], BF16, "w1_0")[:])]
        w0_mx = quantised(w0[:].rearrange("p q t -> p (q t)"), NQ, "w0")
        last_v = [quantised(last_woven[0], P, "v10", "p0")]
        w1_mx = [quantised(w1[0], P, "w1_0")]
        first_v = quantised(first_woven, DV, "v0")
        w1.append(weights(p1[1], 1, sbuf([P, P, PACK], BF16, "w1_1")[:]))
        last_v.append(quantised(last_woven[1], P, "v11"))
        w1_mx.append(quantised(w1[1], P, "w1_1"))

        pieces = [(qh, h) for qh in range(Q_TILES) for h in range(V_TILES)]
        y_banks = [bank(3 + i, [P, P], F32, "y_bank") for i in range(len(pieces))]
        for g in range(SLOT_PASSES):
            for i, (qh, h) in enumerate(pieces):
                rows, features = slice(qh * P, (qh + 1) * P), slice(h * P, (h + 1) * P)
                w_codes, w_plane = (part[:, rows] for part in w0_mx) if g == 0 else (part[:] for part in w1_mx[qh])
                v_codes, v_plane = (part[:, features] for part in first_v) if g == 0 else (part[:] for part in last_v[h])
                nc.tensor.matmul_mx(out=y_banks[i][:], lhsT=w_codes.bitcast(FP8X4), lhsT_scale=w_plane,
                                    rhs=v_codes.bitcast(FP8X4), rhs_scale=v_plane,
                                    start=(g == 0), stop=(g == SLOT_PASSES - 1))
        for i, (qh, h) in enumerate(pieces):
            y = sbuf([P, P], F32, "y%d" % i)
            if i != 2:
                nc.scalar.activation(out=y[:], in_=y_banks[i][:], func=ACT.Copy, scale=1.0 / 16.0)
            else:
                nc.vector.tensor_scalar_mul(y[:], y_banks[i][:], 1.0 / 16.0)
            nc.sync.dma_start(out=out[0, qh * P:(qh + 1) * P, h * P:(h + 1) * P], in_=y[:])
